import numpy as np, ml_dtypes
CORES = [6,15,38,47]
N = 4
BF = ml_dtypes.bfloat16
W, VI, CR, S, EV = 1984, 320, 8, 4, 2
V = W - VI
R, NEED, DT, DL = 0.75, 9, 0.0625, 0.1875
def invol(rng, lone):
    o = np.argsort(rng.random((N, 8, CR, W)), axis=-1); x, y = o[..., 0::2], o[..., 1::2]; m = rng.random(x.shape) < lone
    c = np.empty((N, 8, CR, W), np.int64)
    np.put_along_axis(c, x, np.where(m, x, y), -1); np.put_along_axis(c, y, np.where(m, y, x), -1)
    return c
def join(row, x, y):
    p, s = int(row[x]), int(row[y])
    if p == y: return
    row[x] = y; row[y] = x
    if p != x and s != y: row[p] = s; row[s] = p
    elif p != x: row[p] = p
    elif s != y: row[s] = s
def signs(rng, shape): return np.where(rng.random(shape) < 0.5, -1.0, 1.0)
def parts(rng):
    sh = (N, 8, 16, W)
    q = 2.0 * rng.random(sh) - 1.0; v = signs(rng, sh) * (0.5 + 1.5 * rng.random(sh)); k = 0.125 + 0.375 * rng.random(sh)
    a = 2.0 * rng.random((N, 8, W)) - 1.0; con = invol(rng, 0.02)
    u = rng.random((N, 8, W)); far = rng.integers(0, CR, (N, 8, W))
    cur = (rng.integers(0, CR, (N, 8, 1)) + np.where(u < 0.7, 0, np.where(u < 0.8, 1, np.where(u < 0.9, 2, far)))) & (CR - 1)
    return q, v, k, a, con, cur
def small(x, least):
    return np.where(np.abs(x) < least, 0.0, x).astype(np.float32).astype(BF)
def camps(rng, near):
    o = rng.permutation(W); h = W // 2; side = np.empty(W); side[o[:h]] = 1.0; side[o[h:]] = -1.0
    rows = np.empty((CR, W), np.int64)
    for m in range(CR):
        x, y = rng.permutation(o[:h]), rng.permutation(o[h:])
        if near[m]: x, y = np.concatenate([x[0::2], y[0::2]]), np.concatenate([x[1::2], y[1::2]])
        rows[m, x] = y; rows[m, y] = x
    return side, rows
def brink(rng):
    F = np.float32; n = 2 ** 18
    ki = (rng.integers(160, 256, n) * 2.0 ** -9).astype(F); kj = (rng.integers(160, 256, n) * 2.0 ** -9).astype(F)
    vi = (rng.integers(128, 256, n) * 2.0 ** -7).astype(F); vj = (rng.integers(-255, -127, n) * 2.0 ** -21).astype(F)
    dv = vi - vj; kk = ki * kj; p = kk * dv; x = kk.astype(np.float64) * dv.astype(np.float64)
    t = DT * ((vi - p).astype(np.float64) - (vj + p).astype(np.float64))
    hi = small(t, 2.0 ** -20).astype(F); lo = small(t - hi, 2.0 ** -20).astype(F)
    def behind(a, b): return (F(DT) * a - hi) - (lo + F(DT) * b) < 0
    right = behind(vi - p, vj + p)
    wrong = (behind(vi - ki * (kj * dv), vj + kj * (ki * dv)), behind(vi - x, vj + x), behind((vi - x).astype(F), (vj + x).astype(F)))
    best = np.stack([np.argsort(right == w, kind="stable")[:96] for w in wrong])
    return np.stack([-hi, lo, vi, vj, ki, kj])[:, best]
def pack(q, v, k, a, con, cur):
    return {"q0": small(q, 2.0 ** -20).reshape(N, 128, W), "v0": small(v, 2.0 ** -16).reshape(N, 128, W), "kap": k.astype(np.float32).astype(BF).reshape(N, 128, W), "aim": small(a, 2.0 ** -20),
            "con": np.ascontiguousarray(con.reshape(N, 8 * CR, W)).astype(np.int32), "cur": np.ascontiguousarray(cur).astype(np.int32)}
def setup_inputs(rng):
    return pack(*parts(rng))
def setup_inputs_calm(rng):
    q, v, k, a, con, cur = parts(rng); v = v * 0.5
    g = np.arange(8)[None, :, None]; r = np.arange(N)[:, None, None]
    cur = (np.where(r % 2 == 0, g - 2, CR - 3 - g) & (CR - 1)) + np.zeros((N, 8, W), np.int64)
    return pack(q, v, k, a, con, cur)
def setup_inputs_corners(rng):
    q, v, k, a, con, cur = parts(rng); s = int(rng.integers(0, 8)); here = np.arange(W)
    for r in range(N):
        for g in range(8):
            z = (g + 3 * r + s) % 8
            if z == 0: con[r, g] = here
            elif z == 1:
                join(con[r, g, 0], 0, W - 1); con[r, g] = con[r, g, 0].copy(); q[r, g] = q[r, g] * 0.25
            elif z == 2: k[r, g] = np.where(rng.random((16, W)) < 0.5, 0.0625, 0.5)
            elif z == 3: q[r, g] = q[r, g, :, :1].copy()
            elif z == 4:
                side, rows = camps(rng, [m % 2 == 1 for m in range(CR)])
                con[r, g] = rows; q[r, g] = side[None, :] * (0.75 + 0.25 * rng.random((16, W))); cur[r, g] = 2 * int(rng.integers(0, CR // 2))
            elif z == 5:
                for m in range(CR):
                    x, y = 1 + m, W - 2 - m
                    join(con[r, g, m], 0, x); join(con[r, g, m], W - 1, y)
                    q[r, g, :, x] = q[r, g, :, 0]; q[r, g, :, y] = q[r, g, :, W - 1]; cur[r, g, x] = m; cur[r, g, y] = m
            elif z == 6:
                for m in range(CR):
                    o = rng.permutation(V); row = con[r, g, m]; h = (V - VI) // 2
                    row[V:] = o[:VI]; row[o[:VI]] = V + np.arange(VI)
                    x, y = o[VI:VI + h], o[VI + h:]
                    row[x] = y; row[y] = x
            else:
                side, rows = camps(rng, [1 <= m <= CR - 3 for m in range(CR)])
                con[r, g] = rows; q[r, g] = side[None, :] * (0.75 + 0.25 * rng.random((16, W))); cur[r, g] = CR - 1 - rng.integers(0, 2, W)
    return pack(q, v, k, a, con, cur)
def setup_inputs_ends(rng):
    q, v, k, a, con, cur = parts(rng); q = signs(rng, q.shape)
    for r in range(N):
        for g in range(8):
            for m in (0, CR - 1):
                join(con[r, g, m], 0, W - 1); join(con[r, g, m], 1, W - 2)
            e = 1.0 if (r + g) % 2 == 0 else -1.0
            q[r, g, :, W - 1] = e * q[r, g, :, 0]; q[r, g, :, W - 2] = -e * q[r, g, :, 1]
    v = np.where(rng.random(q.shape) < 0.875, -2.0, 2.0) * q
    k = np.where(rng.random(q.shape) < 0.8, 0.5, 0.0625); a = signs(rng, a.shape)
    cur = np.where(rng.random(cur.shape) < 0.75, 0, CR - 1)
    return pack(q, v, k, a, con, cur)
def setup_inputs_spread(rng):
    q, v, k, a, con, cur = parts(rng); sh = (N, 8, 16, W); one = (N, 8, 1, W)
    q = q * np.exp2(-rng.random(one)); v = signs(rng, sh) * (0.5 + 0.5 * rng.random(sh)) * np.exp2(2.0 * rng.random(one) - 1.0)
    k = (0.25 + 0.25 * rng.random(sh)) * np.exp2(-2.0 * rng.random(one)); a = a * np.exp2(-2.0 * rng.random(a.shape))
    cur = np.where(rng.random((N, 8, 1)) < 0.5, rng.integers(0, CR, cur.shape), cur)
    return pack(q, v, k, a, con, cur)
def setup_inputs_ties(rng):
    q, v, k, a, con, cur = parts(rng); edge = brink(rng)
    q = rng.integers(-8, 9, q.shape) * 0.125; v = rng.integers(-1, 2, v.shape) * 2.0; k = np.where(rng.random(k.shape) < 0.9, 0.5, 0.0625); a = rng.integers(-8, 9, a.shape) * 0.125
    for r in range(N):
        for g in range(8):
            b = int(rng.integers(0, CR)); row = con[r, g, b]; x = np.flatnonzero(np.arange(W) < row); x = rng.permutation(x)[:len(x) // 4]; y = row[x]
            n = rng.integers(NEED - 1, NEED + 1, len(x)); low = rng.integers(-8, 2, (16, len(x))); place = np.argsort(rng.random((16, len(x))), axis=0)
            q[r, g][:, x] = low * 0.125; q[r, g][:, y] = (low + np.where(place < n[None, :], 6, 7)) * 0.125; v[r, g][:, y] = v[r, g][:, x]
            cur[r, g] = (cur[r, g] - cur[r, g, 0] + b) & (CR - 1); cur[r, g, x] = b; cur[r, g, y] = b
            o = rng.permutation(V)
            for p in range(4):
                x, y = int(o[2 * p]), int(o[2 * p + 1]); e = signs(rng, 16)
                for m in range(CR): join(con[r, g, m], x, y)
                a[r, g, x] = 0.25; a[r, g, y] = -0.25
                if p < 2: z = edge[:, np.arange(16) % 3, rng.integers(0, 96, 16)].astype(np.float64)
                else:
                    lane = rng.permutation(16); near = lane < 8; one = lane == 8
                    z = np.stack([np.where(near, -0.25, np.where(one, 0.75, -0.875)), np.where(near, 0.25, np.where(one, 2.0 ** -20, 0.875)),
                                  np.where(near, 1.0, 0.0), np.where(near, -1.0, np.where(one, -129.0 * 2.0 ** -23, 0.0)), np.full(16, 0.375), np.full(16, 0.375)])
                q[r, g, :, x] = e * z[0]; q[r, g, :, y] = e * z[1]; v[r, g, :, x] = e * z[2]; v[r, g, :, y] = e * z[3]; k[r, g, :, x] = z[4]; k[r, g, :, y] = z[5]
    return pack(q, v, k, a, con, cur)
def check_ranges(d):
    bad = []
    for n, lo, hi, least in (("q0", -1.0, 1.0, 2.0 ** -20), ("v0", -2.0, 2.0, 2.0 ** -16), ("kap", 0.0625, 0.5, 0.0625), ("aim", -1.0, 1.0, 2.0 ** -20)):
        x = np.asarray(d[n]).astype(np.float64); s = np.abs(x)
        if not np.all((x >= lo) & (x <= hi) & ((s == 0) | (s >= least))): bad.append("range of " + n)
    for n, hi in (("con", W - 1), ("cur", CR - 1)):
        if np.min(d[n]) < 0 or np.max(d[n]) > hi: bad.append("range of " + n)
    if "range of con" not in bad:
        c = np.asarray(d["con"]).astype(np.int64)
        if np.any(np.take_along_axis(c, c, 2) != np.arange(W)): bad.append("a row of con is no involution")
    return bad
def pick(x, j):
    y = np.empty_like(x)
    for r in range(N):
        for g in range(8): y[r, g] = np.take(x[r, g], j[r, g], axis=1)
    return y
def travel(x, d):
    y = x.copy(); H = V + VI // 2
    y[..., V:H] = np.roll(x[..., V:H], (d, d), axis=(0, 1)); y[..., H:] = np.roll(x[..., H:], (d, 4 * d), axis=(0, 1))
    return y
def reference(q0, v0, kap, aim, con, cur):
    F = np.float32; sh = (N, 8, 16, W)
    qs = q0.astype(F).reshape(sh); vs = v0.astype(F).reshape(sh); ks = kap.astype(F).reshape(sh); target = aim.astype(F).reshape(N, 8, 1, W)
    ct = con.astype(np.int64).reshape(N, 8, CR, W); cs = cur.astype(np.int64).reshape(N, 8, W); here = np.arange(W)[None, None, :]
    total = ks.astype(np.float64)
    for shot in range(2):
        q, v, k, c, log = qs, vs, ks, cs, []
        for t in range(1, S + 1):
            j0 = np.take_along_axis(ct, c[:, :, None, :], 2)[:, :, 0]; j1 = np.take_along_axis(ct, ((c + 1) & (CR - 1))[:, :, None, :], 2)[:, :, 0]
            d0 = q - pick(q, j0); d1 = q - pick(q, j1)
            o0 = np.sum(np.abs(d0) <= F(R), axis=2) >= NEED; o1 = np.sum(np.abs(d1) <= F(R), axis=2) >= NEED
            some = o0 | o1; j = np.where(o0, j0, np.where(o1, j1, here)); choice = np.where(some, j, -1)
            mutual = some & (np.take_along_axis(choice, j, 2) == here)
            dq = np.where(o0[:, :, None], d0, d1); dv = v - pick(v, j); kj = pick(k, j)
            hit = mutual[:, :, None] & (dq * dv < F(0))
            kk = np.where(hit, k * kj, F(0)); w = np.where(hit, kj.astype(np.float64) * dv, 0.0); log.append((j, kk, w))
            v = v - kk * dv
            c = np.where(mutual & o0, c + 1, c + 2) & (CR - 1)
            q = q + F(DT) * v
            if t % EV == 0 and t < S: q, v, k = travel(q, 1), travel(v, 1), travel(k, 1)
        aq = q - target; av = np.zeros(sh, F); gain = np.zeros(sh, np.float64)
        for t in range(S, 0, -1):
            if t % EV == 0 and t < S: aq, av, gain = travel(aq, -1), travel(av, -1), travel(gain, -1)
            av = av + F(DT) * aq
            j, kk, w = log[t - 1]; da = av - pick(av, j)
            gain = gain - w * da.astype(np.float64)
            av = av - kk * da
        total = total + gain
        vs = vs - np.clip(av, F(-DL), F(DL))
    return {"yg": total.reshape(N, 128, W).astype(np.float32), "yv": vs.reshape(N, 128, W).astype(np.float32)}

def check_inputs(d):
    bad = list(check_ranges(d))
    if not bad:
        for name, y in reference(**d).items():
            for q in range(N):
                v = np.abs(np.asarray(y[q], np.float64)); s = np.sqrt(np.mean(v * v))
                if v.max() > 14 * s or s < 2.0 ** -4: bad.append('%s of rank %d is uneven or too small' % (name, q))
    return bad

@@ -1,0 +1,723 @@
+import numpy as np
+from concourse.mybir import AluOpType, ActivationFunctionType
+
+W, V0, VI, PAD = 1984, 1664, 320, 8
+WP = W + PAD
+CH = [(0, 512), (512, 1024), (1024, 1536), (1536, W)]
+MC = [(0, 26), (26, 52), (52, 78), (78, 104), (104, 124)]
+CENTER = [8 * (a + b) + 8 for a, b in MC]
+F, B, I, U = "float32", "bfloat16", "int32", "uint16"
+MSG = ["k", "q0", "v0", "a0", "w0", "q1", "v1", "a1", "w1", "G"]
+
+SCRATCH = {}
+for _n, _s, _d in (
+    [("q", [2, WP + PAD], F), ("vs", [2, WP + PAD], F), ("k3", [2, 448], B), ("D", [2 * WP + PAD], F), ("X", [WP + PAD], F), ("pr", [W], F), ("kk01", [W], F),
+     ("G", [W], F), ("Gh", [VI], F), ("rk", [W], F), ("v0f", [W], F), ("ind", [2, W], B), ("mg", [W], B), ("sg", [W], B), ("sg1", [W], B),
+     ("q0b", [WP], B), ("kA", [WP + PAD], B), ("kB", [WP + PAD], B), ("aimA", [W], B), ("Wc", [16, 128], B),
+     ("E", [256], F), ("ones", [128], F), ("Ib", [128], B), ("Ic", [128], B), ("Sel", [128], B),
+     ("L", [16, 8], F), ("L1", [16, 8], F), ("L2", [16, 8], F),
+     ("iL", [16, 8], I), ("iS", [128], I), ("iO", [16], I), ("iG", [8], I), ("iP", [1], I), ("pcol", [1], F), ("oh", [16], F),
+     ("G8", [8], B), ("nb", [2], F), ("bias", [248], B), ("i8", [124], F), ("i8b", [124], F), ("tgt", [124], F),
+     ("ct", [2, 31, 16], I), ("conf", [31, 32], F),
+     ("cu", [2, 4, 16], I), ("cf", [4, 32], F), ("cf2", [4, 32], F), ("curB", [124], F), ("c2", [124], F), ("ci", [124], I),
+     ("Pi", [248], I), ("Ph", [248], I), ("JJ", [248], I), ("JJ2", [248], I), ("of", [248], U), ("of2", [248], U), ("A", [124], F),
+     ("cw", [124], F), ("lvl", [124], B), ("so", [124], U), ("ab", [124], F),
+     ("PT", [248], F), ("TA", [372], F), ("TB", [372], F), ("UV", [248], F)]
+    + [("kk%d" % t, [W], F) for t in (1, 2, 3, 4)] + [("nv%d" % t, [W], F) for t in (1, 2, 3, 4)]
+    + [("j%d" % t, [124], U) for t in (1, 2, 3, 4)] + [("l_" + m, [VI], F) for m in "kqvawG"]
+):
+    SCRATCH[_n] = ("sbuf", [128] + _s, _d)
+for _n in ("N0", "N1", "N2", "H0", "H1", "Q0", "Q1", "C"):
+    SCRATCH[_n] = ("psum", [128, 512], F)
+ENG = ["v", "s", "t", "g", "y"]
+SEMAPHORES = ["e_" + e for e in ENG] + ["d%d" % n for n in range(130)] + ["r_" + m for m in MSG]
+
+ALL = slice(None)
+OPT = {"NXV": 6,
+       "QD": (3, 0),
+       "BD": (3, 0),
+       "SD": (1, 2),
+       "RC": 16}
+
+
+def ap(name, *idx):
+    return (name, (ALL,) + idx)
+
+
+def app(name, part, *idx):
+    return (name, (part,) + idx)
+
+
+def cols(name, a, b, step=None):
+    if name[-1] in "'*":
+        return (name[:-1], (ALL, 1 if name[-1] == "'" else ALL, slice(a, b, step)))
+    if name in ("q", "vs"):
+        return (name, (ALL, 0, slice(a, b, step)))
+    return (name, (ALL, slice(a, b, step)))
+
+
+def ind(win, off):
+    return ("@", win, off)
+
+
+def build(g, T, nxt, prv):
+    A, AF = AluOpType, ActivationFunctionType
+    ops = []
+
+    def R(x):
+        if not isinstance(x, tuple):
+            return x
+        if x[0] == "@":
+            return R(x[1]).indirect(R(x[2]))
+        return T[x[0]][x[1]]
+
+    def parts(xs):
+        out = []
+        for x in xs:
+            if isinstance(x, tuple):
+                out += [x[1], x[2]] if x[0] == "@" else [x]
+        return [x for x in out if x[0] in SCRATCH]
+
+    def add(eng, f, rd, wr, kind="c", **kw):
+        ops.append(dict(eng=eng, f=f, rd=parts(rd), wr=parts(wr), kind=kind, **kw))
+
+    def tt(o, a, b, op):
+        add("v", lambda: g.vector.tensor_tensor(R(o), R(a), R(b), op), [a, b], [o])
+
+    def ts(o, a, s1, op0, s2=None, op1=None):
+        if op1 is None:
+            add("v", lambda: g.vector.tensor_scalar(R(o), R(a), R(s1), None, op0), [a, s1], [o])
+        else:
+            add("v", lambda: g.vector.tensor_scalar(R(o), R(a), R(s1), R(s2), op0, op1), [a, s1, s2], [o])
+
+    def cp(o, a):
+        add("v", lambda: g.vector.tensor_copy(R(o), R(a)), [a], [o])
+
+    def fill(o, c):
+        add("v", lambda: g.vector.memset(R(o), c), [], [o])
+
+    def flip(o, a):
+        add("v", lambda: g.vector.transpose(R(o), R(a)), [a], [o])
+
+    def act(o, a, func, bias=0.0, scale=1.0):
+        add("s", lambda: g.scalar.activation(R(o), R(a), func, bias=R(bias), scale=R(scale)), [a, bias, scale], [o])
+
+    def mm(o, l, r, start=True, stop=True):
+        add("t", lambda: g.tensor.matmul(R(o), R(l), R(r), start, stop), [l, r], [o])
+
+    def iota(o, pattern, base, mult):
+        if SCRATCH[o[0]][2] != I:
+            add("g", lambda: g.iota(R(o), pattern, base, mult, allow_small_or_imprecise_dtypes=True), [], [o])
+        else:
+            add("g", lambda: g.iota(R(o), pattern, base, mult), [], [o])
+
+    def dma(eng, o, a, acc=False):
+        qu = {"g": g, "s": g.scalar, "y": g.sync}[eng]
+        if acc:
+            add(eng, lambda: qu.dma_start(R(o), R(a), accum_op=A.add), [a, o], [o], "d")
+        else:
+            add(eng, lambda: qu.dma_start(R(o), R(a)), [a], [o], "d")
+
+    def send(m, src, to):
+        add("g", None, [src], [], "r", msg=m, src=R(src), to=to)
+
+    def turn(m, dst, fwd, bank, plus=None):
+        add("t", None, [], [ap("l_" + m[0])], "a", msg=m)
+        s1 = 16 if fwd else 112
+        mm(cols(bank, 0, 160), cols("E", 128 - s1, 256 - s1), cols("l_" + m[0], 0, 160))
+        mm(cols(bank, 160, 320), cols("E", 64, 192), cols("l_" + m[0], 160, 320))
+        if plus is None:
+            for d in dst:
+                act(d, cols(bank, 0, VI), AF.Copy)
+        else:
+            tt(dst, plus, cols(bank, 0, VI), A.add)
+
+    If = cols("E", 0, 128)
+    vis = lambda n: cols(n, PAD + V0, WP)
+    vis2 = lambda n: [vis(n), vis(n + "'")]
+    whole = lambda n: cols(n, 0, WP + PAD)
+    DT = cols("G", 0, 992)
+    st = lambda n, c: cols(n, PAD + CH[c][0], PAD + CH[c][1])
+    ch = lambda n, c: cols(n, CH[c][0], CH[c][1])
+    bk = lambda n, c: cols(n, 0, CH[c][1] - CH[c][0])
+    lst = lambda n, c, o=0: cols(n, o + CH[c][0] // 16, o + CH[c][1] // 16)
+    DOFF = (WP + PAD, PAD)
+    dd = lambda e, c: cols("D", DOFF[e] + CH[c][0], DOFF[e] + CH[c][1])
+    msk, sc, scl = cols("rk", 0, 992), cols("rk", 992, W), cols("rk", 999, W, 8)
+    extra = []
+
+    def spare(n=1):
+        for _ in range(n):
+            if extra:
+                extra.pop(0)()
+
+    fill(ap("cu"), 0)
+    fill(ap("ones"), 1.0)
+    for gi in range(8):
+        a, y = gi // 2, gi % 2
+        dma("y" if y else "s", app("ct", slice(32 * a, 32 * a + 32), y), ("con", (slice(8 * gi, 8 * gi + 8), ALL)))
+    for gi in range(8):
+        a, y = gi // 2, gi % 2
+        dma("y" if y else "s", app("cu", slice(32 * a, 32 * a + 31), y), ("cur", (gi, ALL)))
+    dma("y", ap("sg"), ("v0", (ALL, ALL)))
+    dma("y", cols("q0b", PAD, WP), ("q0", (ALL, ALL)))
+    dma("y", cols("kA", PAD, WP), ("kap", (ALL, ALL)))
+    dma("y", app("aimA", slice(0, 8)), ("aim", (ALL, ALL)))
+    dma("y", ap("k3", 0), ("kap", (ALL, slice(*CH[3]))))
+    dma("y", ap("k3", 1, slice(0, 128)), ("kap", (ALL, slice(CH[3][0], V0))))
+    dma("y", cols("kB", PAD, PAD + V0), ("kap", (ALL, slice(0, V0))))
+    iota(ap("iL"), [[-32, 4], [-1, 4], [-4, 8]], 0, 1)
+    iota(ap("iG"), [[-16, 8]], 128, 1)
+    iota(ap("iS"), [[1, 128]], 2048, -16)
+    iota(ap("iO"), [[-1, 16]], 16, 1)
+    iota(ap("iP"), [[0, 1]], 0, 1)
+    iota(ap("i8"), [[16, 124]], 8, 0)
+    for h in (0, 1):
+        add("g", lambda h=h: g.affine_select(R(cols("E", 128 * h, 128 * h + 128)), R(ap("ones")), [[-1, 128]], A.is_equal, 0.0, 0, 1),
+            [ap("ones")], [cols("E", 128 * h, 128 * h + 128)])
+    dma("g", cols("q'", PAD, WP), ("q0", (ALL, ALL)))
+    iota(cols("q0b", 0, PAD), [[0, PAD]], 0, 0)
+    iota(ap("Wc"), [[0, 2048]], 0, 0)
+    iota(cols("bias", 0, 124), [[0, 124]], -8192, 0)
+    iota(cols("bias", 124, 248), [[0, 124]], -17 * 8192, 0)
+    for n in ("vs", "X", "D", "kA", "q", "kB"):
+        iota(cols(n, 0, PAD), [[0, PAD]], 0, 0)
+        iota(cols(n, WP, WP + PAD), [[0, PAD]], 0, 0)
+    iota(cols("D", 2 * WP, 2 * WP + PAD), [[0, PAD]], 0, 0)
+    ts(ap("L"), ap("iL"), 0.0, A.is_equal, 2048.0, A.mult)
+    ts(ap("L1", ALL, slice(0, 7)), ap("iL", ALL, slice(0, 7)), 4.0, A.is_equal, -2049.0, A.mult)
+    ts(ap("L1", ALL, 7), ap("iL", ALL, 7), -28.0, A.is_equal, -1.0, A.mult)
+    ts(ap("L2", ALL, slice(0, 6)), ap("iL", ALL, slice(0, 6)), 8.0, A.is_equal)
+    ts(ap("L2", ALL, 6), ap("iL", ALL, 6), -24.0, A.is_equal)
+    tt(ap("L"), ap("L"), ap("L1"), A.add)
+    ts(ap("iG"), ap("iG"), 4, A.arith_shift_right)
+    ts(ap("iS"), ap("iS"), 4, A.arith_shift_right)
+    tt(ap("L", ALL, slice(0, 7)), ap("L", ALL, slice(0, 7)), ap("L2", ALL, slice(0, 7)), A.add)
+    ts(ap("Sel"), ap("iS"), 128.0, A.is_equal)
+    act(cols("vs", PAD, WP), ap("sg"), AF.Copy, scale=0.0625)
+    dma("y", cols("vs'", PAD, WP), cols("vs", PAD, WP))
+    for y in (0, 1):
+        ts(ap("conf", ALL, slice(16 * y, 16 * y + 16)), ap("ct", y), 8.0, A.add)
+    mm(cols("N0", 0, 512), ap("L"), ap("conf", slice(0, 16)))
+    mm(cols("N1", 0, 480), ap("L"), ap("conf", slice(16, 31)))
+    for y in (0, 1):
+        cp(ap("cf", ALL, slice(16 * y, 16 * y + 16)), ap("cu", y))
+    ts(ap("G8"), ap("iG"), 8.0, A.is_equal, 8192.0, A.mult)
+    flip(ap("cf2"), ap("cf"))
+    ts(ap("iP"), ap("iP"), 15, A.bitwise_and)
+    for z in range(4):
+        cp(cols("curB", z, 124, 4), ap("cf2", z, slice(0, 31)))
+
+    def mask(src, e):
+        for m in range(8):
+            act(cols("rk", m, 992, 8), ap(src), AF.Abs, bias=-float(2 ** 24) * ((m - e) & 7), scale=float(2 ** 24))
+
+    def scan():
+        add("v", lambda: g.vector.tensor_tensor_scan(R(sc), R(msk), R(DT), 8.0e6, A.min, A.add), [msk, DT], [sc])
+
+    def unpack(jj, of):
+        ts(cols(jj, 0, 124), cols("Pi", 0, 124), 11, A.arith_shift_right)
+        ts(cols(jj, 124, 248), cols("Pi", 0, 124), 2047, A.bitwise_and)
+        ts(cols(of, 0, 124), cols(jj, 0, 124), -2048.0, A.add)
+        ts(cols(of, 124, 248), cols(jj, 124, 248), -1.0, A.mult, 2048.0, A.add)
+
+    mask("curB", 0)
+    flip(ap("conf", slice(0, 16)), cols("N0", 0, 512))
+    cp(ap("pcol"), ap("iP"))
+    ts(ap("iO"), ap("iO"), 15, A.bitwise_and)
+    flip(ap("conf", slice(16, 31)), cols("N1", 0, 480))
+    ts(ap("i8"), ap("i8"), ap("pcol"), A.add)
+    for qq in range(4):
+        o, a = cols("G", 248 * qq, 248 * qq + 248), ap("conf", ALL, slice(8 * qq, 8 * qq + 8))
+        if qq == 3:
+            act(o, a, AF.Copy)
+        else:
+            cp(o, a)
+    ts(ap("oh"), ap("iO"), 0.0, A.is_equal)
+    ts(cols("G", 7, 992, 8), cols("G", 7, 992, 8), float(2 ** 22 + 2048), A.add)
+    fill(ap("nb"), float(2 ** 63))
+    scan()
+    cp(cols("Pi", 0, 124), scl)
+    ts(cols("nb", 0, 1), cols("nb", 0, 1), -1.0, A.mult, cols("nb", 1, 2), A.mult)
+    for l in range(16):
+        act(ap("Wc", l, slice(l, 128, 16)), ap("G8"), AF.Copy)
+    act(ap("Ib"), If, AF.Copy)
+    unpack("JJ", "of")
+
+    def consts():
+        act(ap("Ic"), If, AF.Copy, scale=WP / 2)
+        act(ap("i8b"), ap("i8"), AF.Identity, bias=WP / 2)
+        for (a, b), c in zip(MC, CENTER):
+            act(cols("tgt", a, b), cols("i8", a, b), AF.Identity, bias=16.0 * 8192 * c, scale=-8192.0)
+
+    consts()
+
+    def recip(n):
+        w = W // OPT["RC"]
+        a = cols("rk", w * n, w * n + w)
+        add("v", lambda: g.vector.reciprocal(R(a), R(a)), [a], [a])
+
+    NB = {3: "N0", 0: "N1", 1: "N2", 2: "N0"}
+    HB = {3: "H0", 0: "H1", 1: "H0", 2: "H1"}
+    on_vector = lambda t: [c for c in (3, 0, 1, 2) if c not in OPT["QD"] or t == 4 or (t == 2 and c == 3)]
+
+    def load_n(t, c):
+        mm(bk(NB[c], c), If, ch("nv%d" % t, c))
+
+    def load_q(t, n):
+        if n < len(on_vector(t)):
+            c = on_vector(t)[n]
+            o = bk("Q%d" % (n % 2), c)
+            mm(o, ap("Ib"), st("q0b", c)) if t == 1 else mm(o, If, st("q", c))
+
+    def speeds(t):
+        for c in (3, 0, 1, 2):
+            tt(ch("nv%d" % t, c), ind(whole("vs"), lst("j%d" % t, c)), st("vs'", c), A.subtract)
+        load_n(t, 3), load_n(t, 0)
+
+    def tests(t, shot):
+        qn = "q0b" if t == 1 else "q"
+        load_q(t, 0), load_q(t, 1)
+        jj, of = ("JJ2", "of2") if t == 2 else ("JJ", "of")
+        win = cols(qn, 0, WP)
+        cnt = lambda e, a, b: [mm(cols("C", 124 * e + a, 124 * e + b), ap("Ib"), cols("bias", 124 * e + a, 124 * e + b), True, False)] + [
+            mm(cols("C", 124 * e + a, 124 * e + b), ap("Wc", l), ap("ind", e, slice(16 * a + l, 16 * b, 16)), False, l == 15) for l in range(16)]
+        ic = lambda e, c: ap("ind", e, slice(*CH[c]))
+        near = lambda e, c: act(ic(e, c), dd(e, c), AF.Abs, scale=348.0 / 512)
+        for c in (3, 0, 1, 2):
+            tt(dd(0, c), ind(win, lst(of, c)), st("q'", c), A.subtract)
+            near(0, c)
+            act(ic(0, c), ic(0, c), AF.Sign, bias=261.0 / 512, scale=-1.0)
+        cnt(0, 0, 124)
+        for c in range(4):
+            tt(dd(1, c), ind(win, lst(of, c, 124)), st("q'", c), A.subtract)
+            near(1, c)
+        for c in range(4):
+            ts(ic(1, c), ic(1, c), 261.0 / 512, A.is_le, 2.0, A.mult)
+            if c == 1:
+                tt(ap("A"), cols("C", 0, 124), cols(jj, 0, 124), A.min)
+            if c == 2:
+                cnt(1, 0, 96)
+        cnt(1, 96, 124)
+        spare()
+        m = cols("C", 124, 248)
+        tt(m, m, cols(jj, 124, 248), A.min)
+        tt(m, m, ap("A"), A.max)
+        act(ap("cw"), m, AF.Abs, bias=-2048.0)
+        act(ap("lvl"), m, AF.Sign, bias=-2048.0)
+        ts(ap("j%d" % t), ap("cw"), float(WP), A.min)
+
+    def mutual(t):
+        j, kn = "j%d" % t, "kA" if t <= 2 else "kB"
+        for b in range(16):
+            o = cols("X", PAD + b, WP, 16)
+            if b < OPT["NXV"]:
+                ts(o, ap("cw"), cols("oh", b, b + 1), A.mult)
+            else:
+                act(o, ap("cw"), AF.Copy, scale=cols("oh", b, b + 1))
+        speeds(t)
+
+        def back(a, b):
+            z = cols("C", 256 + a, 256 + b)
+            mm(z, If, cols("tgt", a, b), True, False)
+            for l in range(16):
+                mm(z, ap("Wc", l), cols("mg", 16 * a + l, 16 * b, 16), False, False)
+            mm(z, ap("Ic"), cols("lvl", a, b), False, False)
+            mm(z, If, cols("i8b", a, b), False, True)
+
+        for n, (a, b) in enumerate(MC):
+            act(cols("mg", 16 * a, 16 * b), ind(ap("X"), cols(j, a, b)), AF.Identity, bias=-float(CENTER[n]))
+            if n == 2:
+                back(0, b)
+        back(MC[3][0], 124)
+        load_n(t, 1)
+        k0 = "kk01" if t == 1 else "kk%d" % t
+        own = lambda c: ap("k3", t // 3) if c == 3 else st("kB" if t <= 2 else "kA", c)
+        kj = lambda c: tt(ch(k0, c), ind(ap(kn), lst(j, c)), own(c), A.mult)
+        kj(3), kj(0)
+        ts(ap("so"), cols("C", 256, 380), 0.0, A.max, float(2 * WP), A.min)
+        kj(1), kj(2)
+
+    def cursor_s(t):
+        if t == 4:
+            return
+        act(ap("ab"), cols("C", 256, 380), AF.Abs, bias=-2991.5)
+        act(ap("ab"), ap("ab"), AF.Sign, bias=992.25, scale=-1.0)
+        for n in range(3 if t == 2 else 1):
+            act(cols("C", 124 * n, 124 * n + 124), ap("ab"), AF.Relu)
+
+    def cursor_v(t):
+        if t == 1:
+            tt(cols("C", 0, 124), ap("curB"), cols("C", 0, 124), A.subtract)
+            yield
+            ts(ap("ci"), cols("C", 0, 124), 2.0, A.add)
+            yield
+            ts(ap("ci"), ap("ci"), 7, A.bitwise_and)
+            yield
+            cp(ap("c2"), ap("ci"))
+            mask("c2", 0)
+            yield
+            yield
+            scan()
+            cp(cols("Pi", 0, 124), scl)
+            mask("c2", 2)
+            yield
+            unpack("JJ2", "of2")
+            yield
+            yield
+            pair(2)
+            yield
+            yield
+            yield
+            extra.extend([lambda: pair(4), lambda: list(tables())])
+        elif t == 2:
+            tt(cols("C", 0, 372), cols("C", 0, 372), ap("TB"), A.mult)
+            yield
+            tt(cols("Pi", 0, 124), cols("C", 0, 124), cols("TA", 0, 124), A.add)
+            tt(ap("UV"), cols("C", 124, 372), cols("TA", 124, 372), A.add)
+            yield
+            unpack("JJ", "of")
+        elif t == 3:
+            tt(cols("C", 0, 124), cols("C", 0, 124), cols("UV", 124, 248), A.mult)
+            yield
+            tt(cols("Pi", 0, 124), cols("C", 0, 124), cols("UV", 0, 124), A.add)
+            yield
+            unpack("JJ", "of")
+
+    def pair(e):
+        scan()
+        act(cols("TA", 62 * e - 124, 62 * e), scl, AF.Copy)
+        if e == 2:
+            mask("c2", 4)
+
+    def tables():
+        cp(ap("Pi"), cols("TA", 0, 248))
+        ts(cols("PT", 0, 124), cols("JJ2", 124, 248), -2048.0, A.mult, float(2 ** 23 + 4096), A.add)
+        ts(ap("Ph"), ap("Pi"), 11, A.arith_shift_right)
+        ts(cols("Pi", 0, 124), cols("Pi", 0, 124), 2047, A.bitwise_and)
+        tt(cols("PT", 0, 124), cols("PT", 0, 124), cols("Ph", 0, 124), A.subtract)
+        ts(cols("PT", 124, 248), cols("Pi", 0, 124), -2048.0, A.mult, float(2 ** 23 + 4096), A.add)
+        tt(cols("TB", 0, 124), cols("PT", 0, 124), cols("TA", 0, 124), A.subtract)
+        tt(cols("PT", 124, 248), cols("PT", 124, 248), cols("Ph", 124, 248), A.subtract)
+        yield
+        tt(cols("TB", 124, 248), cols("PT", 124, 248), cols("TA", 124, 248), A.subtract)
+        tt(cols("TB", 248, 372), cols("TA", 0, 124), cols("PT", 124, 248), A.subtract)
+        act(cols("TA", 248, 372), cols("TB", 124, 248), AF.Copy)
+        yield
+        tt(cols("TB", 248, 372), cols("TB", 248, 372), cols("TB", 124, 248), A.subtract)
+
+    def recip_start():
+        for c in range(4):
+            act(ch("rk", c), st("kA", c), AF.Copy, scale=-0.0625)
+        extra.extend([lambda n=n: recip(n) for n in range(OPT["RC"])])
+
+    def update(t, shot):
+        again = shot == 1 and t == 1
+        sg, kk = "sg1" if t == 1 else "sg", "kk%d" % t
+        k0 = "kk01" if t == 1 else kk
+        qd = [c for c in range(4) if c not in on_vector(t)]
+        QB = {c: "Q%d" % (n % 2) for n, c in enumerate(on_vector(t))}
+        s = lambda c: None if again else act(ch(sg, c), ind(ap("D"), lst("so", c)), AF.Sign)
+        pr = lambda c: tt(ch("pr", c), bk(NB[c], c), ch(sg, c), A.mult)
+        h = lambda c: act(bk(HB[c], c), ch("pr", c), AF.Relu, scale=cols("nb", 0, 1))
+        k = lambda c: tt(ch(kk, c), bk(HB[c], c), ch(k0, c), A.min)
+        p = lambda c: tt(bk(HB[c], c), bk(NB[c], c), ch(kk, c), A.mult)
+
+        def v(c):
+            tt(st("vs", c), bk(HB[c], c), st("vs", c), A.add)
+            if c in qd or (t == 2 and c == 3):
+                act(st("vs'", c), st("vs", c), AF.Copy)
+            elif t < 4:
+                dma("y", st("vs'", c), st("vs", c))
+
+        def q(c):
+            if c in qd:
+                dma("g", st("q*", c), st("vs*", c), True)
+            elif t < 4:
+                tt(st("q", c), bk(QB[c], c), st("vs", c), A.add)
+                act(st("q'", c), st("q", c), AF.Copy)
+                if t == 2 and c == 3:
+                    send("q%d" % shot, vis("q"), nxt)
+                    send("v%d" % shot, vis("vs"), nxt)
+            else:
+                tt(bk(QB[c], c), bk(QB[c], c), st("vs", c), A.add)
+
+        def aq(c):
+            if t == 4:
+                tt(bk(QB[c], c), bk(QB[c], c), ch("aimA", c), A.subtract)
+                act(st("q", c), bk(QB[c], c), AF.Copy, scale=0.0625)
+                if c not in OPT["SD"]:
+                    act(st("q'", c), bk(QB[c], c), AF.Copy, scale=0.0625)
+                if c == 3:
+                    send("a%d" % shot, vis("q"), prv)
+
+        cur = iter(()) if again else cursor_v(t)
+        nx = lambda: next(cur, None)
+        s(3), pr(3), s(0), h(3), pr(0), s(1), h(0), k(3), pr(1), s(2)
+        if not again:
+            cursor_s(t)
+        p(3), load_n(t, 2), k(0), v(3), h(1), nx(), p(0), nx(), q(3), v(0), nx(), pr(2), h(2), nx(), aq(3), load_q(t, 2), q(0)
+        if (shot, t) == (0, 2):
+            recip_start()
+        if (shot, t) == (0, 3):
+            for c in range(4):
+                mm(bk("C", c), app("Sel", slice(0, 8)), app("aimA", slice(0, 8), slice(*CH[c])))
+                act(ch("aimA", c), bk("C", c), AF.Copy)
+        k(1), aq(0), load_q(t, 3), k(2), nx(), p(1), nx(), p(2), nx(), v(1), nx(), v(2)
+        if t == 2:
+            turn("q%d" % shot, vis2("q"), True, "N1")
+        nx(), q(1), nx(), q(2), nx(), aq(1), aq(2)
+        for _ in cur:
+            pass
+        if t == 2:
+            turn("v%d" % shot, [vis("vs")], True, "N2")
+            dma("y", vis("vs'"), vis("vs"))
+            spare()
+
+    KB = [{3: "N0", 0: "N1", 1: "N2", 2: "Q0"}, {3: "N0", 0: "N1", 1: "H0", 2: "H1"}]
+    YB = {3: "N2", 0: "Q0", 1: "Q1", 2: "C"}
+    late = []
+
+    def loadk(t, cs):
+        for c in cs:
+            act(bk(KB[t % 2][c], c), ch("kk%d" % t, c), AF.Copy, scale=-1.0 if c in OPT["SD"] else 1.0)
+
+    def backward(t, shot):
+        av, nv = "q" if t == 4 else "vs", "nv%d" % t
+        last = shot == 1 and t == 1
+        direct = shot == 0 and t == 4
+        bd = [c for c in OPT["BD"] if t > 1 and not (t == 3 and c == 3)]
+        yo = ("D", WP + PAD) if t % 2 else ("X", PAD)
+        yc = lambda a, b: cols(yo[0], yo[1] + a, yo[1] + b)
+        xb = lambda c: bk(KB[t % 2][c], c)
+        kb = lambda c: bk(KB[(t + (0 if last else 1)) % 2][c], c)
+        yb = lambda c: bk(YB[c], c)
+        x = lambda c: tt(xb(c), xb(c), dd(1, c), A.mult)
+
+        def a(c):
+            if c in bd:
+                tt(st("vs", c), xb(c), st(av, c), A.add)
+                act(st("vs'", c), st("vs", c), AF.Copy)
+            else:
+                tt(kb(c), xb(c), st(av, c), A.add)
+
+        def y(c):
+            o = yb(c) if last else ch("G", c) if direct else yc(*CH[c])
+            tt(o, xb(c), ch(nv, c), A.mult)
+
+        def gain(lo, hi):
+            if direct or last:
+                return
+            if t > 2 or hi < W:
+                dma("g", cols("G", lo, hi), yc(lo, hi), True)
+            else:
+                dma("g", cols("G", lo, V0), yc(lo, V0), True)
+                dma("g", ap("Gh"), yc(V0, W), not (shot == 0 and t == 2))
+
+        def b(c):
+            if c in bd:
+                dma("g", st("vs*", c), st("q*", c), True)
+            elif t > 1:
+                tt(st("vs", c), kb(c), st("q", c), A.add)
+                if t == 3 and c == 3:
+                    send("w%d" % shot, vis("vs"), prv)
+                if c not in OPT["SD"]:
+                    act(st("vs'", c), st("vs", c), AF.Copy)
+                loadk(t - 1, [c])
+            else:
+                ts(kb(c), kb(c), -0.1875, A.max, 0.1875, A.min)
+
+        def e(c):
+            if t == 1:
+                tt(ch("v0f", c), ch("v0f", c), kb(c), A.subtract)
+                if shot:
+                    dma("y", ("yv", (ALL, slice(*CH[c]))), ch("v0f", c))
+                else:
+                    act(st("vs", c), ch("v0f", c), AF.Copy, scale=0.0625)
+                    act(st("vs'", c), ch("v0f", c), AF.Copy, scale=0.0625)
+
+        for c in (3, 0, 1, 2):
+            if c in OPT["SD"]:
+                act(dd(1, c), ind(whole(av), lst("j%d" % t, c)), AF.Copy, scale=-1.0)
+                dma("g", dd(1, c), st(av, c), True)
+            else:
+                tt(dd(1, c), ind(whole(av), lst("j%d" % t, c)), st(av + "'", c), A.subtract)
+        if not last:
+            if t == 1:
+                x(3), x(0), y(3), y(0), a(3), a(0), b(3), b(0), e(3), e(0)
+            elif t == 3:
+                x(3), x(0), y(3), y(0), a(3), a(0), b(3), b(0), loadk(t - 1, [0])
+            else:
+                x(3), x(0), a(3), b(3), a(0), b(0), y(3), loadk(t - 1, [3]), y(0), loadk(t - 1, [0])
+            if late:
+                late.pop()()
+            elif t == 4:
+                spare(2)
+
+            def rest():
+                y(1), y(2), gain(0, W)
+                if (shot, t) == (1, 3):
+                    send("G", cols("G", V0, W), prv)
+
+            x(1), x(2)
+            if (shot, t) == (1, 2):
+                rest()
+            else:
+                late.append(rest)
+            a(1), a(2)
+            if t == 3:
+                turn("a%d" % shot, vis2("q"), False, "Q1")
+            b(1)
+            if t == 3:
+                turn("w%d" % shot, vis2("vs"), False, "C")
+            b(2), e(1), e(2)
+            if t == 3:
+                spare(2)
+            return
+        u1 = lambda c: tt(yb(c), yb(c), ch("G", c), A.add)
+
+        def u2(c):
+            if c == 3:
+                tt(yb(c), yb(c), ch("rk", c), A.mult)
+            else:
+                tt(ch("pr", c), yb(c), ch("rk", c), A.mult)
+                add("g", lambda: g.dma_start(T.yg[:, CH[c][0]:CH[c][1]], R(ch("pr", c)), accum_op=A.add), [ch("pr", c), ap("ones")], [], "d")
+
+        x(3), x(0), y(3), y(0), a(3), a(0), b(3), b(0), e(3), e(0)
+        x(1), x(2), y(1), y(2), u1(0), u1(1), u2(0), u1(2), u2(1), u2(2)
+        turn("G", cols("G", V0, W), False, "Q0", ap("Gh"))
+        a(1), a(2), u1(3), b(1), b(2), u2(3), e(1), e(2)
+        tt(ch("pr", 3), yb(3), st("kA", 3), A.add)
+        dma("s", ("yg", (ALL, slice(*CH[3]))), ch("pr", 3))
+
+    def q_start(rows):
+        for c in OPT["QD"]:
+            for n in rows:
+                dma("g", st(n, c), ("q0", (ALL, slice(*CH[c]))))
+
+    for shot in (0, 1):
+        for t in (1, 2, 3, 4):
+            first = shot == 0 and t == 1
+            if shot == 1 and t == 1:
+                q_start(["q", "q'"])
+                late.pop()()
+                speeds(1)
+                load_n(1, 1), load_q(1, 0), load_q(1, 1)
+            else:
+                if first:
+                    act(cols("pr", 0, VI), vis("kA"), AF.Copy)
+                    send("k", cols("pr", 0, VI), nxt)
+                    q_start(["q"])
+                    dma("g", ap("v0f"), ("v0", (ALL, ALL)))
+                    for c in (0, 1, 2):
+                        add("g", lambda c=c: g.dma_start(T.yg[:, CH[c][0]:CH[c][1]], T.kap[:, CH[c][0]:CH[c][1]]), [], [cols("ones", 4 * c, 4 * c + 4)], "d")
+                tests(t, shot)
+                mutual(t)
+                if (shot, t) == (0, 2):
+                    spare()
+            update(t, shot)
+            if (shot, t) == (0, 2):
+                turn("k", [vis("kB"), ap("k3", 1, slice(128, 448))], True, "N1")
+        loadk(4, [3, 0, 1, 2])
+        spare()
+        for t in (4, 3, 2, 1):
+            if shot == 1 and t == 1:
+                spare(99)
+            backward(t, shot)
+    return ops
+
+
+def order(ops):
+    wr, rd, bank = {}, {}, {}
+    flat = {n: np.arange(int(np.prod(s[1][1:]))).reshape(s[1][1:]) for n, s in SCRATCH.items()}
+    for n in SCRATCH:
+        wr[n] = np.full((4, flat[n].size), -1)
+        rd[n] = {}
+        bank[n] = {}
+
+    def region(x):
+        p = range(128)[x[1][0]]
+        return slice(p[0] // 32, p[-1] // 32 + 1), flat[x[0]][x[1][1:]].ravel()
+
+    who = lambda m: ops[m]["eng"] if ops[m]["kind"] == "c" else "x%d" % m
+    for n, o in enumerate(ops):
+        deps = set()
+        me = who(n)
+        for x in o["rd"]:
+            qd, c = region(x)
+            deps.update(int(m) for m in np.unique(wr[x[0]][qd][:, c]) if m >= 0 and not (me == "t" and who(m) == "t"))
+        for x in o["wr"]:
+            qd, c = region(x)
+            deps.update(int(m) for m in np.unique(wr[x[0]][qd][:, c]) if m >= 0 and not (me == "t" and who(m) == "t"))
+            for e, arr in rd[x[0]].items():
+                if not (me == "t" and e == "t"):
+                    deps.update(int(m) for m in np.unique(arr[qd][:, c]) if m >= 0)
+        for x in o["rd"] + o["wr"]:
+            if SCRATCH[x[0]][0] == "psum":
+                deps.update(m for e, m in bank[x[0]].items() if e != me)
+                bank[x[0]][me] = n
+        for x in o["rd"]:
+            qd, c = region(x)
+            arr = rd[x[0]].setdefault(me, np.full((4, flat[x[0]].size), -1))
+            arr[qd, c] = n
+        for x in o["wr"]:
+            qd, c = region(x)
+            wr[x[0]][qd, c] = n
+        deps.discard(n)
+        o["deps"] = deps
+    known = {e: {} for e in ENG}
+    for n, o in enumerate(ops):
+        kn, waits = known[o["eng"]], []
+        if o["kind"] != "a":
+            for m in sorted(o["deps"], reverse=True):
+                if kn.get(who(m), -1) < m:
+                    waits.append(m)
+                    kn[who(m)] = m
+                    for k2, m2 in ops[m]["snap"].items():
+                        kn[k2] = max(kn.get(k2, -1), m2)
+        o["waits"] = waits
+        o["snap"] = {} if o["kind"] == "a" else dict(kn)
+    return known
+
+
+def rank_program(g, core, T, topo):
+    rank = T.rank_of(core)
+    if rank is None:
+        return
+    n = len(T.cores)
+    nxt, prv = T.cores[(rank + 1) % n], T.cores[(rank - 1) % n]
+    ops = build(g, T, nxt, prv)
+    known = order(ops)
+    wanted = set(m for o in ops for m in o["waits"])
+    count = {e: 0 for e in ENG}
+    nd = 0
+    for m, o in enumerate(ops):
+        if o["kind"] == "c":
+            if m in wanted:
+                count[o["eng"]] += 1
+                o["tok"] = ("e_" + o["eng"], count[o["eng"]])
+        elif o["kind"] == "a":
+            src = prv if o["msg"][0] in "kqv" else nxt
+            o["tok"] = ("r_" + o["msg"], len(topo.engines(src, core)))
+        else:
+            o["tok"] = ("d%d" % nd, 16 if o["kind"] == "d" else len(topo.engines(core, o["to"])))
+            nd += 1
+    qu = {"v": g.vector, "s": g.scalar, "t": g.tensor, "g": g, "y": g.sync}
+    for o in ops:
+        for m in o["waits"]:
+            qu[o["eng"]].wait_ge(T.sem[ops[m]["tok"][0]], ops[m]["tok"][1])
+        if o["kind"] == "a":
+            continue
+        if o["kind"] == "r":
+            rid, pid = topo.addr(o["to"])[:2]
+            g.remote_dma(T["l_" + o["msg"][0]][:], o["src"], T.sem["r_" + o["msg"]], T.sem[o["tok"][0]], pid, rid, topo.mask(core, o["to"]))
+            continue
+        ins = o["f"]()
+        if "tok" in o:
+            ins.then_inc(T.sem[o["tok"][0]], 16 if o["kind"] == "d" else 1)
+    for m, o in enumerate(ops):
+        if o["kind"] != "c" and known["g"].get("x%d" % m, -1) < m:
+            g.wait_ge(T.sem[o["tok"][0]], o["tok"][1])
+    for e in ENG:
+        if count[e]:
+            g.wait_ge(T.sem["e_" + e], count[e])

@@ -3,41 +3,49 @@ from concourse.mybir import AluOpType, ActivationFunctionType
 
 W, V0, VI, PAD = 1984, 1664, 320, 8
 WP = W + PAD
-CH = [(0, 512), (512, 1024), (1024, 1536), (1536, W)]
 MC = [(0, 26), (26, 52), (52, 78), (78, 104), (104, 124)]
+CH = [(16 * a, 16 * b) for a, b in MC]
+VC = 4
+ORD = (4, 3, 2, 1, 0)
 CENTER = [8 * (a + b) + 8 for a, b in MC]
+NEAR = 11228502 * 2.0 ** -24
+GRID = 1.5 * 2 ** 23
 F, B, I, U = "float32", "bfloat16", "int32", "uint16"
 MSG = ["k", "q0", "v0", "a0", "w0", "q1", "v1", "a1", "w1", "G"]
 
 SCRATCH = {}
 for _n, _s, _d in (
-    [("q", [2, WP + PAD], F), ("vs", [2, WP + PAD], F), ("k3", [2, 448], B), ("D", [2 * WP + PAD], F), ("X", [WP + PAD], F), ("pr", [W], F), ("kk01", [W], F),
-     ("G", [W], F), ("Gh", [VI], F), ("rk", [W], F), ("v0f", [W], F), ("ind", [2, W], B), ("mg", [W], B), ("sg", [W], B), ("sg1", [W], B),
-     ("q0b", [WP], B), ("kA", [WP + PAD], B), ("kB", [WP + PAD], B), ("aimA", [W], B), ("Wc", [16, 128], B),
-     ("E", [256], F), ("ones", [128], F), ("Ib", [128], B), ("Ic", [128], B), ("Sel", [128], B),
-     ("L", [16, 8], F), ("L1", [16, 8], F), ("L2", [16, 8], F),
+    [("q", [2, WP + PAD], F), ("vs", [2, WP + PAD], F), ("kV", [2, VI], B), ("D", [2, W], F), ("Ew", [2 * WP + PAD], B), ("X", [WP + PAD], F),
+     ("kk01", [W], F), ("G", [W], F), ("Gh", [VI], F), ("rk", [W], F), ("v0f", [W], F), ("ind", [2, W], B), ("mg", [W], B), ("pr", [W], B),
+     ("sg1", [W], B), ("q0b", [WP], B), ("kA", [WP + PAD], B), ("kB", [WP + PAD], B), ("aimA", [W], B), ("Wc", [16, 128], B),
+     ("E", [256], F), ("Eb", [256], B), ("ones", [128], F), ("Nf", [128], F), ("Nb", [128], B), ("Ic", [128], B), ("Sel", [128], B),
+     ("BP", [128], B), ("BN", [128], B), ("L", [16, 8], F), ("L1", [16, 8], F), ("L2", [16, 8], F),
      ("iL", [16, 8], I), ("iS", [128], I), ("iO", [16], I), ("iG", [8], I), ("iP", [1], I), ("pcol", [1], F), ("oh", [16], F),
-     ("G8", [8], B), ("nb", [2], F), ("bias", [248], B), ("i8", [124], F), ("i8b", [124], F), ("tgt", [124], F),
+     ("G8", [8], B), ("bias", [124], B), ("i8", [124], F), ("i8b", [124], F), ("tgt", [124], F),
      ("ct", [2, 31, 16], I), ("conf", [31, 32], F),
      ("cu", [2, 4, 16], I), ("cf", [4, 32], F), ("cf2", [4, 32], F), ("curB", [124], F), ("c2", [124], F), ("ci", [124], I),
      ("Pi", [248], I), ("Ph", [248], I), ("JJ", [248], I), ("JJ2", [248], I), ("of", [248], U), ("of2", [248], U), ("A", [124], F),
      ("cw", [124], F), ("lvl", [124], B), ("so", [124], U), ("ab", [124], F),
-     ("PT", [248], F), ("TA", [372], F), ("TB", [372], F), ("UV", [248], F)]
+     ("PT", [248], F), ("TA", [372], F), ("TB", [372], F), ("UV", [248], F), ("l_k", [VI], B)]
     + [("kk%d" % t, [W], F) for t in (1, 2, 3, 4)] + [("nv%d" % t, [W], F) for t in (1, 2, 3, 4)]
-    + [("j%d" % t, [124], U) for t in (1, 2, 3, 4)] + [("l_" + m, [VI], F) for m in "kqvawG"]
+    + [("j%d" % t, [124], U) for t in (1, 2, 3, 4)] + [("l_" + m, [VI], F) for m in "qvawG"]
 ):
     SCRATCH[_n] = ("sbuf", [128] + _s, _d)
-for _n in ("N0", "N1", "N2", "H0", "H1", "Q0", "Q1", "C"):
+BANKS = ["P%d" % _n for _n in range(8)]
+for _n in BANKS:
     SCRATCH[_n] = ("psum", [128, 512], F)
 ENG = ["v", "s", "t", "g", "y"]
 SEMAPHORES = ["e_" + e for e in ENG] + ["d%d" % n for n in range(130)] + ["r_" + m for m in MSG]
 
 ALL = slice(None)
-OPT = {"NXV": 6,
-       "QD": (3, 0),
-       "BD": (3, 0),
-       "SD": (1, 2),
-       "RC": 16}
+OPT = {"T0": "VVVPP", "T1": "VVVPP",
+       "F0": "VVVPP", "F1": "VVVPP",
+       "E0": "SSSSS", "E1": "VSSSS", "INV": 1, "VV": "VVVVV",
+       "DV": "DdPVV", "D1": "PPPVV", "K0": "VVVVV", "MG": "SSSSS", "PR": "SSSVV", "Q": "VVPDd", "Q2": "DDDDD", "AQ": "VVPPP",
+       "DA": "PPPVV", "BB": "VVVVV", "GG": "DdDdd", "YA": "AAAAA", "C0": "PVVVV", "C1": "VVDdd", "U": "PVVVP", "TF": True,
+       "NXV": 8, "MV": 0, "HALF": ((0, 78), (78, 124)), "BACK": ((104, 124), (52, 104), (0, 52)), "RES": 1, "ALPHA": 0.2, "LEAD": 1.0, "STEP": 0.0, "FIRST": 4.0, "PASS": 3, "PRIO": "order", "CUR": 3, "THEN": ((4, 3, 2), (1, 0), ()),
+       "GI": 1.1, "GD": 2.2, "RD": 3.0, "RC": 2.5, "HOP": 0.12}
+CY, PE, GA = 0.83e-3, 0.42e-3, 1.56
 
 
 def ap(name, *idx):
@@ -49,8 +57,8 @@ def app(name, part, *idx):
 
 
 def cols(name, a, b, step=None):
-    if name[-1] in "'*":
-        return (name[:-1], (ALL, 1 if name[-1] == "'" else ALL, slice(a, b, step)))
+    if name[-1] == "'":
+        return (name[:-1], (ALL, 1, slice(a, b, step)))
     if name in ("q", "vs"):
         return (name, (ALL, 0, slice(a, b, step)))
     return (name, (ALL, slice(a, b, step)))
@@ -60,96 +68,152 @@ def ind(win, off):
     return ("@", win, off)
 
 
-def build(g, T, nxt, prv):
+FLAT = {n: np.arange(int(np.prod(s[1][1:]))).reshape(s[1][1:]) for n, s in SCRATCH.items()}
+
+
+def psum(x):
+    return x[0][0] == "#" or x[0] in BANKS
+
+
+def flat(name):
+    return FLAT["P0" if name[0] == "#" else name]
+
+
+def size(x):
+    return 16 * size(x[2]) if x[0] == "@" else int(flat(x[0])[x[1][1:]].size)
+
+
+def narrow(*xs):
+    return all(not psum(x) and SCRATCH[x[0]][2] in (B, U) for x in xs)
+
+
+def build(g, T, nxt, prv, place):
     A, AF = AluOpType, ActivationFunctionType
     ops = []
+    nb, lead, mark = [0], [0], [0, 0]
+
+    def bank():
+        nb[0] += 1
+        return "#%d" % nb[0]
 
     def R(x):
         if not isinstance(x, tuple):
             return x
         if x[0] == "@":
             return R(x[1]).indirect(R(x[2]))
-        return T[x[0]][x[1]]
+        return T[place.get(x[0], x[0])][x[1]]
 
     def parts(xs):
         out = []
         for x in xs:
             if isinstance(x, tuple):
                 out += [x[1], x[2]] if x[0] == "@" else [x]
-        return [x for x in out if x[0] in SCRATCH]
+        return [x for x in out if x[0] in SCRATCH or x[0][0] == "#"]
 
-    def add(eng, f, rd, wr, kind="c", **kw):
-        ops.append(dict(eng=eng, f=f, rd=parts(rd), wr=parts(wr), kind=kind, **kw))
+    def add(eng, f, rd, wr, cost, kind="c", **kw):
+        ops.append(dict(eng=eng, f=f, rd=parts(rd), wr=parts(wr), cost=cost, kind=kind, lead=lead[0], **kw))
+
+    def chunks():
+        for n, c in enumerate(ORD):
+            lead[0] = OPT["STEP"] * (len(ORD) - 1 - n)
+            yield c
+        lead[0] = 0
+
+    def price(o, a, b=None):
+        if a[0] == "@":
+            return 0.06 + size(a) * GA * CY
+        r = 0.5 if narrow(o, a) else 1.0
+        if b is not None:
+            r = 1.0 if psum(a) or psum(b) else 2.0
+        return 0.04 + max(64, size(a) * r) * CY
 
     def tt(o, a, b, op):
-        add("v", lambda: g.vector.tensor_tensor(R(o), R(a), R(b), op), [a, b], [o])
+        add("v", lambda: g.vector.tensor_tensor(R(o), R(a), R(b), op), [a, b], [o], price(o, a, b))
 
     def ts(o, a, s1, op0, s2=None, op1=None):
         if op1 is None:
-            add("v", lambda: g.vector.tensor_scalar(R(o), R(a), R(s1), None, op0), [a, s1], [o])
+            add("v", lambda: g.vector.tensor_scalar(R(o), R(a), R(s1), None, op0), [a, s1], [o], price(o, a))
         else:
-            add("v", lambda: g.vector.tensor_scalar(R(o), R(a), R(s1), R(s2), op0, op1), [a, s1, s2], [o])
+            add("v", lambda: g.vector.tensor_scalar(R(o), R(a), R(s1), R(s2), op0, op1), [a, s1, s2], [o], price(o, a))
 
     def cp(o, a):
-        add("v", lambda: g.vector.tensor_copy(R(o), R(a)), [a], [o])
+        add("v", lambda: g.vector.tensor_copy(R(o), R(a)), [a], [o], price(o, a))
 
     def fill(o, c):
-        add("v", lambda: g.vector.memset(R(o), c), [], [o])
+        add("v", lambda: g.vector.memset(R(o), c), [], [o], price(o, o))
 
     def flip(o, a):
-        add("v", lambda: g.vector.transpose(R(o), R(a)), [a], [o])
+        add("v", lambda: g.vector.transpose(R(o), R(a)), [a], [o], price(o, a))
 
-    def act(o, a, func, bias=0.0, scale=1.0):
-        add("s", lambda: g.scalar.activation(R(o), R(a), func, bias=R(bias), scale=R(scale)), [a, bias, scale], [o])
+    def act(o, a, func, bias=0.0, scale=1.0, more=0.0, **kw):
+        c = price(o, a) if a[0] == "@" else 0.05 + max(64, size(a)) * CY
+        add("s", lambda: g.scalar.activation(R(o), R(a), func, bias=R(bias), scale=R(scale)), [a, bias, scale], [o], c + more, **kw)
 
-    def mm(o, l, r, start=True, stop=True):
-        add("t", lambda: g.tensor.matmul(R(o), R(l), R(r), start, stop), [l, r], [o])
+    def mm(o, l, r, start=True, stop=True, early=False):
+        c = max(64, size(r)) * PE * (1 if narrow(r) else 4)
+        add("t", lambda: g.tensor.matmul(R(o), R(l), R(r), start, stop), [l, r], [o], c, early=early or (start and not stop))
+
+    def total(o, *terms):
+        for n, (l, r) in enumerate(terms):
+            mm(o, l, r, n == 0, n == len(terms) - 1, early=n == 0 and len(terms) > 1)
 
     def iota(o, pattern, base, mult):
+        c = 0.13 + 2 * size(o) * CY
         if SCRATCH[o[0]][2] != I:
-            add("g", lambda: g.iota(R(o), pattern, base, mult, allow_small_or_imprecise_dtypes=True), [], [o])
+            add("g", lambda: g.iota(R(o), pattern, base, mult, allow_small_or_imprecise_dtypes=True), [], [o], c)
         else:
-            add("g", lambda: g.iota(R(o), pattern, base, mult), [], [o])
+            add("g", lambda: g.iota(R(o), pattern, base, mult), [], [o], c)
 
     def dma(eng, o, a, acc=False):
         qu = {"g": g, "s": g.scalar, "y": g.sync}[eng]
+        x = o if o[0] in SCRATCH else a
+        c = size(x) * (2 if narrow(x) else 4) * 128 / 600e3
         if acc:
-            add(eng, lambda: qu.dma_start(R(o), R(a), accum_op=A.add), [a, o], [o], "d")
+            add(eng, lambda: qu.dma_start(R(o), R(a), accum_op=A.add), [a, o], [o], 2 * c, "d")
         else:
-            add(eng, lambda: qu.dma_start(R(o), R(a)), [a], [o], "d")
+            add(eng, lambda: qu.dma_start(R(o), R(a)), [a], [o], c, "d")
 
     def send(m, src, to):
-        add("g", None, [src], [], "r", msg=m, src=R(src), to=to)
+        add("g", None, [src], [], OPT["RC"], "r", msg=m, src=R(src), to=to)
 
-    def turn(m, dst, fwd, bank, plus=None):
-        add("t", None, [], [ap("l_" + m[0])], "a", msg=m)
+    def arrive(m):
+        add("t", None, [], [ap("l_" + m[0])], 0.0, "a", msg=m)
+
+    def turn(fwd, msgs, outs, plus=(), onto=None):
+        z = bank()
         s1 = 16 if fwd else 112
-        mm(cols(bank, 0, 160), cols("E", 128 - s1, 256 - s1), cols("l_" + m[0], 0, 160))
-        mm(cols(bank, 160, 320), cols("E", 64, 192), cols("l_" + m[0], 160, 320))
-        if plus is None:
-            for d in dst:
-                act(d, cols(bank, 0, VI), AF.Copy)
-        else:
-            tt(dst, plus, cols(bank, 0, VI), A.add)
+        for a, b, lo in ((0, 160, 128 - s1), (160, 320, 64)):
+            total(cols(z, a, b), *([(cols("Eb" if m == "k" else "E", lo, lo + 128), cols("l_" + m[0], a, b)) for m in msgs]
+                                   + [(If, cols(n, a, b)) for n in plus]))
+        if onto:
+            tt(onto[0], cols(z, 0, VI), onto[1], A.add)
+        for d in outs:
+            act(d, cols(z, 0, VI), AF.Copy)
 
-    If = cols("E", 0, 128)
+    If, Ib, Nf, Nb = cols("E", 0, 128), cols("Eb", 0, 128), ap("Nf"), ap("Nb")
     vis = lambda n: cols(n, PAD + V0, WP)
-    vis2 = lambda n: [vis(n), vis(n + "'")]
     whole = lambda n: cols(n, 0, WP + PAD)
     DT = cols("G", 0, 992)
     st = lambda n, c: cols(n, PAD + CH[c][0], PAD + CH[c][1])
     ch = lambda n, c: cols(n, CH[c][0], CH[c][1])
     bk = lambda n, c: cols(n, 0, CH[c][1] - CH[c][0])
-    lst = lambda n, c, o=0: cols(n, o + CH[c][0] // 16, o + CH[c][1] // 16)
-    DOFF = (WP + PAD, PAD)
-    dd = lambda e, c: cols("D", DOFF[e] + CH[c][0], DOFF[e] + CH[c][1])
+    lst = lambda n, c, o=0: cols(n, o + MC[c][0], o + MC[c][1])
+    two = lambda n, e, c: ap(n, e, slice(*CH[c]))
+    EOFF = (WP + PAD, PAD)
+    ew = lambda e, c: cols("Ew", EOFF[e] + CH[c][0], EOFF[e] + CH[c][1])
     msk, sc, scl = cols("rk", 0, 992), cols("rk", 992, W), cols("rk", 999, W, 8)
-    extra = []
+    q_twice = lambda c: "V" in (OPT["T0"][c], OPT["T1"][c])
+    dv = lambda t, shot: "D1" if (shot, t) == (1, 1) else "DV"
+    v_twice = lambda c, key="DV": OPT[key][c] == "V"
+    ups = lambda t, shot, c: OPT[dv(t, shot)][c] != "V"
 
-    def spare(n=1):
-        for _ in range(n):
-            if extra:
-                extra.pop(0)()
+    def span(key, c, off=0, top=VC):
+        if OPT[key][c] == "d":
+            return None
+        h = c
+        while h < top and OPT[key][h + 1] == "d":
+            h += 1
+        return off + CH[c][0], off + CH[h][1]
 
     fill(ap("cu"), 0)
     fill(ap("ones"), 1.0)
@@ -159,13 +223,13 @@ def build(g, T, nxt, prv):
     for gi in range(8):
         a, y = gi // 2, gi % 2
         dma("y" if y else "s", app("cu", slice(32 * a, 32 * a + 31), y), ("cur", (gi, ALL)))
-    dma("y", ap("sg"), ("v0", (ALL, ALL)))
     dma("y", cols("q0b", PAD, WP), ("q0", (ALL, ALL)))
+    dma("y", ap("sg1"), ("q0", (ALL, ALL)))
+    dma("y", ap("pr"), ("v0", (ALL, ALL)))
     dma("y", cols("kA", PAD, WP), ("kap", (ALL, ALL)))
-    dma("y", app("aimA", slice(0, 8)), ("aim", (ALL, ALL)))
-    dma("y", ap("k3", 0), ("kap", (ALL, slice(*CH[3]))))
-    dma("y", ap("k3", 1, slice(0, 128)), ("kap", (ALL, slice(CH[3][0], V0))))
+    dma("y", ap("kV", 0), ("kap", (ALL, slice(V0, W))))
     dma("y", cols("kB", PAD, PAD + V0), ("kap", (ALL, slice(0, V0))))
+    dma("y", app("aimA", slice(0, 8)), ("aim", (ALL, ALL)))
     iota(ap("iL"), [[-32, 4], [-1, 4], [-4, 8]], 0, 1)
     iota(ap("iG"), [[-16, 8]], 128, 1)
     iota(ap("iS"), [[1, 128]], 2048, -16)
@@ -174,16 +238,14 @@ def build(g, T, nxt, prv):
     iota(ap("i8"), [[16, 124]], 8, 0)
     for h in (0, 1):
         add("g", lambda h=h: g.affine_select(R(cols("E", 128 * h, 128 * h + 128)), R(ap("ones")), [[-1, 128]], A.is_equal, 0.0, 0, 1),
-            [ap("ones")], [cols("E", 128 * h, 128 * h + 128)])
-    dma("g", cols("q'", PAD, WP), ("q0", (ALL, ALL)))
-    iota(cols("q0b", 0, PAD), [[0, PAD]], 0, 0)
-    iota(ap("Wc"), [[0, 2048]], 0, 0)
-    iota(cols("bias", 0, 124), [[0, 124]], -8192, 0)
-    iota(cols("bias", 124, 248), [[0, 124]], -17 * 8192, 0)
-    for n in ("vs", "X", "D", "kA", "q", "kB"):
-        iota(cols(n, 0, PAD), [[0, PAD]], 0, 0)
-        iota(cols(n, WP, WP + PAD), [[0, PAD]], 0, 0)
-    iota(cols("D", 2 * WP, 2 * WP + PAD), [[0, PAD]], 0, 0)
+            [ap("ones")], [cols("E", 128 * h, 128 * h + 128)], 0.4)
+    fill(cols("q0b", 0, PAD), 0.0)
+    fill(ap("Wc"), 0.0)
+    fill(ap("bias"), -8.5 * 16384)
+    for n in ("vs", "vs'", "X", "Ew", "kA", "q", "kB"):
+        fill(cols(n, 0, PAD), 0.0)
+        fill(cols(n, WP, WP + PAD), 0.0)
+    fill(cols("Ew", 2 * WP, 2 * WP + PAD), 0.0)
     ts(ap("L"), ap("iL"), 0.0, A.is_equal, 2048.0, A.mult)
     ts(ap("L1", ALL, slice(0, 7)), ap("iL", ALL, slice(0, 7)), 4.0, A.is_equal, -2049.0, A.mult)
     ts(ap("L1", ALL, 7), ap("iL", ALL, 7), -28.0, A.is_equal, -1.0, A.mult)
@@ -193,16 +255,19 @@ def build(g, T, nxt, prv):
     ts(ap("iG"), ap("iG"), 4, A.arith_shift_right)
     ts(ap("iS"), ap("iS"), 4, A.arith_shift_right)
     tt(ap("L", ALL, slice(0, 7)), ap("L", ALL, slice(0, 7)), ap("L2", ALL, slice(0, 7)), A.add)
-    ts(ap("Sel"), ap("iS"), 128.0, A.is_equal)
-    act(cols("vs", PAD, WP), ap("sg"), AF.Copy, scale=0.0625)
-    dma("y", cols("vs'", PAD, WP), cols("vs", PAD, WP))
+    ts(ap("Sel"), ap("iS"), 128.0, A.is_equal, -1.0, A.mult)
+    for c in ORD:
+        act(st("vs", c), ch("pr", c), AF.Copy, scale=0.0625)
+        if v_twice(c):
+            dma("y", st("vs'", c), st("vs", c))
     for y in (0, 1):
         ts(ap("conf", ALL, slice(16 * y, 16 * y + 16)), ap("ct", y), 8.0, A.add)
-    mm(cols("N0", 0, 512), ap("L"), ap("conf", slice(0, 16)))
-    mm(cols("N1", 0, 480), ap("L"), ap("conf", slice(16, 31)))
+    n0, n1 = bank(), bank()
+    mm(cols(n0, 0, 512), ap("L"), ap("conf", slice(0, 16)))
+    mm(cols(n1, 0, 480), ap("L"), ap("conf", slice(16, 31)))
     for y in (0, 1):
         cp(ap("cf", ALL, slice(16 * y, 16 * y + 16)), ap("cu", y))
-    ts(ap("G8"), ap("iG"), 8.0, A.is_equal, 8192.0, A.mult)
+    ts(ap("G8"), ap("iG"), 8.0, A.is_equal, 16384.0, A.mult)
     flip(ap("cf2"), ap("cf"))
     ts(ap("iP"), ap("iP"), 15, A.bitwise_and)
     for z in range(4):
@@ -210,10 +275,13 @@ def build(g, T, nxt, prv):
 
     def mask(src, e):
         for m in range(8):
-            act(cols("rk", m, 992, 8), ap(src), AF.Abs, bias=-float(2 ** 24) * ((m - e) & 7), scale=float(2 ** 24))
+            if m < OPT["MV"]:
+                ts(cols("rk", m, 992, 8), ap(src), float((m - e) & 7), A.not_equal, float(2 ** 24), A.mult)
+            else:
+                act(cols("rk", m, 992, 8), ap(src), AF.Abs, bias=-float(2 ** 24) * ((m - e) & 7), scale=float(2 ** 24))
 
     def scan():
-        add("v", lambda: g.vector.tensor_tensor_scan(R(sc), R(msk), R(DT), 8.0e6, A.min, A.add), [msk, DT], [sc])
+        add("v", lambda: g.vector.tensor_tensor_scan(R(sc), R(msk), R(DT), 8.0e6, A.min, A.add), [msk, DT], [sc], 0.04 + 992 * CY)
 
     def unpack(jj, of):
         ts(cols(jj, 0, 124), cols("Pi", 0, 124), 11, A.arith_shift_right)
@@ -222,92 +290,92 @@ def build(g, T, nxt, prv):
         ts(cols(of, 124, 248), cols(jj, 124, 248), -1.0, A.mult, 2048.0, A.add)
 
     mask("curB", 0)
-    flip(ap("conf", slice(0, 16)), cols("N0", 0, 512))
+    flip(ap("conf", slice(0, 16)), cols(n0, 0, 512))
     cp(ap("pcol"), ap("iP"))
     ts(ap("iO"), ap("iO"), 15, A.bitwise_and)
-    flip(ap("conf", slice(16, 31)), cols("N1", 0, 480))
+    flip(ap("conf", slice(16, 31)), cols(n1, 0, 480))
     ts(ap("i8"), ap("i8"), ap("pcol"), A.add)
     for qq in range(4):
         o, a = cols("G", 248 * qq, 248 * qq + 248), ap("conf", ALL, slice(8 * qq, 8 * qq + 8))
-        if qq == 3:
+        if qq % 2:
             act(o, a, AF.Copy)
         else:
             cp(o, a)
     ts(ap("oh"), ap("iO"), 0.0, A.is_equal)
     ts(cols("G", 7, 992, 8), cols("G", 7, 992, 8), float(2 ** 22 + 2048), A.add)
-    fill(ap("nb"), float(2 ** 63))
     scan()
     cp(cols("Pi", 0, 124), scl)
-    ts(cols("nb", 0, 1), cols("nb", 0, 1), -1.0, A.mult, cols("nb", 1, 2), A.mult)
     for l in range(16):
         act(ap("Wc", l, slice(l, 128, 16)), ap("G8"), AF.Copy)
-    act(ap("Ib"), If, AF.Copy)
+    act(ap("Eb"), ap("E"), AF.Copy)
+    act(Nf, If, AF.Copy, scale=-1.0)
+    act(Nb, If, AF.Copy, scale=-1.0)
+    act(ap("BP"), If, AF.Copy, scale=float(2 ** 63))
+    act(ap("BN"), ap("BP"), AF.Copy, scale=-float(2 ** 63))
+    act(ap("BP"), ap("BP"), AF.Copy, scale=float(2 ** 63))
     unpack("JJ", "of")
+    act(ap("Ic"), If, AF.Copy, scale=WP / 2)
+    act(ap("i8b"), ap("i8"), AF.Identity, bias=WP / 2)
+    for (a, b), c in zip(MC, CENTER):
+        act(cols("tgt", a, b), cols("i8", a, b), AF.Identity, bias=16.0 * 16384 * c, scale=-16384.0)
 
-    def consts():
-        act(ap("Ic"), If, AF.Copy, scale=WP / 2)
-        act(ap("i8b"), ap("i8"), AF.Identity, bias=WP / 2)
-        for (a, b), c in zip(MC, CENTER):
-            act(cols("tgt", a, b), cols("i8", a, b), AF.Identity, bias=16.0 * 8192 * c, scale=-8192.0)
+    def speeds(t, shot, c):
+        nv, key = ch("nv%d" % t, c), dv(t, shot)
+        if OPT[key][c] == "P":
+            z = bk(bank(), c)
+            mm(z, If, st("vs", c), True, False)
+            act(nv, ind(whole("vs"), lst("j%d" % t, c)), AF.Copy)
+            mm(z, Nf, nv, False, True)
+            act(nv, z, AF.Copy)
+        elif OPT[key][c] != "V":
+            act(nv, ind(whole("vs"), lst("j%d" % t, c)), AF.Copy, scale=-1.0)
+            if span(key, c):
+                dma("g", cols("nv%d" % t, *span(key, c)), cols("vs", *span(key, c, PAD)), True)
+        else:
+            tt(nv, ind(whole("vs"), lst("j%d" % t, c)), st("vs'", c), A.subtract)
 
-    consts()
-
-    def recip(n):
-        w = W // OPT["RC"]
-        a = cols("rk", w * n, w * n + w)
-        add("v", lambda: g.vector.reciprocal(R(a), R(a)), [a], [a])
-
-    NB = {3: "N0", 0: "N1", 1: "N2", 2: "N0"}
-    HB = {3: "H0", 0: "H1", 1: "H0", 2: "H1"}
-    on_vector = lambda t: [c for c in (3, 0, 1, 2) if c not in OPT["QD"] or t == 4 or (t == 2 and c == 3)]
-
-    def load_n(t, c):
-        mm(bk(NB[c], c), If, ch("nv%d" % t, c))
-
-    def load_q(t, n):
-        if n < len(on_vector(t)):
-            c = on_vector(t)[n]
-            o = bk("Q%d" % (n % 2), c)
-            mm(o, ap("Ib"), st("q0b", c)) if t == 1 else mm(o, If, st("q", c))
-
-    def speeds(t):
-        for c in (3, 0, 1, 2):
-            tt(ch("nv%d" % t, c), ind(whole("vs"), lst("j%d" % t, c)), st("vs'", c), A.subtract)
-        load_n(t, 3), load_n(t, 0)
-
-    def tests(t, shot):
+    def tests(t):
         qn = "q0b" if t == 1 else "q"
-        load_q(t, 0), load_q(t, 1)
         jj, of = ("JJ2", "of2") if t == 2 else ("JJ", "of")
         win = cols(qn, 0, WP)
-        cnt = lambda e, a, b: [mm(cols("C", 124 * e + a, 124 * e + b), ap("Ib"), cols("bias", 124 * e + a, 124 * e + b), True, False)] + [
-            mm(cols("C", 124 * e + a, 124 * e + b), ap("Wc", l), ap("ind", e, slice(16 * a + l, 16 * b, 16)), False, l == 15) for l in range(16)]
-        ic = lambda e, c: ap("ind", e, slice(*CH[c]))
-        near = lambda e, c: act(ic(e, c), dd(e, c), AF.Abs, scale=348.0 / 512)
-        for c in (3, 0, 1, 2):
-            tt(dd(0, c), ind(win, lst(of, c)), st("q'", c), A.subtract)
-            near(0, c)
-            act(ic(0, c), ic(0, c), AF.Sign, bias=261.0 / 512, scale=-1.0)
-        cnt(0, 0, 124)
-        for c in range(4):
-            tt(dd(1, c), ind(win, lst(of, c, 124)), st("q'", c), A.subtract)
-            near(1, c)
-        for c in range(4):
-            ts(ic(1, c), ic(1, c), 261.0 / 512, A.is_le, 2.0, A.mult)
-            if c == 1:
-                tt(ap("A"), cols("C", 0, 124), cols(jj, 0, 124), A.min)
-            if c == 2:
-                cnt(1, 0, 96)
-        cnt(1, 96, 124)
-        spare()
-        m = cols("C", 124, 248)
-        tt(m, m, cols(jj, 124, 248), A.min)
-        tt(m, m, ap("A"), A.max)
-        act(ap("cw"), m, AF.Abs, bias=-2048.0)
-        act(ap("lvl"), m, AF.Sign, bias=-2048.0)
-        ts(ap("j%d" % t), ap("cw"), float(WP), A.min)
+        for a, b in OPT["HALF"]:
+            cnt = []
+            lead[0] = OPT["FIRST"] * ((a, b) == OPT["HALF"][0])
+            for e in (0, 1):
+                for c in [c for c in ORD if a <= MC[c][0] < b]:
+                    how, got = OPT["FT"[t > 1] + str(e)][c], ind(win, lst(of, c, 124 * e))
+                    d, s = two("D", e, c), NEAR
+                    if how == "V":
+                        tt(d, got, ch("sg1", c) if t == 1 else st("q'", c), A.subtract)
+                        s = -NEAR
+                    elif how == "D":
+                        act(d, got, AF.Copy, scale=-1.0)
+                        dma("g", d, st("q", c), True)
+                    else:
+                        x = two("ind", e, c) if t == 1 else d
+                        d = bk(bank(), c)
+                        mm(d, Ib if t == 1 else If, st(qn, c), True, False, t == 1 or OPT["TF"])
+                        act(x, got, AF.Copy)
+                        mm(d, Nb if t == 1 else Nf, x, False, True)
+                    if OPT["E%d" % e][c] == "S":
+                        act(ew(e, c), d, AF.Copy, scale=s)
+                    else:
+                        ts(ew(e, c), d, s, A.mult)
+                    ts(two("ind", e, c), ew(e, c), GRID, A.add, GRID, A.is_equal)
+                z = cols(bank(), a, b)
+                cnt.append(z)
+                mm(z, Ib, cols("bias", a, b), True, False)
+                for l in range(16):
+                    mm(z, ap("Wc", l), ap("ind", e, slice(16 * a + l, 16 * b, 16)), False, l == 15)
+            m = cnt[1]
+            tt(cols("A", a, b), cnt[0], cols(jj, a, b), A.min)
+            tt(m, m, cols(jj, 124 + a, 124 + b), A.min)
+            tt(m, m, cols("A", a, b), A.max)
+            act(cols("cw", a, b), m, AF.Abs, bias=-2048.0)
+            act(cols("lvl", a, b), m, AF.Sign, bias=-2048.0)
+            ts(cols("j%d" % t, a, b), cols("cw", a, b), float(WP), A.min)
 
-    def mutual(t):
+    def mutual(t, shot):
         j, kn = "j%d" % t, "kA" if t <= 2 else "kB"
         for b in range(16):
             o = cols("X", PAD + b, WP, 16)
@@ -315,80 +383,69 @@ def build(g, T, nxt, prv):
                 ts(o, ap("cw"), cols("oh", b, b + 1), A.mult)
             else:
                 act(o, ap("cw"), AF.Copy, scale=cols("oh", b, b + 1))
-        speeds(t)
+        k0 = "kk01" if t == 1 else "kk%d" % t
 
-        def back(a, b):
-            z = cols("C", 256 + a, 256 + b)
+        def partner(c):
+            speeds(t, shot, c)
+            own = ap("kV", t // 3) if c == VC else st("kB" if t <= 2 else "kA", c)
+            if OPT["K0"][c] == "V":
+                tt(ch(k0, c), ind(ap(kn), lst(j, c)), own, A.mult)
+            else:
+                z = bk(bank(), c)
+                act(two("ind", 0, c), ind(ap(kn), lst(j, c)), AF.Copy)
+                mm(z, Ib, own, early=True)
+                tt(ch(k0, c), z, two("ind", 0, c), A.mult)
+
+        for (a, b), then in zip(OPT["BACK"], OPT["THEN"]):
+            for c in [c for c in ORD if a <= MC[c][0] < b]:
+                if OPT["MG"][c] == "S":
+                    act(ch("mg", c), ind(ap("X"), lst(j, c)), AF.Identity, bias=-float(CENTER[c]))
+                else:
+                    ts(ch("mg", c), ind(ap("X"), lst(j, c)), -float(CENTER[c]), A.add)
+            z = cols(bank(), a, b)
             mm(z, If, cols("tgt", a, b), True, False)
             for l in range(16):
                 mm(z, ap("Wc", l), cols("mg", 16 * a + l, 16 * b, 16), False, False)
             mm(z, ap("Ic"), cols("lvl", a, b), False, False)
             mm(z, If, cols("i8b", a, b), False, True)
+            ts(cols("so", a, b), z, 0.0, A.max, float(2 * WP), A.min)
+            if t < 4:
+                act(cols("ab", a, b), z, AF.Abs, bias=-2991.5)
+            for c in then:
+                partner(c)
 
-        for n, (a, b) in enumerate(MC):
-            act(cols("mg", 16 * a, 16 * b), ind(ap("X"), cols(j, a, b)), AF.Identity, bias=-float(CENTER[n]))
-            if n == 2:
-                back(0, b)
-        back(MC[3][0], 124)
-        load_n(t, 1)
-        k0 = "kk01" if t == 1 else "kk%d" % t
-        own = lambda c: ap("k3", t // 3) if c == 3 else st("kB" if t <= 2 else "kA", c)
-        kj = lambda c: tt(ch(k0, c), ind(ap(kn), lst(j, c)), own(c), A.mult)
-        kj(3), kj(0)
-        ts(ap("so"), cols("C", 256, 380), 0.0, A.max, float(2 * WP), A.min)
-        kj(1), kj(2)
-
-    def cursor_s(t):
+    def cursor(t):
         if t == 4:
             return
-        act(ap("ab"), cols("C", 256, 380), AF.Abs, bias=-2991.5)
+        z = bank()
         act(ap("ab"), ap("ab"), AF.Sign, bias=992.25, scale=-1.0)
         for n in range(3 if t == 2 else 1):
-            act(cols("C", 124 * n, 124 * n + 124), ap("ab"), AF.Relu)
-
-    def cursor_v(t):
+            act(cols(z, 124 * n, 124 * n + 124), ap("ab"), AF.Relu)
         if t == 1:
-            tt(cols("C", 0, 124), ap("curB"), cols("C", 0, 124), A.subtract)
-            yield
-            ts(ap("ci"), cols("C", 0, 124), 2.0, A.add)
-            yield
+            tt(cols(z, 0, 124), ap("curB"), cols(z, 0, 124), A.subtract)
+            ts(ap("ci"), cols(z, 0, 124), 2.0, A.add)
             ts(ap("ci"), ap("ci"), 7, A.bitwise_and)
-            yield
             cp(ap("c2"), ap("ci"))
             mask("c2", 0)
-            yield
-            yield
             scan()
             cp(cols("Pi", 0, 124), scl)
             mask("c2", 2)
-            yield
             unpack("JJ2", "of2")
-            yield
-            yield
-            pair(2)
-            yield
-            yield
-            yield
-            extra.extend([lambda: pair(4), lambda: list(tables())])
-        elif t == 2:
-            tt(cols("C", 0, 372), cols("C", 0, 372), ap("TB"), A.mult)
-            yield
-            tt(cols("Pi", 0, 124), cols("C", 0, 124), cols("TA", 0, 124), A.add)
-            tt(ap("UV"), cols("C", 124, 372), cols("TA", 124, 372), A.add)
-            yield
-            unpack("JJ", "of")
-        elif t == 3:
-            tt(cols("C", 0, 124), cols("C", 0, 124), cols("UV", 124, 248), A.mult)
-            yield
-            tt(cols("Pi", 0, 124), cols("C", 0, 124), cols("UV", 0, 124), A.add)
-            yield
-            unpack("JJ", "of")
-
-    def pair(e):
-        scan()
-        act(cols("TA", 62 * e - 124, 62 * e), scl, AF.Copy)
-        if e == 2:
+            scan()
+            act(cols("TA", 0, 124), scl, AF.Copy)
             mask("c2", 4)
+            scan()
+            act(cols("TA", 124, 248), scl, AF.Copy)
+            tables()
+        elif t == 2:
+            tt(cols(z, 0, 372), cols(z, 0, 372), ap("TB"), A.mult)
+            tt(cols("Pi", 0, 124), cols(z, 0, 124), cols("TA", 0, 124), A.add)
+            tt(ap("UV"), cols(z, 124, 372), cols("TA", 124, 372), A.add)
+            unpack("JJ", "of")
+        else:
+            tt(cols(z, 0, 124), cols(z, 0, 124), cols("UV", 124, 248), A.mult)
+            tt(cols("Pi", 0, 124), cols(z, 0, 124), cols("UV", 0, 124), A.add)
+            unpack("JJ", "of")
 
     def tables():
         cp(ap("Pi"), cols("TA", 0, 248))
@@ -399,285 +456,482 @@ def build(g, T, nxt, prv):
         ts(cols("PT", 124, 248), cols("Pi", 0, 124), -2048.0, A.mult, float(2 ** 23 + 4096), A.add)
         tt(cols("TB", 0, 124), cols("PT", 0, 124), cols("TA", 0, 124), A.subtract)
         tt(cols("PT", 124, 248), cols("PT", 124, 248), cols("Ph", 124, 248), A.subtract)
-        yield
         tt(cols("TB", 124, 248), cols("PT", 124, 248), cols("TA", 124, 248), A.subtract)
         tt(cols("TB", 248, 372), cols("TA", 0, 124), cols("PT", 124, 248), A.subtract)
         act(cols("TA", 248, 372), cols("TB", 124, 248), AF.Copy)
-        yield
         tt(cols("TB", 248, 372), cols("TB", 248, 372), cols("TB", 124, 248), A.subtract)
 
-    def recip_start():
-        for c in range(4):
-            act(ch("rk", c), st("kA", c), AF.Copy, scale=-0.0625)
-        extra.extend([lambda n=n: recip(n) for n in range(OPT["RC"])])
-
-    def update(t, shot):
-        again = shot == 1 and t == 1
-        sg, kk = "sg1" if t == 1 else "sg", "kk%d" % t
-        k0 = "kk01" if t == 1 else kk
-        qd = [c for c in range(4) if c not in on_vector(t)]
-        QB = {c: "Q%d" % (n % 2) for n, c in enumerate(on_vector(t))}
-        s = lambda c: None if again else act(ch(sg, c), ind(ap("D"), lst("so", c)), AF.Sign)
-        pr = lambda c: tt(ch("pr", c), bk(NB[c], c), ch(sg, c), A.mult)
-        h = lambda c: act(bk(HB[c], c), ch("pr", c), AF.Relu, scale=cols("nb", 0, 1))
-        k = lambda c: tt(ch(kk, c), bk(HB[c], c), ch(k0, c), A.min)
-        p = lambda c: tt(bk(HB[c], c), bk(NB[c], c), ch(kk, c), A.mult)
-
-        def v(c):
-            tt(st("vs", c), bk(HB[c], c), st("vs", c), A.add)
-            if c in qd or (t == 2 and c == 3):
-                act(st("vs'", c), st("vs", c), AF.Copy)
-            elif t < 4:
-                dma("y", st("vs'", c), st("vs", c))
-
-        def q(c):
-            if c in qd:
-                dma("g", st("q*", c), st("vs*", c), True)
-            elif t < 4:
-                tt(st("q", c), bk(QB[c], c), st("vs", c), A.add)
-                act(st("q'", c), st("q", c), AF.Copy)
-                if t == 2 and c == 3:
-                    send("q%d" % shot, vis("q"), nxt)
-                    send("v%d" % shot, vis("vs"), nxt)
-            else:
-                tt(bk(QB[c], c), bk(QB[c], c), st("vs", c), A.add)
-
-        def aq(c):
-            if t == 4:
-                tt(bk(QB[c], c), bk(QB[c], c), ch("aimA", c), A.subtract)
-                act(st("q", c), bk(QB[c], c), AF.Copy, scale=0.0625)
-                if c not in OPT["SD"]:
-                    act(st("q'", c), bk(QB[c], c), AF.Copy, scale=0.0625)
-                if c == 3:
-                    send("a%d" % shot, vis("q"), prv)
-
-        cur = iter(()) if again else cursor_v(t)
-        nx = lambda: next(cur, None)
-        s(3), pr(3), s(0), h(3), pr(0), s(1), h(0), k(3), pr(1), s(2)
-        if not again:
-            cursor_s(t)
-        p(3), load_n(t, 2), k(0), v(3), h(1), nx(), p(0), nx(), q(3), v(0), nx(), pr(2), h(2), nx(), aq(3), load_q(t, 2), q(0)
-        if (shot, t) == (0, 2):
-            recip_start()
-        if (shot, t) == (0, 3):
-            for c in range(4):
-                mm(bk("C", c), app("Sel", slice(0, 8)), app("aimA", slice(0, 8), slice(*CH[c])))
-                act(ch("aimA", c), bk("C", c), AF.Copy)
-        k(1), aq(0), load_q(t, 3), k(2), nx(), p(1), nx(), p(2), nx(), v(1), nx(), v(2)
-        if t == 2:
-            turn("q%d" % shot, vis2("q"), True, "N1")
-        nx(), q(1), nx(), q(2), nx(), aq(1), aq(2)
-        for _ in cur:
+    def update(t, shot, c):
+        kk, nv = ch("kk%d" % t, c), ch("nv%d" % t, c)
+        z = bk(bank(), c)
+        up = ups(t, shot, c)
+        big = ap("BN" if up else "BP")
+        got = ind(ap("Ew"), lst("so", c))
+        if t == 1 or OPT["PR"][c] == "S":
+            sg = ch("sg1" if t == 1 else "pr", c)
+            if t > 1 or shot == 0:
+                act(sg, got, AF.Sign)
+            mm(z, big, sg, early=True)
+            tt(z, z, nv, A.mult)
+        else:
+            tt(ch("pr", c), got, nv, A.mult)
+            mm(z, big, ch("pr", c))
+        tt(kk, z, ch("kk01", c) if t == 1 else kk, A.min)
+        act(z, kk, AF.Relu)
+        if OPT["VV"][c] == "P":
+            tt(two("D", 0, c), z, nv, A.mult)
+            z = bk(bank(), c)
+            total(z, (If, st("vs", c)), (Nf if up else If, two("D", 0, c)))
+            act(st("vs", c), z, AF.Copy)
+        else:
+            tt(z, z, nv, A.mult)
+        if OPT["VV"][c] == "P":
             pass
-        if t == 2:
-            turn("v%d" % shot, [vis("vs")], True, "N2")
-            dma("y", vis("vs'"), vis("vs"))
-            spare()
-
-    KB = [{3: "N0", 0: "N1", 1: "N2", 2: "Q0"}, {3: "N0", 0: "N1", 1: "H0", 2: "H1"}]
-    YB = {3: "N2", 0: "Q0", 1: "Q1", 2: "C"}
-    late = []
-
-    def loadk(t, cs):
-        for c in cs:
-            act(bk(KB[t % 2][c], c), ch("kk%d" % t, c), AF.Copy, scale=-1.0 if c in OPT["SD"] else 1.0)
-
-    def backward(t, shot):
-        av, nv = "q" if t == 4 else "vs", "nv%d" % t
-        last = shot == 1 and t == 1
-        direct = shot == 0 and t == 4
-        bd = [c for c in OPT["BD"] if t > 1 and not (t == 3 and c == 3)]
-        yo = ("D", WP + PAD) if t % 2 else ("X", PAD)
-        yc = lambda a, b: cols(yo[0], yo[1] + a, yo[1] + b)
-        xb = lambda c: bk(KB[t % 2][c], c)
-        kb = lambda c: bk(KB[(t + (0 if last else 1)) % 2][c], c)
-        yb = lambda c: bk(YB[c], c)
-        x = lambda c: tt(xb(c), xb(c), dd(1, c), A.mult)
-
-        def a(c):
-            if c in bd:
-                tt(st("vs", c), xb(c), st(av, c), A.add)
-                act(st("vs'", c), st("vs", c), AF.Copy)
-            else:
-                tt(kb(c), xb(c), st(av, c), A.add)
-
-        def y(c):
-            o = yb(c) if last else ch("G", c) if direct else yc(*CH[c])
-            tt(o, xb(c), ch(nv, c), A.mult)
-
-        def gain(lo, hi):
-            if direct or last:
-                return
-            if t > 2 or hi < W:
-                dma("g", cols("G", lo, hi), yc(lo, hi), True)
-            else:
-                dma("g", cols("G", lo, V0), yc(lo, V0), True)
-                dma("g", ap("Gh"), yc(V0, W), not (shot == 0 and t == 2))
-
-        def b(c):
-            if c in bd:
-                dma("g", st("vs*", c), st("q*", c), True)
-            elif t > 1:
-                tt(st("vs", c), kb(c), st("q", c), A.add)
-                if t == 3 and c == 3:
-                    send("w%d" % shot, vis("vs"), prv)
-                if c not in OPT["SD"]:
-                    act(st("vs'", c), st("vs", c), AF.Copy)
-                loadk(t - 1, [c])
-            else:
-                ts(kb(c), kb(c), -0.1875, A.max, 0.1875, A.min)
-
-        def e(c):
-            if t == 1:
-                tt(ch("v0f", c), ch("v0f", c), kb(c), A.subtract)
-                if shot:
-                    dma("y", ("yv", (ALL, slice(*CH[c]))), ch("v0f", c))
-                else:
-                    act(st("vs", c), ch("v0f", c), AF.Copy, scale=0.0625)
-                    act(st("vs'", c), ch("v0f", c), AF.Copy, scale=0.0625)
-
-        for c in (3, 0, 1, 2):
-            if c in OPT["SD"]:
-                act(dd(1, c), ind(whole(av), lst("j%d" % t, c)), AF.Copy, scale=-1.0)
-                dma("g", dd(1, c), st(av, c), True)
-            else:
-                tt(dd(1, c), ind(whole(av), lst("j%d" % t, c)), st(av + "'", c), A.subtract)
-        if not last:
-            if t == 1:
-                x(3), x(0), y(3), y(0), a(3), a(0), b(3), b(0), e(3), e(0)
-            elif t == 3:
-                x(3), x(0), y(3), y(0), a(3), a(0), b(3), b(0), loadk(t - 1, [0])
-            else:
-                x(3), x(0), a(3), b(3), a(0), b(0), y(3), loadk(t - 1, [3]), y(0), loadk(t - 1, [0])
-            if late:
-                late.pop()()
-            elif t == 4:
-                spare(2)
-
-            def rest():
-                y(1), y(2), gain(0, W)
-                if (shot, t) == (1, 3):
-                    send("G", cols("G", V0, W), prv)
-
-            x(1), x(2)
-            if (shot, t) == (1, 2):
-                rest()
-            else:
-                late.append(rest)
-            a(1), a(2)
-            if t == 3:
-                turn("a%d" % shot, vis2("q"), False, "Q1")
-            b(1)
-            if t == 3:
-                turn("w%d" % shot, vis2("vs"), False, "C")
-            b(2), e(1), e(2)
-            if t == 3:
-                spare(2)
+        elif up:
+            tt(st("vs", c), st("vs", c), z, A.subtract)
+        else:
+            tt(st("vs", c), z, st("vs", c), A.add)
+        if t == 2 and c == VC:
+            send("v%d" % shot, vis("vs"), nxt)
             return
-        u1 = lambda c: tt(yb(c), yb(c), ch("G", c), A.add)
-
-        def u2(c):
-            if c == 3:
-                tt(yb(c), yb(c), ch("rk", c), A.mult)
+        old = (Ib, st("q0b", c)) if t == 1 else (If, st("q", c))
+        if t == 4:
+            z, aim = bk(bank(), c), (app("Sel", slice(0, 8)), app("aimA", slice(0, 8), slice(*CH[c])))
+            if OPT["AQ"][c] == "P":
+                total(z, old, (If, st("vs", c)), aim)
+                act(st("q", c), z, AF.Copy)
             else:
-                tt(ch("pr", c), yb(c), ch("rk", c), A.mult)
-                add("g", lambda: g.dma_start(T.yg[:, CH[c][0]:CH[c][1]], R(ch("pr", c)), accum_op=A.add), [ch("pr", c), ap("ones")], [], "d")
+                mm(z, *old, early=True)
+                tt(st("q'", c), z, st("vs", c), A.add)
+                z = bk(bank(), c)
+                mm(z, *aim, early=True)
+                tt(st("q", c), z, st("q'", c), A.add)
+            if c == VC:
+                send("a%d" % shot, vis("q"), prv)
+            return
+        if v_twice(c):
+            dma("y", st("vs'", c), st("vs", c))
+        how = OPT["Q"][c]
+        if how in "dD":
+            r = span("Q", c, PAD, VC - (t == 2))
+            if r:
+                for n in ("q", "q'")[:1 + q_twice(c)]:
+                    dma("g", cols(n, *r), cols("vs", *r), True)
+            if t == 1 and r and r[1] == WP:
+                send("q%d" % shot, vis("q"), nxt)
+            return
+        else:
+            z = bk(bank(), c)
+            if how == "P":
+                total(z, old, (If, st("vs", c)))
+                act(st("q", c), z, AF.Copy)
+            else:
+                mm(z, *old, early=True)
+                tt(st("q", c), z, st("vs", c), A.add)
+            if q_twice(c):
+                if OPT["Q2"][c] == "S":
+                    act(st("q'", c), z if how == "P" else st("q", c), AF.Copy)
+                else:
+                    dma("y", st("q'", c), st("q", c))
+        if t == 1 and c == VC:
+            send("q%d" % shot, vis("q"), nxt)
 
-        x(3), x(0), y(3), y(0), a(3), a(0), b(3), b(0), e(3), e(0)
-        x(1), x(2), y(1), y(2), u1(0), u1(1), u2(0), u1(2), u2(1), u2(2)
-        turn("G", cols("G", V0, W), False, "Q0", ap("Gh"))
-        a(1), a(2), u1(3), b(1), b(2), u2(3), e(1), e(2)
-        tt(ch("pr", 3), yb(3), st("kA", 3), A.add)
-        dma("s", ("yg", (ALL, slice(*CH[3]))), ch("pr", 3))
+    def q_start():
+        for c in ORD:
+            if OPT["Q"][c] == "D":
+                for n in ("q", "q'")[:1 + q_twice(c)]:
+                    dma("g", cols(n, *span("Q", c, PAD)), ("q0", (ALL, slice(*span("Q", c)))))
 
-    def q_start(rows):
-        for c in OPT["QD"]:
-            for n in rows:
-                dma("g", st(n, c), ("q0", (ALL, slice(*CH[c]))))
+    def inverse(after):
+        for c in ORD:
+            act(ch("rk", c), st("kA", c), AF.Ln, more=1.3 * (c == ORD[0]), after=after)
+            after = len(ops) - 1
+        for c in ORD:
+            act(ch("rk", c), ch("rk", c), AF.Exp, scale=-1.0, more=1.5 * (c == ORD[0]), after=after)
+            z = bk(bank(), c)
+            mm(z, Ib, st("kA", c), early=True)
+            tt(z, z, ch("rk", c), A.mult)
+            act(z, z, AF.Identity, bias=-2.0)
+            tt(ch("rk", c), z, ch("rk", c), A.mult)
 
+    def squares(after):
+        for c in ORD:
+            o = ap("Gh") if c == VC else ch("nv4", c)
+            act(o, st("kA", c), AF.Square, after=after)
+            act(o, o, AF.Copy, scale=-1.0)
+        dma("g", cols("G", 0, V0), cols("nv4", 0, V0), True)
+
+    AV = {4: ("q", "vs'"), 3: ("vs'", "vs"), 2: ("vs", "vs'"), 1: ("vs'", None)}
+
+    def product(t, shot, c):
+        av, kk, d, up = AV[t][0], ch("kk%d" % t, c), two("D", 0, c), ups(t, shot, c)
+        got = ind(whole(av), lst("j%d" % t, c))
+        x = bk(bank(), c)
+        if OPT["DA"][c] == "P":
+            act(kk, kk, AF.Relu, after=mark[t == 4])
+            mm(x, If if up else Nf, st(av, c), True, False, "fresh")
+            act(d, got, AF.Copy)
+            mm(x, Nf if up else If, d, False, True)
+        elif OPT["DA"][c] == "V":
+            act(st("q'", c), st(av, c), AF.Copy)
+            tt(d, got, st("q'", c), A.subtract)
+        else:
+            act(d, got, AF.Copy, scale=-1.0)
+            if span("DA", c):
+                dma("g", ap("D", 0, slice(*span("DA", c))), cols(av, *span("DA", c, PAD)), True)
+        return x
+
+    def backward(t, shot, c, x):
+        av, new = AV[t]
+        kk, nv = ch("kk%d" % t, c), ch("nv%d" % t, c)
+        last = shot == 1 and t == 1
+        d = two("D", 0, c)
+        ys = lambda a, b: ap("D", 1, slice(a, b)) if t % 2 else cols("X", PAD + a, PAD + b)
+        y = ys(*CH[c])
+        if OPT["DA"][c] == "P":
+            tt(x, x, kk, A.mult)
+        else:
+            act(x, kk, AF.Relu, early=True)
+            tt(x, x, d, A.mult)
+
+        def gains():
+            if last:
+                z = bk(bank(), c)
+                if OPT["U"][c] == "P":
+                    tt(y, x, nv, A.mult)
+                    total(z, (If, ch("G", c)), (If, y))
+                else:
+                    tt(z, x, nv, A.mult)
+                    tt(z, z, ch("G", c), A.add)
+                tt(y, z, ch("rk", c), A.mult)
+                dma("y", ("yg", (ALL, slice(*CH[c]))), y)
+            elif (shot, t) == (0, 4):
+                tt(ch("G", c), x, nv, A.mult)
+            else:
+                tt(y, x, nv, A.mult)
+                apart = t <= 2 or (shot, t) == (1, 3)
+                if c == VC and apart:
+                    dma("g", ap("Gh") if t <= 2 else ch("G", c), y, True)
+                    if t == 3:
+                        send("G", ch("G", c), prv)
+                elif span("GG", c):
+                    r = span("GG", c, 0, VC - apart)
+                    dma("g", cols("G", *r), ys(*r), True)
+
+        def less(o):
+            if ups(t, shot, c):
+                tt(o, st(av, c), x, A.subtract)
+            else:
+                tt(o, x, st(av, c), A.add)
+
+        if t == 3 and c == VC:
+            less(st(new, c))
+            send("w%d" % shot, st(new, c), prv)
+            gains()
+        elif t > 1 and OPT["BB"][c] in "dD":
+            less(st(new, c))
+            r = span("BB", c, PAD, VC - (t == 3))
+            if r:
+                dma("g", cols(new, *r), cols("q", *r), True)
+            gains()
+        else:
+            if OPT["YA"][c] == "I":
+                gains()
+                z = x
+                less(z)
+            else:
+                z = bk(bank(), c)
+                less(z)
+                gains()
+            if t > 1:
+                tt(st(new, c), z, st("q", c), A.add)
+            else:
+                how = OPT["C%d" % shot][c]
+                if how in "dD":
+                    ts(z, z, -3.0, A.max, 3.0, A.min)
+                    act(d, z, AF.Copy, scale=-0.0625)
+                    if how == "D":
+                        r = span("C1", c)
+                        add("g", lambda: g.dma_start(T.yv[:, r[0]:r[1]], R(ap("D", 0, slice(*r))), accum_op=A.add),
+                            [ap("D", 0, slice(*r)), ap("ones")], [], (r[1] - r[0]) * 1024 / 600e3, "d")
+                    return
+                if how == "P":
+                    ts(d, z, -3.0, A.max, 3.0, A.min)
+                    z = bk(bank(), c)
+                    total(z, (If, ch("v0f", c)), (Nf, d))
+                    if not shot:
+                        act(ch("v0f", c), z, AF.Copy)
+                else:
+                    ts(z, z, -3.0, A.max, 3.0, A.min)
+                    tt(ch("v0f", c), ch("v0f", c), z, A.subtract)
+                    z = ch("v0f", c)
+                if shot:
+                    act(ch("v0f", c), z, AF.Copy, scale=0.0625)
+                    dma("s", ("yv", (ALL, slice(*CH[c]))), ch("v0f", c))
+                else:
+                    for n in ("vs", "vs'")[:1 + v_twice(c, "D1")]:
+                        act(st(n, c), z, AF.Copy, scale=2.0 ** -8)
+
+    send("k", ap("kV", 0), nxt)
     for shot in (0, 1):
+        q_start()
         for t in (1, 2, 3, 4):
-            first = shot == 0 and t == 1
             if shot == 1 and t == 1:
-                q_start(["q", "q'"])
-                late.pop()()
-                speeds(1)
-                load_n(1, 1), load_q(1, 0), load_q(1, 1)
+                for c in chunks():
+                    speeds(1, 1, c)
             else:
-                if first:
-                    act(cols("pr", 0, VI), vis("kA"), AF.Copy)
-                    send("k", cols("pr", 0, VI), nxt)
-                    q_start(["q"])
-                    dma("g", ap("v0f"), ("v0", (ALL, ALL)))
-                    for c in (0, 1, 2):
-                        add("g", lambda c=c: g.dma_start(T.yg[:, CH[c][0]:CH[c][1]], T.kap[:, CH[c][0]:CH[c][1]]), [], [cols("ones", 4 * c, 4 * c + 4)], "d")
-                tests(t, shot)
-                mutual(t)
-                if (shot, t) == (0, 2):
-                    spare()
-            update(t, shot)
-            if (shot, t) == (0, 2):
-                turn("k", [vis("kB"), ap("k3", 1, slice(128, 448))], True, "N1")
-        loadk(4, [3, 0, 1, 2])
-        spare()
+                tests(t)
+                mutual(t, shot)
+            mark[1] = len(ops) - 1
+            for c in chunks():
+                update(t, shot, c)
+                if c == OPT["CUR"] and (shot, t) != (1, 1):
+                    cursor(t)
+            mark[0] = len(ops) - 1
+            if (shot, t) == (0, 1):
+                arrive("k")
+                turn(True, ["k"], [vis("kB"), ap("kV", 1)])
+            if t == 2:
+                arrive("q%d" % shot)
+                turn(True, ["q"], [vis("q")])
+                arrive("v%d" % shot)
+                turn(True, ["v"], [vis("vs")], onto=(vis("q"), vis("q")))
+                for n in ["q"] * q_twice(VC) + ["vs"] * v_twice(VC):
+                    dma("y", vis(n + "'"), vis(n))
         for t in (4, 3, 2, 1):
-            if shot == 1 and t == 1:
-                spare(99)
-            backward(t, shot)
+            if (shot, t) == (1, 1):
+                arrive("G")
+                turn(False, ["G"], [ch("G", VC)], ["Gh"])
+            x = {c: product(t, shot, c) for c in chunks()}
+            for c in chunks():
+                backward(t, shot, c, x[c])
+            if (shot, t) == (0, 4):
+                dma("y", ap("mg"), ("v0", (ALL, ALL)))
+                for c in ORD:
+                    act(ch("v0f", c), ch("mg", c), AF.Copy, scale=16.0)
+                squares(mark[0])
+            if (shot, t) == (OPT["INV"], 4):
+                inverse(mark[0])
+            if (shot, t) == (1, 4):
+                for c in [c for c in ORD if OPT["C1"][c] in "dD"]:
+                    act(ch("v0f", c), ch("v0f", c), AF.Copy, scale=0.0625, after=mark[0])
+                    add("y", lambda c=c: g.sync.dma_start(T.yv[:, CH[c][0]:CH[c][1]], R(ch("v0f", c))), [ch("v0f", c)],
+                        [cols("ones", 4 * c, 4 * c + 4)], 0.4, "d")
+            if t == 4:
+                arrive("a%d" % shot)
+                turn(False, ["a"], [vis("q")])
+            if t == 3:
+                arrive("w%d" % shot)
+                turn(False, ["w"], [], onto=(vis("vs"), vis("q")))
     return ops
 
 
-def order(ops):
-    wr, rd, bank = {}, {}, {}
-    flat = {n: np.arange(int(np.prod(s[1][1:]))).reshape(s[1][1:]) for n, s in SCRATCH.items()}
-    for n in SCRATCH:
-        wr[n] = np.full((4, flat[n].size), -1)
-        rd[n] = {}
-        bank[n] = {}
+def region(x):
+    p = range(128)[x[1][0]]
+    return slice(p[0] // 32, p[-1] // 32 + 1), flat(x[0])[x[1][1:]].ravel()
 
-    def region(x):
-        p = range(128)[x[1][0]]
-        return slice(p[0] // 32, p[-1] // 32 + 1), flat[x[0]][x[1][1:]].ravel()
 
+def needs(ops, name, banks):
+    wr, rd, last = {}, {}, {}
     who = lambda m: ops[m]["eng"] if ops[m]["kind"] == "c" else "x%d" % m
+    out = []
     for n, o in enumerate(ops):
-        deps = set()
-        me = who(n)
-        for x in o["rd"]:
-            qd, c = region(x)
-            deps.update(int(m) for m in np.unique(wr[x[0]][qd][:, c]) if m >= 0 and not (me == "t" and who(m) == "t"))
-        for x in o["wr"]:
-            qd, c = region(x)
-            deps.update(int(m) for m in np.unique(wr[x[0]][qd][:, c]) if m >= 0 and not (me == "t" and who(m) == "t"))
-            for e, arr in rd[x[0]].items():
-                if not (me == "t" and e == "t"):
-                    deps.update(int(m) for m in np.unique(arr[qd][:, c]) if m >= 0)
-        for x in o["rd"] + o["wr"]:
-            if SCRATCH[x[0]][0] == "psum":
-                deps.update(m for e, m in bank[x[0]].items() if e != me)
-                bank[x[0]][me] = n
-        for x in o["rd"]:
-            qd, c = region(x)
-            arr = rd[x[0]].setdefault(me, np.full((4, flat[x[0]].size), -1))
-            arr[qd, c] = n
-        for x in o["wr"]:
-            qd, c = region(x)
-            wr[x[0]][qd, c] = n
-        deps.discard(n)
-        o["deps"] = deps
-    known = {e: {} for e in ENG}
+        deps, me = set(), who(n)
+        R = [(name(x), region(x)) for x in o["rd"]]
+        Wr = [(name(x), region(x)) for x in o["wr"]]
+        for k, (qd, c) in R + Wr:
+            if k not in wr:
+                wr[k], rd[k], last[k] = np.full((4, flat(k).size), -1), {}, {}
+            deps.update(np.unique(wr[k][qd][:, c]).tolist())
+        for k, (qd, c) in Wr:
+            for m, arr in list(rd[k].items()):
+                if arr[qd][:, c].any():
+                    deps.add(m)
+                    arr[qd, c] = False
+                    if not arr.any():
+                        del rd[k][m]
+        for k, _ in R + Wr:
+            if psum((k,)):
+                deps.update(m for e, m in last[k].items() if (e != me if banks else e == me == "t"))
+                last[k][me] = n
+        for k, (qd, c) in R:
+            rd[k].setdefault(n, np.zeros((4, flat(k).size), bool))[qd, c] = True
+        for k, (qd, c) in Wr:
+            wr[k][qd, c] = n
+        deps -= {-1, n}
+        out.append(deps)
+    return out
+
+
+def arrange(ops):
+    deps = needs(ops, lambda x: x[0], False)
+    sent = {o["msg"]: n for n, o in enumerate(ops) if o["kind"] == "r"}
     for n, o in enumerate(ops):
-        kn, waits = known[o["eng"]], []
+        if o["kind"] == "a":
+            deps[n] = deps[n] | {sent[o["msg"]]}
+        if "after" in o:
+            deps[n] = deps[n] | {o["after"]}
+    issue = lambda o: o["cost"] if o["kind"] == "c" else 0.0 if o["kind"] == "a" else OPT["GI"] if o["eng"] == "g" else 0.06
+    delay = lambda o: {"c": 0.0, "a": 0.0, "d": OPT["GD"], "r": OPT["RD"]}[o["kind"]]
+    hop = lambda a, b: 0.0 if a["eng"] == b["eng"] == "t" and a["kind"] == "c" else OPT["HOP"]
+    kids = [[] for _ in ops]
+    for n, d in enumerate(deps):
+        for m in d:
+            kids[m].append(n)
+    chain = [0.0] * len(ops)
+    for n in range(len(ops) - 1, -1, -1):
+        o = ops[n]
+        chain[n] = o["cost"] + delay(o) + (issue(o) if o["kind"] != "c" else 0) + max([chain[k] + hop(o, ops[k]) for k in kids[n]], default=0.0)
+    chain = [x + OPT["LEAD"] * o["lead"] for x, o in zip(chain, ops)]
+    names = [sorted(set(x[0] for x in o["rd"] + o["wr"] if psum(x))) for o in ops]
+    left, users = {}, {}
+    for n, ns in enumerate(names):
+        for k in ns:
+            left[k] = left.get(k, 0) + 1
+            users.setdefault(k, []).append(n)
+    for n, o in enumerate(ops):
+        if o.get("early") is True:
+            us = users[names[n][0]]
+            for d in deps[us[us.index(n) + 1]] - {n}:
+                for m in deps[d] - deps[n]:
+                    deps[n].add(m)
+                    kids[m].append(n)
+    best = None
+    if OPT["PRIO"] == "order":
+        chain = [-2.0 * n for n in range(len(ops))]
+    for _ in range(OPT["PASS"]):
+        out, place, end = forwards(ops, deps, kids, names, dict(left), chain, issue, delay, hop)
+        if best is None or max(end) < best[0]:
+            best = (max(end), out, place)
+        chain = [x + OPT["LEAD"] * o["lead"] for x, o in zip(backwards(ops, deps, kids, end, issue, delay, hop), ops)]
+    return best[1:]
+
+
+def backwards(ops, deps, kids, end, issue, delay, hop):
+    clock = {e: 0.0 for e in ENG}
+    can, wait, lead = [0.0] * len(ops), [len(k) for k in kids], [0.0] * len(ops)
+    ready = {e: [] for e in ENG}
+    for n, o in enumerate(ops):
+        if not wait[n]:
+            can[n] = 0.0 if o["kind"] == "c" else o["cost"] + delay(o)
+            ready[o["eng"]].append(n)
+    for _ in ops:
+        now, e = min((max(clock[e], min(can[n] for n in r)), e) for e, r in ready.items() if r)
+        n = max([n for n in ready[e] if can[n] <= now + 0.05], key=lambda n: end[n])
+        ready[e].remove(n)
+        lead[n] = max(can[n], clock[e]) + issue(ops[n])
+        if ops[n]["kind"] != "a":
+            clock[e] = lead[n]
+        for m in deps[n]:
+            o = ops[m]
+            can[m] = max(can[m], lead[n] + hop(o, ops[n]) + (0.0 if o["kind"] == "c" else o["cost"] + delay(o)))
+            wait[m] -= 1
+            if not wait[m]:
+                ready[o["eng"]].append(m)
+    return lead
+
+
+def forwards(ops, deps, kids, names, left, chain, issue, delay, hop):
+    place, free, used = {}, {b: 0.0 for b in BANKS}, {b: {} for b in BANKS}
+    clock = {e: 0.0 for e in ENG}
+    pipe = {"d": 0.0, "r": 0.0}
+    end, wait = [0.0] * len(ops), [len(d) for d in deps]
+    can = [0.0] * len(ops)
+    ready = {e: [] for e in ENG}
+    for n, o in enumerate(ops):
+        if not wait[n]:
+            ready[o["eng"]].append(n)
+    out = []
+
+    def start(n, spare):
+        o, t = ops[n], can[n]
+        new = [k for k in names[n] if k not in place]
+        if new:
+            if len(free) < len(new) + (spare if o.get("early") else 0):
+                return None
+            t = max(t, sorted(free.values())[len(new) - 1] + 0.1)
+        for k in names[n]:
+            if k in place:
+                t = max([t] + [x + 0.1 for e, x in used[place[k]].items() if e != o["eng"]])
+        return t
+
+    while len(out) < len(ops):
+        for spare in (OPT["RES"], 0):
+            cand = {e: [(t, n) for n in ready[e] for t in [start(n, spare)] if t is not None] for e in ENG}
+            when = [(max(clock[e], min(c)[0]), e) for e, c in cand.items() if c]
+            if when:
+                break
+        now, e = min(when)
+        t, n = max([x for x in cand[e] if x[0] <= now + 0.05], key=lambda x: chain[x[1]])
+        soon = [x for x in cand[e] if x[0] < now + OPT["ALPHA"] * issue(ops[n]) and chain[x[1]] > chain[n] + 1.0]
+        if soon:
+            t, n = max(soon, key=lambda x: chain[x[1]])
+        o = ops[n]
+        t = max(t, clock[e])
+        for k in names[n]:
+            if k not in place:
+                place[k] = min(free, key=free.get)
+                del free[place[k]]
         if o["kind"] != "a":
-            for m in sorted(o["deps"], reverse=True):
-                if kn.get(who(m), -1) < m:
-                    waits.append(m)
+            clock[e] = t + issue(o)
+        if o["kind"] in pipe:
+            pipe[o["kind"]] = max(t + issue(o) + delay(o) / 2, pipe[o["kind"]]) + o["cost"]
+            end[n] = pipe[o["kind"]] + delay(o) / 2
+        else:
+            end[n] = t + o["cost"]
+        for k in names[n]:
+            used[place[k]][e] = end[n]
+            left[k] -= 1
+            if not left[k]:
+                free[place[k]] = max(used[place[k]].values())
+        ready[e].remove(n)
+        out.append(n)
+        for k in kids[n]:
+            can[k] = max(can[k], end[n] + hop(o, ops[k]))
+            wait[k] -= 1
+            if not wait[k]:
+                ready[ops[k]["eng"]].append(k)
+    return out, place, end
+
+
+def order(ops, place):
+    deps = needs(ops, lambda x: place.get(x[0], x[0]), True)
+    who = lambda m: ops[m]["eng"] if ops[m]["kind"] == "c" else "x%d" % m
+    known = {e: {} for e in ENG}
+    snap, waits = [], []
+    for n, o in enumerate(ops):
+        kn, w = known[o["eng"]], []
+        if o["kind"] != "a":
+            for m in sorted(deps[n], reverse=True):
+                if kn.get(who(m), -1) < m and not (who(m) == "t" == who(n)):
+                    w.append(m)
                     kn[who(m)] = m
-                    for k2, m2 in ops[m]["snap"].items():
+                    for k2, m2 in snap[m].items():
                         kn[k2] = max(kn.get(k2, -1), m2)
-        o["waits"] = waits
-        o["snap"] = {} if o["kind"] == "a" else dict(kn)
-    return known
+        waits.append(w)
+        snap.append({} if o["kind"] == "a" else dict(kn))
+    waiters = {}
+    for n, w in enumerate(waits):
+        for m in w:
+            waiters.setdefault(m, []).append(n)
+    sems, slot = [], {}
+    for n, o in enumerate(ops):
+        if o["kind"] in "dr":
+            kind = o["kind"] + o["eng"]
+            passed = lambda w: w < n and (ops[w]["eng"] == o["eng"] or (ops[w]["kind"] == "c" and snap[n].get(ops[w]["eng"], -1) >= w)
+                                          or snap[n].get("x%d" % w, -1) >= w)
+            s = [s for s, (k, m, _) in enumerate(sems) if k == kind and o["kind"] == "d" and snap[n].get("x%d" % m, -1) >= m
+                 and all(passed(w) for w in waiters.get(m, []))]
+            if s:
+                sems[s[0]] = (kind, n, sems[s[0]][2] + 1)
+                slot[n] = (s[0], sems[s[0]][2])
+            else:
+                sems.append((kind, n, 1))
+                slot[n] = (len(sems) - 1, 1)
+    return waits, slot, known["g"]
+
+
+PLAN = {}
 
 
 def rank_program(g, core, T, topo):
@@ -686,11 +940,16 @@ def rank_program(g, core, T, topo):
         return
     n = len(T.cores)
     nxt, prv = T.cores[(rank + 1) % n], T.cores[(rank - 1) % n]
-    ops = build(g, T, nxt, prv)
-    known = order(ops)
-    wanted = set(m for o in ops for m in o["waits"])
+    place = {}
+    ops = build(g, T, nxt, prv, place)
+    if not PLAN:
+        seq, where = arrange(ops)
+        PLAN.update(seq=seq, where=where, rest=order([ops[m] for m in seq], where))
+    place.update(PLAN["where"])
+    ops = [ops[m] for m in PLAN["seq"]]
+    waits, slot, known = PLAN["rest"]
+    wanted = set(m for w in waits for m in w)
     count = {e: 0 for e in ENG}
-    nd = 0
     for m, o in enumerate(ops):
         if o["kind"] == "c":
             if m in wanted:
@@ -700,11 +959,10 @@ def rank_program(g, core, T, topo):
             src = prv if o["msg"][0] in "kqv" else nxt
             o["tok"] = ("r_" + o["msg"], len(topo.engines(src, core)))
         else:
-            o["tok"] = ("d%d" % nd, 16 if o["kind"] == "d" else len(topo.engines(core, o["to"])))
-            nd += 1
+            o["tok"] = ("d%d" % slot[m][0], 16 * slot[m][1] if o["kind"] == "d" else len(topo.engines(core, o["to"])))
     qu = {"v": g.vector, "s": g.scalar, "t": g.tensor, "g": g, "y": g.sync}
-    for o in ops:
-        for m in o["waits"]:
+    for o, w in zip(ops, waits):
+        for m in w:
             qu[o["eng"]].wait_ge(T.sem[ops[m]["tok"][0]], ops[m]["tok"][1])
         if o["kind"] == "a":
             continue
@@ -716,7 +974,7 @@ def rank_program(g, core, T, topo):
         if "tok" in o:
             ins.then_inc(T.sem[o["tok"][0]], 16 if o["kind"] == "d" else 1)
     for m, o in enumerate(ops):
-        if o["kind"] != "c" and known["g"].get("x%d" % m, -1) < m:
+        if o["kind"] != "c" and known.get("x%d" % m, -1) < m:
             g.wait_ge(T.sem[o["tok"][0]], o["tok"][1])
     for e in ENG:
         if count[e]:

@@ -10,6 +10,7 @@ ORD = (4, 3, 2, 1, 0)
 CENTER = [8 * (a + b) + 8 for a, b in MC]
 NEAR = 11228502 * 2.0 ** -24
 GRID = 1.5 * 2 ** 23
+BASE = float(2 ** 22 + 2048)
 F, B, I, U = "float32", "bfloat16", "int32", "uint16"
 MSG = ["k", "q0", "v0", "a0", "w0", "q1", "v1", "a1", "w1", "G"]
 
@@ -19,14 +20,14 @@ for _n, _s, _d in (
      ("kk01", [W], F), ("G", [W], F), ("Gh", [VI], F), ("rk", [W], F), ("v0f", [W], F), ("ind", [2, W], B), ("mg", [W], B), ("pr", [W], B),
      ("sg1", [W], B), ("q0b", [WP], B), ("kA", [WP + PAD], B), ("kB", [WP + PAD], B), ("aimA", [W], B), ("Wc", [16, 128], B),
      ("E", [256], F), ("Eb", [256], B), ("ones", [128], F), ("Nf", [128], F), ("Nb", [128], B), ("Ic", [128], B), ("Sel", [128], B),
-     ("BP", [128], B), ("BN", [128], B), ("L", [16, 8], F), ("L1", [16, 8], F), ("L2", [16, 8], F),
+     ("BP", [128], B), ("BN", [128], B), ("L", [16, 8], F), ("L1", [16, 8], F),
      ("iL", [16, 8], I), ("iS", [128], I), ("iO", [16], I), ("iG", [8], I), ("iP", [1], I), ("pcol", [1], F), ("oh", [16], F),
      ("G8", [8], B), ("bias", [124], B), ("i8", [124], F), ("i8b", [124], F), ("tgt", [124], F),
      ("ct", [2, 31, 16], I), ("conf", [31, 32], F),
      ("cu", [2, 4, 16], I), ("cf", [4, 32], F), ("cf2", [4, 32], F), ("curB", [124], F), ("c2", [124], F), ("ci", [124], I),
      ("Pi", [248], I), ("Ph", [248], I), ("JJ", [248], I), ("JJ2", [248], I), ("of", [248], U), ("of2", [248], U), ("A", [124], F),
      ("cw", [124], F), ("lvl", [124], B), ("so", [124], U), ("ab", [124], F),
-     ("PT", [248], F), ("TA", [372], F), ("TB", [372], F), ("UV", [248], F), ("l_k", [VI], B)]
+     ("TA", [372], F), ("TB", [372], F), ("UV", [248], F), ("l_k", [VI], B)]
     + [("kk%d" % t, [W], F) for t in (1, 2, 3, 4)] + [("nv%d" % t, [W], F) for t in (1, 2, 3, 4)]
     + [("j%d" % t, [124], U) for t in (1, 2, 3, 4)] + [("l_" + m, [VI], F) for m in "qvawG"]
 ):
@@ -38,13 +39,14 @@ ENG = ["v", "s", "t", "g", "y"]
 SEMAPHORES = ["e_" + e for e in ENG] + ["d%d" % n for n in range(130)] + ["r_" + m for m in MSG]
 
 ALL = slice(None)
-OPT = {"T0": "VVVPP", "T1": "VVVPP",
+OPT = {"T0": "VVVPD", "T1": "VVVPP",
        "F0": "VVVPP", "F1": "VVVPP",
-       "E0": "SSSSS", "E1": "VSSSS", "INV": 1, "VV": "VVVVV",
-       "DV": "DdPVV", "D1": "PPPVV", "K0": "VVVVV", "MG": "SSSSS", "PR": "SSSVV", "Q": "VVPDd", "Q2": "DDDDD", "AQ": "VVPPP",
-       "DA": "PPPVV", "BB": "VVVVV", "GG": "DdDdd", "YA": "AAAAA", "C0": "PVVVV", "C1": "VVDdd", "U": "PVVVP", "TF": True,
-       "NXV": 8, "MV": 0, "HALF": ((0, 78), (78, 124)), "BACK": ((104, 124), (52, 104), (0, 52)), "RES": 1, "ALPHA": 0.2, "LEAD": 1.0, "STEP": 0.0, "FIRST": 4.0, "PASS": 3, "PRIO": "order", "CUR": 3, "THEN": ((4, 3, 2), (1, 0), ()),
-       "GI": 1.1, "GD": 2.2, "RD": 3.0, "RC": 2.5, "HOP": 0.12}
+       "E0": "SSSSS", "E1": "SSSSS", "INV": (0, 3, 1), "NEW": ((4, 3), (2, 1, 0)), "RL": 0,
+       "DV": "DdPVV", "D1": "PPPVV", "K0": "VVVVV", "MG": "SSSSS", "PR": "SSVVV", "Q": "VVPDD", "Q1": "VVPDd", "Q2": "DDDDD", "AQ": "VVPPP",
+       "SPLIT": 0, "OV": 0.01, "DA": "PPPVV", "A0": "PPPPV", "A1": "PPPPV", "BB": "VVVVD", "GG": "DdDdd", "YA": "AAAAA", "C0": "PVVVV", "C1": "VVDdd", "U": "PPPVP", "TF": True,
+       "SPREAD": (((0, 78), 5), ((78, 124), 7)), "MV": 0, "HALF": ((0, 78), (78, 124)), "BACK": ((104, 124), (52, 104), (0, 52)), "RES": 0, "OWE": 0.8, "SQ": 4, "GV": 0, "SPARE": {"k": 10.0, "q": 5.0, "a": 3.0}, "MAKE": 2, "CASES": ((1.1, 1.0, 0.85, 0.9), (1.25, 1.0, 0.6, 0.7)), "MID": None,
+       "WAIT": [(a, h, gap) for a, h in ((0.3, 0.7), (0.2, 0.5), (0.4, 1.0), (0.25, 1.0), (0.35, 0.5)) for gap in (1.0, 0.6)], "GAP": 1.0, "STEP": 0.0, "FIRST": 4.0, "PASS": 3, "PRIO": "order", "CUR": 2, "THEN": ((4, 3, 2), (1, 0), ()),
+       "GI": 1.1, "GD": 2.2, "RD": 3.0, "RC": 2.5, "HOP": 0.2, "GA": 1.56, "PE": 0.42e-3}
 CY, PE, GA = 0.83e-3, 0.42e-3, 1.56
 
 
@@ -90,7 +92,7 @@ def narrow(*xs):
 def build(g, T, nxt, prv, place):
     A, AF = AluOpType, ActivationFunctionType
     ops = []
-    nb, lead, mark = [0], [0], [0, 0]
+    nb, lead, mark, ends = [0], [0], [0, 0, 0], {}
 
     def bank():
         nb[0] += 1
@@ -111,7 +113,15 @@ def build(g, T, nxt, prv, place):
         return [x for x in out if x[0] in SCRATCH or x[0][0] == "#"]
 
     def add(eng, f, rd, wr, cost, kind="c", **kw):
-        ops.append(dict(eng=eng, f=f, rd=parts(rd), wr=parts(wr), cost=cost, kind=kind, lead=lead[0], **kw))
+        ops.append(dict(eng=eng, f=f, rd=parts(rd), wr=parts(wr), cost=cost, kind=kind, lead=lead[0],
+                        gather=any(isinstance(x, tuple) and x[0] == "@" for x in rd), **kw))
+
+    def gate(first):
+        [o for o in ops[first:] if o["cost"] > 0.3 and o["eng"] in "vs" and len(o["rd"]) > 1][0]["gate"] = True
+
+    def haste(first):
+        for o in ops[first:]:
+            o["haste"] = True
 
     def chunks():
         for n, c in enumerate(ORD):
@@ -121,14 +131,23 @@ def build(g, T, nxt, prv, place):
 
     def price(o, a, b=None):
         if a[0] == "@":
-            return 0.06 + size(a) * GA * CY
+            return 0.06 + size(a) * OPT["GA"] * CY
         r = 0.5 if narrow(o, a) else 1.0
         if b is not None:
             r = 1.0 if psum(a) or psum(b) else 2.0
-        return 0.04 + max(64, size(a) * r) * CY
+        return OPT["OV"] + max(64, size(a) * r) * CY
+
+    def halves(*xs):
+        n = size(xs[0])
+        ok = all(x[0] != "@" and isinstance(x[1][-1], slice) and x[1][-1].start is not None and x[1][-1].step is None
+                 and x[1][-1].stop - x[1][-1].start == n for x in xs)
+        if not OPT["SPLIT"] or n < 300 or not ok:
+            return [xs]
+        cut = lambda x, a, b: (x[0], x[1][:-1] + (slice(x[1][-1].start + a, x[1][-1].start + b),))
+        return [[cut(x, a, b) for x in xs] for a, b in ((0, n // 2), (n // 2, n))]
 
     def tt(o, a, b, op):
-        add("v", lambda: g.vector.tensor_tensor(R(o), R(a), R(b), op), [a, b], [o], price(o, a, b))
+        add("v", lambda: [g.vector.tensor_tensor(R(x), R(y), R(z), op) for x, y, z in halves(o, a, b)][-1], [a, b], [o], price(o, a, b))
 
     def ts(o, a, s1, op0, s2=None, op1=None):
         if op1 is None:
@@ -146,12 +165,20 @@ def build(g, T, nxt, prv, place):
         add("v", lambda: g.vector.transpose(R(o), R(a)), [a], [o], price(o, a))
 
     def act(o, a, func, bias=0.0, scale=1.0, more=0.0, **kw):
-        c = price(o, a) if a[0] == "@" else 0.05 + max(64, size(a)) * CY
-        add("s", lambda: g.scalar.activation(R(o), R(a), func, bias=R(bias), scale=R(scale)), [a, bias, scale], [o], c + more, **kw)
+        c = price(o, a) if a[0] == "@" else OPT["OV"] + max(64, size(a)) * CY
+        add("s", lambda: [g.scalar.activation(R(x), R(y), func, bias=R(bias), scale=R(scale)) for x, y in halves(o, a)][-1], [a, bias, scale], [o], c + more, **kw)
 
     def mm(o, l, r, start=True, stop=True, early=False):
-        c = max(64, size(r)) * PE * (1 if narrow(r) else 4)
+        c = max(64, size(r)) * OPT["PE"] * (1 if narrow(r) else 4)
         add("t", lambda: g.tensor.matmul(R(o), R(l), R(r), start, stop), [l, r], [o], c, early=early or (start and not stop))
+
+    def lanes(o, first, src, last):
+        group([(o, l, r) for l, r in [first] + [(ap("Wc", l), src(l)) for l in range(16)] + last])
+
+    def group(terms):
+        c = sum(max(64, size(r)) * OPT["PE"] * (1 if narrow(r) else 4) for _, _, r in terms)
+        add("t", lambda: [g.tensor.matmul(R(o), R(l), R(r), n == 0, n == len(terms) - 1) for n, (o, l, r) in enumerate(terms)][-1],
+            [x for p in terms for x in p[1:]], [terms[0][0]], c)
 
     def total(o, *terms):
         for n, (l, r) in enumerate(terms):
@@ -174,7 +201,7 @@ def build(g, T, nxt, prv, place):
             add(eng, lambda: qu.dma_start(R(o), R(a)), [a], [o], c, "d")
 
     def send(m, src, to):
-        add("g", None, [src], [], OPT["RC"], "r", msg=m, src=R(src), to=to)
+        add("g", None, [src], [], OPT["RC"], "r", msg=m, src=R(src), to=to, spare=OPT["SPARE"].get(m[0], 0.0))
 
     def arrive(m):
         add("t", None, [], [ap("l_" + m[0])], 0.0, "a", msg=m)
@@ -249,19 +276,20 @@ def build(g, T, nxt, prv, place):
     ts(ap("L"), ap("iL"), 0.0, A.is_equal, 2048.0, A.mult)
     ts(ap("L1", ALL, slice(0, 7)), ap("iL", ALL, slice(0, 7)), 4.0, A.is_equal, -2049.0, A.mult)
     ts(ap("L1", ALL, 7), ap("iL", ALL, 7), -28.0, A.is_equal, -1.0, A.mult)
-    ts(ap("L2", ALL, slice(0, 6)), ap("iL", ALL, slice(0, 6)), 8.0, A.is_equal)
-    ts(ap("L2", ALL, 6), ap("iL", ALL, 6), -24.0, A.is_equal)
     tt(ap("L"), ap("L"), ap("L1"), A.add)
+    ts(ap("L1", ALL, slice(0, 6)), ap("iL", ALL, slice(0, 6)), 8.0, A.is_equal)
+    ts(ap("L1", ALL, 6), ap("iL", ALL, 6), -24.0, A.is_equal)
     ts(ap("iG"), ap("iG"), 4, A.arith_shift_right)
     ts(ap("iS"), ap("iS"), 4, A.arith_shift_right)
-    tt(ap("L", ALL, slice(0, 7)), ap("L", ALL, slice(0, 7)), ap("L2", ALL, slice(0, 7)), A.add)
+    tt(ap("L", ALL, slice(0, 7)), ap("L", ALL, slice(0, 7)), ap("L1", ALL, slice(0, 7)), A.add)
     ts(ap("Sel"), ap("iS"), 128.0, A.is_equal, -1.0, A.mult)
     for c in ORD:
         act(st("vs", c), ch("pr", c), AF.Copy, scale=0.0625)
         if v_twice(c):
             dma("y", st("vs'", c), st("vs", c))
-    for y in (0, 1):
-        ts(ap("conf", ALL, slice(16 * y, 16 * y + 16)), ap("ct", y), 8.0, A.add)
+    for k in (slice(0, 16), slice(16, 31)):
+        for y in (0, 1):
+            ts(ap("conf", k, slice(16 * y, 16 * y + 16)), ap("ct", y, k), 8.0, A.add)
     n0, n1 = bank(), bank()
     mm(cols(n0, 0, 512), ap("L"), ap("conf", slice(0, 16)))
     mm(cols(n1, 0, 480), ap("L"), ap("conf", slice(16, 31)))
@@ -302,7 +330,7 @@ def build(g, T, nxt, prv, place):
         else:
             cp(o, a)
     ts(ap("oh"), ap("iO"), 0.0, A.is_equal)
-    ts(cols("G", 7, 992, 8), cols("G", 7, 992, 8), float(2 ** 22 + 2048), A.add)
+    ts(cols("G", 7, 992, 8), cols("G", 7, 992, 8), BASE, A.add)
     scan()
     cp(cols("Pi", 0, 124), scl)
     for l in range(16):
@@ -364,25 +392,26 @@ def build(g, T, nxt, prv, place):
                     ts(two("ind", e, c), ew(e, c), GRID, A.add, GRID, A.is_equal)
                 z = cols(bank(), a, b)
                 cnt.append(z)
-                mm(z, Ib, cols("bias", a, b), True, False)
-                for l in range(16):
-                    mm(z, ap("Wc", l), ap("ind", e, slice(16 * a + l, 16 * b, 16)), False, l == 15)
+                lanes(z, (Ib, cols("bias", a, b)), lambda l: ap("ind", e, slice(16 * a + l, 16 * b, 16)), [])
             m = cnt[1]
+            first = len(ops)
             tt(cols("A", a, b), cnt[0], cols(jj, a, b), A.min)
             tt(m, m, cols(jj, 124 + a, 124 + b), A.min)
             tt(m, m, cols("A", a, b), A.max)
             act(cols("cw", a, b), m, AF.Abs, bias=-2048.0)
-            act(cols("lvl", a, b), m, AF.Sign, bias=-2048.0)
             ts(cols("j%d" % t, a, b), cols("cw", a, b), float(WP), A.min)
+            haste(first)
+            act(cols("lvl", a, b), m, AF.Sign, bias=-2048.0)
 
     def mutual(t, shot):
         j, kn = "j%d" % t, "kA" if t <= 2 else "kB"
-        for b in range(16):
-            o = cols("X", PAD + b, WP, 16)
-            if b < OPT["NXV"]:
-                ts(o, ap("cw"), cols("oh", b, b + 1), A.mult)
-            else:
-                act(o, ap("cw"), AF.Copy, scale=cols("oh", b, b + 1))
+        for (lo, hi), nxv in OPT["SPREAD"]:
+            for b in range(16):
+                o = cols("X", PAD + 16 * lo + b, PAD + 16 * hi, 16)
+                if b < nxv:
+                    ts(o, cols("cw", lo, hi), cols("oh", b, b + 1), A.mult)
+                else:
+                    act(o, cols("cw", lo, hi), AF.Copy, scale=cols("oh", b, b + 1))
         k0 = "kk01" if t == 1 else "kk%d" % t
 
         def partner(c):
@@ -400,15 +429,15 @@ def build(g, T, nxt, prv, place):
             for c in [c for c in ORD if a <= MC[c][0] < b]:
                 if OPT["MG"][c] == "S":
                     act(ch("mg", c), ind(ap("X"), lst(j, c)), AF.Identity, bias=-float(CENTER[c]))
+                    if c == OPT["MID"]:
+                        gate(len(ops) - 1)
                 else:
                     ts(ch("mg", c), ind(ap("X"), lst(j, c)), -float(CENTER[c]), A.add)
             z = cols(bank(), a, b)
-            mm(z, If, cols("tgt", a, b), True, False)
-            for l in range(16):
-                mm(z, ap("Wc", l), cols("mg", 16 * a + l, 16 * b, 16), False, False)
-            mm(z, ap("Ic"), cols("lvl", a, b), False, False)
-            mm(z, If, cols("i8b", a, b), False, True)
+            lanes(z, (If, cols("tgt", a, b)), lambda l: cols("mg", 16 * a + l, 16 * b, 16),
+                  [(ap("Ic"), cols("lvl", a, b)), (If, cols("i8b", a, b))])
             ts(cols("so", a, b), z, 0.0, A.max, float(2 * WP), A.min)
+            haste(len(ops) - 2)
             if t < 4:
                 act(cols("ab", a, b), z, AF.Abs, bias=-2991.5)
             for c in then:
@@ -448,18 +477,17 @@ def build(g, T, nxt, prv, place):
             unpack("JJ", "of")
 
     def tables():
+        z = bank()
         cp(ap("Pi"), cols("TA", 0, 248))
-        ts(cols("PT", 0, 124), cols("JJ2", 124, 248), -2048.0, A.mult, float(2 ** 23 + 4096), A.add)
+        ts(cols(z, 0, 124), cols("JJ2", 124, 248), -2048.0, A.mult, float(2 ** 23 + 4096), A.add)
         ts(ap("Ph"), ap("Pi"), 11, A.arith_shift_right)
         ts(cols("Pi", 0, 124), cols("Pi", 0, 124), 2047, A.bitwise_and)
-        tt(cols("PT", 0, 124), cols("PT", 0, 124), cols("Ph", 0, 124), A.subtract)
-        ts(cols("PT", 124, 248), cols("Pi", 0, 124), -2048.0, A.mult, float(2 ** 23 + 4096), A.add)
-        tt(cols("TB", 0, 124), cols("PT", 0, 124), cols("TA", 0, 124), A.subtract)
-        tt(cols("PT", 124, 248), cols("PT", 124, 248), cols("Ph", 124, 248), A.subtract)
-        tt(cols("TB", 124, 248), cols("PT", 124, 248), cols("TA", 124, 248), A.subtract)
-        tt(cols("TB", 248, 372), cols("TA", 0, 124), cols("PT", 124, 248), A.subtract)
+        ts(cols(z, 124, 248), cols("Pi", 0, 124), -2048.0, A.mult, float(2 ** 23 + 4096), A.add)
+        tt(cols(z, 0, 248), cols(z, 0, 248), ap("Ph"), A.subtract)
+        tt(cols("TB", 0, 248), cols(z, 0, 248), cols("TA", 0, 248), A.subtract)
+        tt(cols(z, 248, 372), cols("TA", 0, 124), cols(z, 124, 248), A.subtract)
         act(cols("TA", 248, 372), cols("TB", 124, 248), AF.Copy)
-        tt(cols("TB", 248, 372), cols("TB", 248, 372), cols("TB", 124, 248), A.subtract)
+        tt(cols("TB", 248, 372), cols(z, 248, 372), cols("TB", 124, 248), A.subtract)
 
     def update(t, shot, c):
         kk, nv = ch("kk%d" % t, c), ch("nv%d" % t, c)
@@ -478,16 +506,8 @@ def build(g, T, nxt, prv, place):
             mm(z, big, ch("pr", c))
         tt(kk, z, ch("kk01", c) if t == 1 else kk, A.min)
         act(z, kk, AF.Relu)
-        if OPT["VV"][c] == "P":
-            tt(two("D", 0, c), z, nv, A.mult)
-            z = bk(bank(), c)
-            total(z, (If, st("vs", c)), (Nf if up else If, two("D", 0, c)))
-            act(st("vs", c), z, AF.Copy)
-        else:
-            tt(z, z, nv, A.mult)
-        if OPT["VV"][c] == "P":
-            pass
-        elif up:
+        tt(z, z, nv, A.mult)
+        if up:
             tt(st("vs", c), st("vs", c), z, A.subtract)
         else:
             tt(st("vs", c), z, st("vs", c), A.add)
@@ -511,9 +531,10 @@ def build(g, T, nxt, prv, place):
             return
         if v_twice(c):
             dma("y", st("vs'", c), st("vs", c))
-        how = OPT["Q"][c]
+        key = "Q" if t > 1 else "Q1"
+        how = OPT[key][c]
         if how in "dD":
-            r = span("Q", c, PAD, VC - (t == 2))
+            r = span(key, c, PAD, VC - (t == 2))
             if r:
                 for n in ("q", "q'")[:1 + q_twice(c)]:
                     dma("g", cols(n, *r), cols("vs", *r), True)
@@ -538,9 +559,9 @@ def build(g, T, nxt, prv, place):
 
     def q_start():
         for c in ORD:
-            if OPT["Q"][c] == "D":
+            if OPT["Q1"][c] == "D":
                 for n in ("q", "q'")[:1 + q_twice(c)]:
-                    dma("g", cols(n, *span("Q", c, PAD)), ("q0", (ALL, slice(*span("Q", c)))))
+                    dma("g", cols(n, *span("Q1", c, PAD)), ("q0", (ALL, slice(*span("Q1", c)))))
 
     def inverse(after):
         for c in ORD:
@@ -548,8 +569,12 @@ def build(g, T, nxt, prv, place):
             after = len(ops) - 1
         for c in ORD:
             act(ch("rk", c), ch("rk", c), AF.Exp, scale=-1.0, more=1.5 * (c == ORD[0]), after=after)
+
+    def newton(cs, after):
+        for c in cs:
             z = bk(bank(), c)
-            mm(z, Ib, st("kA", c), early=True)
+            mm(z, Ib, st("kA", c))
+            ops[-1]["after"] = after
             tt(z, z, ch("rk", c), A.mult)
             act(z, z, AF.Identity, bias=-2.0)
             tt(ch("rk", c), z, ch("rk", c), A.mult)
@@ -559,7 +584,6 @@ def build(g, T, nxt, prv, place):
             o = ap("Gh") if c == VC else ch("nv4", c)
             act(o, st("kA", c), AF.Square, after=after)
             act(o, o, AF.Copy, scale=-1.0)
-        dma("g", cols("G", 0, V0), cols("nv4", 0, V0), True)
 
     AV = {4: ("q", "vs'"), 3: ("vs'", "vs"), 2: ("vs", "vs'"), 1: ("vs'", None)}
 
@@ -567,18 +591,27 @@ def build(g, T, nxt, prv, place):
         av, kk, d, up = AV[t][0], ch("kk%d" % t, c), two("D", 0, c), ups(t, shot, c)
         got = ind(whole(av), lst("j%d" % t, c))
         x = bk(bank(), c)
-        if OPT["DA"][c] == "P":
-            act(kk, kk, AF.Relu, after=mark[t == 4])
+        key = "DA" if t > 1 else "A%d" % shot
+        if OPT[key][c] == "P":
+            act(kk, kk, AF.Relu, after=ends[t] if OPT["RL"] else mark[t == 4])
             mm(x, If if up else Nf, st(av, c), True, False, "fresh")
             act(d, got, AF.Copy)
             mm(x, Nf if up else If, d, False, True)
-        elif OPT["DA"][c] == "V":
+        elif OPT[key][c] == "S":
+            act(kk, kk, AF.Relu, after=ends[t] if OPT["RL"] else mark[t == 4])
+            act(x, st(av, c), AF.Copy, early="fresh")
+            act(d, got, AF.Copy)
+            if up:
+                tt(x, x, d, A.subtract)
+            else:
+                tt(x, d, x, A.subtract)
+        elif OPT[key][c] == "V":
             act(st("q'", c), st(av, c), AF.Copy)
             tt(d, got, st("q'", c), A.subtract)
         else:
             act(d, got, AF.Copy, scale=-1.0)
-            if span("DA", c):
-                dma("g", ap("D", 0, slice(*span("DA", c))), cols(av, *span("DA", c, PAD)), True)
+            if span(key, c):
+                dma("g", ap("D", 0, slice(*span(key, c))), cols(av, *span(key, c, PAD)), True)
         return x
 
     def backward(t, shot, c, x):
@@ -588,7 +621,7 @@ def build(g, T, nxt, prv, place):
         d = two("D", 0, c)
         ys = lambda a, b: ap("D", 1, slice(a, b)) if t % 2 else cols("X", PAD + a, PAD + b)
         y = ys(*CH[c])
-        if OPT["DA"][c] == "P":
+        if OPT["DA" if t > 1 else "A%d" % shot][c] in "PS":
             tt(x, x, kk, A.mult)
         else:
             act(x, kk, AF.Relu, early=True)
@@ -607,13 +640,19 @@ def build(g, T, nxt, prv, place):
                 dma("y", ("yg", (ALL, slice(*CH[c]))), y)
             elif (shot, t) == (0, 4):
                 tt(ch("G", c), x, nv, A.mult)
+            elif (shot, t, c) == (1, 3, VC) and not OPT["GV"]:
+                tt(y, x, nv, A.mult)
+                dma("g", ch("G", c), y, True)
+                send("G", ch("G", c), prv)
+            elif (shot, t, c) == (1, 3, VC):
+                tt(x, x, nv, A.mult)
+                tt(ch("G", c), x, ch("G", c), A.add)
+                send("G", ch("G", c), prv)
             else:
                 tt(y, x, nv, A.mult)
                 apart = t <= 2 or (shot, t) == (1, 3)
                 if c == VC and apart:
-                    dma("g", ap("Gh") if t <= 2 else ch("G", c), y, True)
-                    if t == 3:
-                        send("G", ch("G", c), prv)
+                    dma("g", ap("Gh"), y, True)
                 elif span("GG", c):
                     r = span("GG", c, 0, VC - apart)
                     dma("g", cols("G", *r), ys(*r), True)
@@ -627,6 +666,12 @@ def build(g, T, nxt, prv, place):
         if t == 3 and c == VC:
             less(st(new, c))
             send("w%d" % shot, st(new, c), prv)
+            gains()
+        elif t > 1 and OPT["BB"][c] == "P":
+            act(d, x, AF.Copy)
+            z = bk(bank(), c)
+            total(z, (If, st(av, c)), (Nf if ups(t, shot, c) else If, d), (If, st("q", c)))
+            act(st(new, c), z, AF.Copy)
             gains()
         elif t > 1 and OPT["BB"][c] in "dD":
             less(st(new, c))
@@ -676,18 +721,24 @@ def build(g, T, nxt, prv, place):
     for shot in (0, 1):
         q_start()
         for t in (1, 2, 3, 4):
+            first = len(ops)
             if shot == 1 and t == 1:
                 for c in chunks():
                     speeds(1, 1, c)
             else:
                 tests(t)
                 mutual(t, shot)
+            gate(first)
             mark[1] = len(ops) - 1
             for c in chunks():
                 update(t, shot, c)
                 if c == OPT["CUR"] and (shot, t) != (1, 1):
                     cursor(t)
+                if c == OPT["INV"][2]:
+                    mark[2] = ends[t] = len(ops) - 1
             mark[0] = len(ops) - 1
+            if (shot, t) == OPT["INV"][:2]:
+                inverse(mark[2])
             if (shot, t) == (0, 1):
                 arrive("k")
                 turn(True, ["k"], [vis("kB"), ap("kV", 1)])
@@ -696,13 +747,17 @@ def build(g, T, nxt, prv, place):
                 turn(True, ["q"], [vis("q")])
                 arrive("v%d" % shot)
                 turn(True, ["v"], [vis("vs")], onto=(vis("q"), vis("q")))
-                for n in ["q"] * q_twice(VC) + ["vs"] * v_twice(VC):
-                    dma("y", vis(n + "'"), vis(n))
+                if q_twice(VC):
+                    act(vis("q'"), vis("q"), AF.Copy)
+                if v_twice(VC):
+                    dma("y", vis("vs'"), vis("vs"))
         for t in (4, 3, 2, 1):
             if (shot, t) == (1, 1):
                 arrive("G")
                 turn(False, ["G"], [ch("G", VC)], ["Gh"])
+            first = len(ops)
             x = {c: product(t, shot, c) for c in chunks()}
+            gate(first)
             for c in chunks():
                 backward(t, shot, c, x[c])
             if (shot, t) == (0, 4):
@@ -710,17 +765,18 @@ def build(g, T, nxt, prv, place):
                 for c in ORD:
                     act(ch("v0f", c), ch("mg", c), AF.Copy, scale=16.0)
                 squares(mark[0])
-            if (shot, t) == (OPT["INV"], 4):
-                inverse(mark[0])
             if (shot, t) == (1, 4):
                 for c in [c for c in ORD if OPT["C1"][c] in "dD"]:
                     act(ch("v0f", c), ch("v0f", c), AF.Copy, scale=0.0625, after=mark[0])
                     add("y", lambda c=c: g.sync.dma_start(T.yv[:, CH[c][0]:CH[c][1]], R(ch("v0f", c))), [ch("v0f", c)],
                         [cols("ones", 4 * c, 4 * c + 4)], 0.4, "d")
+            if (shot, t) == (0, OPT["SQ"]):
+                dma("g", cols("G", 0, V0), cols("nv4", 0, V0), True)
             if t == 4:
                 arrive("a%d" % shot)
                 turn(False, ["a"], [vis("q")])
             if t == 3:
+                newton(OPT["NEW"][shot], max(n for n, o in enumerate(ops) if o["kind"] == "r" and o["msg"][0] == "w"))
                 arrive("w%d" % shot)
                 turn(False, ["w"], [], onto=(vis("vs"), vis("q")))
     return ops
@@ -771,18 +827,13 @@ def arrange(ops):
             deps[n] = deps[n] | {sent[o["msg"]]}
         if "after" in o:
             deps[n] = deps[n] | {o["after"]}
-    issue = lambda o: o["cost"] if o["kind"] == "c" else 0.0 if o["kind"] == "a" else OPT["GI"] if o["eng"] == "g" else 0.06
-    delay = lambda o: {"c": 0.0, "a": 0.0, "d": OPT["GD"], "r": OPT["RD"]}[o["kind"]]
-    hop = lambda a, b: 0.0 if a["eng"] == b["eng"] == "t" and a["kind"] == "c" else OPT["HOP"]
+    issue = lambda o: o["cost"] if o["kind"] == "c" else 0.0 if o["kind"] == "a" else OPT["GI"] * o["slow"] if o["eng"] == "g" else 0.06
+    delay = lambda o: {"c": 0.0, "a": 0.0, "d": OPT["GD"], "r": OPT["RD"]}[o["kind"]] * o["slow"]
+    hop = lambda a, b: (0.0 if a["eng"] == b["eng"] == "t" and a["kind"] == "c" else OPT["HOP"] * a["lag"]) + a.get("spare", 0.0) * (b["kind"] == "a")
     kids = [[] for _ in ops]
     for n, d in enumerate(deps):
         for m in d:
             kids[m].append(n)
-    chain = [0.0] * len(ops)
-    for n in range(len(ops) - 1, -1, -1):
-        o = ops[n]
-        chain[n] = o["cost"] + delay(o) + (issue(o) if o["kind"] != "c" else 0) + max([chain[k] + hop(o, ops[k]) for k in kids[n]], default=0.0)
-    chain = [x + OPT["LEAD"] * o["lead"] for x, o in zip(chain, ops)]
     names = [sorted(set(x[0] for x in o["rd"] + o["wr"] if psum(x))) for o in ops]
     left, users = {}, {}
     for n, ns in enumerate(names):
@@ -796,15 +847,46 @@ def arrange(ops):
                 for m in deps[d] - deps[n]:
                     deps[n].add(m)
                     kids[m].append(n)
-    best = None
-    if OPT["PRIO"] == "order":
-        chain = [-2.0 * n for n in range(len(ops))]
-    for _ in range(OPT["PASS"]):
-        out, place, end = forwards(ops, deps, kids, names, dict(left), chain, issue, delay, hop)
-        if best is None or max(end) < best[0]:
-            best = (max(end), out, place)
-        chain = [x + OPT["LEAD"] * o["lead"] for x, o in zip(backwards(ops, deps, kids, end, issue, delay, hop), ops)]
-    return best[1:]
+    cases = [[dict(o, cost=o["cost"] * (ga if o.get("gather") else pe if o["eng"] == "t" else 1.0 if o["kind"] == "c" else slow), lag=lag, slow=slow)
+              for o in ops] for ga, pe, lag, slow in OPT["CASES"]]
+    rules = []
+    for case in cases[:OPT["MAKE"]]:
+        for patience in OPT["WAIT"]:
+            chain = [-2.0 * n for n in range(len(ops))]
+            for _ in range(OPT["PASS"]):
+                end = forwards(case, deps, kids, names, left, chain, issue, delay, hop, patience)[5]
+                chain = [x + o["lead"] for x, o in zip(backwards(case, deps, kids, end, issue, delay, hop), ops)]
+                rules.append((chain, patience))
+
+    def replay(case, seq, place, was):
+        clock, pipe, used, end = [dict(x) for x in was]
+        for n in seq:
+            o = case[n]
+            e = o["eng"]
+            t = max([clock.get(e, 0.0)] + [end[m] + hop(case[m], o) for m in deps[n]]
+                    + [x + OPT["HOP"] * o["lag"] for k in names[n] for (b, f), x in used.items() if b == place[k] and f != e])
+            if o["kind"] != "a":
+                clock[e] = t + issue(o)
+            if o["kind"] in "dr":
+                pipe[o["kind"]] = max(t + issue(o) + delay(o) / 2, pipe.get(o["kind"], 0.0)) + o["cost"]
+            end[n] = pipe[o["kind"]] + delay(o) / 2 if o["kind"] in "dr" else t + o["cost"]
+            for k in names[n]:
+                used[place[k], e] = end[n]
+        return clock, pipe, used, end
+
+    state, was = None, [({}, {}, {}, {}) for _ in cases]
+    for gate in [n for n, o in enumerate(ops) if "gate" in o] + [None]:
+        best = None
+        for chain, patience in rules:
+            s = forwards(cases[0], deps, kids, names, left, chain, issue, delay, hop, patience, state, gate)
+            now = [replay(case, s[9][len(state[9]) if state else 0:], s[0], w) for case, w in zip(cases, was)]
+            owed = [] if gate is None else [n for n in set(range(gate)) - set(s[9]) if ops[n]["eng"] == "v"]
+            late = sum(max(x[3].values() if gate is None else [x[3][m] for m in deps[gate]]) + OPT["OWE"] * sum(case[n]["cost"] for n in owed)
+                       for case, x in zip(cases, now))
+            if best is None or late < best[0]:
+                best = (late, s, now)
+        state, was = best[1:]
+    return state[9], state[0]
 
 
 def backwards(ops, deps, kids, end, issue, delay, hop):
@@ -831,17 +913,14 @@ def backwards(ops, deps, kids, end, issue, delay, hop):
     return lead
 
 
-def forwards(ops, deps, kids, names, left, chain, issue, delay, hop):
-    place, free, used = {}, {b: 0.0 for b in BANKS}, {b: {} for b in BANKS}
-    clock = {e: 0.0 for e in ENG}
-    pipe = {"d": 0.0, "r": 0.0}
-    end, wait = [0.0] * len(ops), [len(d) for d in deps]
-    can = [0.0] * len(ops)
-    ready = {e: [] for e in ENG}
-    for n, o in enumerate(ops):
-        if not wait[n]:
-            ready[o["eng"]].append(n)
-    out = []
+def forwards(ops, deps, kids, names, left, chain, issue, delay, hop, patience, state=None, until=None):
+    if state is None:
+        state = ({}, {b: 0.0 for b in BANKS}, {b: {} for b in BANKS}, {e: 0.0 for e in ENG}, {"d": 0.0, "r": 0.0}, [0.0] * len(ops),
+                 [len(d) for d in deps], [0.0] * len(ops), {e: [n for n, o in enumerate(ops) if o["eng"] == e and not deps[n]] for e in ENG}, [], left)
+    place, free, used, clock, pipe, end, wait, can, ready, out, left = state
+    place, free, clock, pipe, left = dict(place), dict(free), dict(clock), dict(pipe), dict(left)
+    used, ready = {b: dict(x) for b, x in used.items()}, {e: list(x) for e, x in ready.items()}
+    end, wait, can, out = list(end), list(wait), list(can), list(out)
 
     def start(n, spare):
         o, t = ops[n], can[n]
@@ -849,13 +928,13 @@ def forwards(ops, deps, kids, names, left, chain, issue, delay, hop):
         if new:
             if len(free) < len(new) + (spare if o.get("early") else 0):
                 return None
-            t = max(t, sorted(free.values())[len(new) - 1] + 0.1)
+            t = max(t, sorted(free.values())[len(new) - 1] + OPT["HOP"] * o["lag"])
         for k in names[n]:
             if k in place:
-                t = max([t] + [x + 0.1 for e, x in used[place[k]].items() if e != o["eng"]])
+                t = max([t] + [x + OPT["HOP"] * o["lag"] for e, x in used[place[k]].items() if e != o["eng"]])
         return t
 
-    while len(out) < len(ops):
+    while len(out) < len(ops) and (until is None or wait[until]):
         for spare in (OPT["RES"], 0):
             cand = {e: [(t, n) for n in ready[e] for t in [start(n, spare)] if t is not None] for e in ENG}
             when = [(max(clock[e], min(c)[0]), e) for e, c in cand.items() if c]
@@ -863,7 +942,8 @@ def forwards(ops, deps, kids, names, left, chain, issue, delay, hop):
                 break
         now, e = min(when)
         t, n = max([x for x in cand[e] if x[0] <= now + 0.05], key=lambda x: chain[x[1]])
-        soon = [x for x in cand[e] if x[0] < now + OPT["ALPHA"] * issue(ops[n]) and chain[x[1]] > chain[n] + 1.0]
+        soon = [x for x in cand[e] if x[0] < now + patience["haste" in ops[x[1]]] * issue(ops[n])
+                and chain[x[1]] > chain[n] + patience[2]]
         if soon:
             t, n = max(soon, key=lambda x: chain[x[1]])
         o = ops[n]
@@ -891,7 +971,7 @@ def forwards(ops, deps, kids, names, left, chain, issue, delay, hop):
             wait[k] -= 1
             if not wait[k]:
                 ready[ops[k]["eng"]].append(k)
-    return out, place, end
+    return place, free, used, clock, pipe, end, wait, can, ready, out, left
 
 
 def order(ops, place):

@@ -3,7 +3,7 @@ from concourse.mybir import AluOpType, ActivationFunctionType
 
 W, V0, VI, PAD = 1984, 1664, 320, 8
 WP = W + PAD
-MC = [(0, 26), (26, 52), (52, 78), (78, 104), (104, 124)]
+MC = [(0, 20), (20, 48), (48, 76), (76, 104), (104, 124)]
 CH = [(16 * a, 16 * b) for a, b in MC]
 VC = 4
 ORD = (4, 3, 2, 1, 0)
@@ -16,17 +16,17 @@ MSG = ["k", "q0", "v0", "a0", "w0", "q1", "v1", "a1", "w1", "G"]
 
 SCRATCH = {}
 for _n, _s, _d in (
-    [("q", [2, WP + PAD], F), ("vs", [2, WP + PAD], F), ("kV", [2, VI], B), ("D", [2, W], F), ("Ew", [2 * WP + PAD], B), ("X", [WP + PAD], F),
+    [("q", [2, WP + PAD], F), ("vs", [2, WP + PAD], F), ("kV", [1, VI], B), ("D", [2, W], F), ("Ew", [2 * WP + PAD], B), ("X", [WP + PAD], F),
      ("kk01", [W], F), ("G", [W], F), ("Gh", [VI], F), ("rk", [W], F), ("v0f", [W], F), ("ind", [2, W], B), ("mg", [W], B), ("pr", [W], B),
      ("sg1", [W], B), ("q0b", [WP], B), ("kA", [WP + PAD], B), ("kB", [WP + PAD], B), ("aimA", [W], B), ("Wc", [16, 128], B),
-     ("E", [256], F), ("Eb", [256], B), ("ones", [128], F), ("Nf", [128], F), ("Nb", [128], B), ("Ic", [128], B), ("Sel", [128], B),
+     ("E", [256], F), ("Eb", [256], B), ("ones", [128], F), ("Nf", [128], F), ("N2", [128], F), ("Nb", [128], B), ("Ic", [128], B), ("Sel", [128], B),
      ("BP", [128], B), ("BN", [128], B), ("L", [16, 8], F), ("L1", [16, 8], F),
      ("iL", [16, 8], I), ("iS", [128], I), ("iO", [16], I), ("iG", [8], I), ("iP", [1], I), ("pcol", [1], F), ("oh", [16], F),
      ("G8", [8], B), ("bias", [124], B), ("i8", [124], F), ("i8b", [124], F), ("tgt", [124], F),
      ("ct", [2, 31, 16], I), ("conf", [31, 32], F),
      ("cu", [2, 4, 16], I), ("cf", [4, 32], F), ("cf2", [4, 32], F), ("curB", [124], F), ("c2", [124], F), ("ci", [124], I),
      ("Pi", [248], I), ("Ph", [248], I), ("JJ", [248], I), ("JJ2", [248], I), ("of", [248], U), ("of2", [248], U), ("A", [124], F),
-     ("cw", [124], F), ("lvl", [124], B), ("so", [124], U), ("ab", [124], F),
+     ("cw", [124], F), ("lvl", [124], B), ("so", [124], U), ("sk", [124], U), ("ab", [124], F), ("mu", [124], B),
      ("TA", [372], F), ("TB", [372], F), ("UV", [248], F), ("l_k", [VI], B)]
     + [("kk%d" % t, [W], F) for t in (1, 2, 3, 4)] + [("nv%d" % t, [W], F) for t in (1, 2, 3, 4)]
     + [("j%d" % t, [124], U) for t in (1, 2, 3, 4)] + [("l_" + m, [VI], F) for m in "qvawG"]
@@ -39,15 +39,19 @@ ENG = ["v", "s", "t", "g", "y"]
 SEMAPHORES = ["e_" + e for e in ENG] + ["d%d" % n for n in range(130)] + ["r_" + m for m in MSG]
 
 ALL = slice(None)
-OPT = {"T0": "VVVPD", "T1": "VVVPP",
-       "F0": "VVVPP", "F1": "VVVPP",
-       "E0": "SSSSS", "E1": "SSSSS", "INV": (0, 3, 1), "NEW": ((4, 3), (2, 1, 0)), "RL": 0,
-       "DV": "DdPVV", "D1": "PPPVV", "K0": "VVVVV", "MG": "SSSSS", "PR": "SSVVV", "Q": "VVPDD", "Q1": "VVPDd", "Q2": "DDDDD", "AQ": "VVPPP",
-       "SPLIT": 0, "OV": 0.01, "DA": "PPPVV", "A0": "PPPPV", "A1": "PPPPV", "BB": "VVVVD", "GG": "DdDdd", "YA": "AAAAA", "C0": "PVVVV", "C1": "VVDdd", "U": "PPPVP", "TF": True,
-       "SPREAD": (((0, 78), 5), ((78, 124), 7)), "MV": 0, "HALF": ((0, 78), (78, 124)), "BACK": ((104, 124), (52, 104), (0, 52)), "RES": 0, "OWE": 0.8, "SQ": 4, "GV": 0, "SPARE": {"k": 10.0, "q": 5.0, "a": 3.0}, "MAKE": 2, "CASES": ((1.1, 1.0, 0.85, 0.9), (1.25, 1.0, 0.6, 0.7)), "MID": None,
-       "WAIT": [(a, h, gap) for a, h in ((0.3, 0.7), (0.2, 0.5), (0.4, 1.0), (0.25, 1.0), (0.35, 0.5)) for gap in (1.0, 0.6)], "GAP": 1.0, "STEP": 0.0, "FIRST": 4.0, "PASS": 3, "PRIO": "order", "CUR": 2, "THEN": ((4, 3, 2), (1, 0), ()),
-       "GI": 1.1, "GD": 2.2, "RD": 3.0, "RC": 2.5, "HOP": 0.2, "GA": 1.56, "PE": 0.42e-3}
-CY, PE, GA = 0.83e-3, 0.42e-3, 1.56
+OPT = {"T0": "VVvPV", "T1": "VvvDP", "F0": "VvvPP", "F1": "VVvPP", "E0": "SSSVS", "E1": "SSSSS", "MG": "SSSSS",
+       "DV": "DDVVV", "D1": "PVPVV", "PR": "VVVVV", "G1": "SSSsS", "NS": "SVSVV", "KM": "SSSSS", "KK": "SVVVS", "K1": "VVvVV",
+       "PL": "SSSSS", "P1": "SSIIK", "VU": "OOOOV", "V1": "VOVVO", "V4": "VVVVV", "Q": "VVVDd", "Q1": "VPPVV", "Q2": "SSSDD", "AQ": "OVOOO",
+       "DA4": "OPPVV", "DA3": "OOVPV", "DA2": "OVOPV", "A0": "PVPOV", "A1": "PPVOV", "KL": "TSSSS", "KM0": "TSSTS", "KM1": "STSSS",
+       "BB4": "VQVDO", "BB3": "VVVDd", "BB2": "VOVOV", "L0": "VQQVV", "L1": "VQVVV", "YA": "AIIII", "Y0": "AAIAA", "Y1": "IAIAA",
+       "GG": "DdDdd", "C0": "VOVVV", "C1": "VVDDD", "U": "VVPOO", "NW": "VOOOO",
+       "HALF": ((0, 76), (76, 124)), "SPREAD": (((0, 76), 8), ((76, 124), 8)), "BACK": ((104, 124), (48, 104), (0, 48)), "THEN": ((4, 3, 2), (1, 0), ()),
+       "INV": (0, 3, 1), "NEW": ((4, 3), (2, 1, 0)), "SQ": 4, "CUR": 2,
+       "GI": 1.1, "GD": 2.2, "RD": 3.0, "RC": 2.5, "HOP": 0.2, "OV": 0.01, "GA": 1.56, "PE": 0.42e-3,
+       "CASES": ((1.0, 1.1, 1.3, 0.85), (1.25, 1.0, 1.0, 0.5), (0.8, 1.0, 1.8, 0.65), (1.0, 1.3, 0.9, 0.55), (1.0, 1.0, 1.3, 1.4)),
+       "WEIGHT": (0.2, 0.25, 0.15, 0.15, 0.25), "WORST": 0.5, "WAIT": ((0.3, 0.7, 1.0), (0.3, 0.7, 0.6)), "SPARE": {"k": 10.0, "q": 5.0, "a": 3.0},
+       "FIRST": 4.0, "PASS": 3, "OWE": 0.8, "AHEAD": 1, "TRIES": 750, "SHAKE": 1.5, "SEED": 2}
+CY = 0.83e-3
 
 
 def ap(name, *idx):
@@ -92,7 +96,7 @@ def narrow(*xs):
 def build(g, T, nxt, prv, place):
     A, AF = AluOpType, ActivationFunctionType
     ops = []
-    nb, lead, mark, ends = [0], [0], [0, 0, 0], {}
+    nb, lead, mark, held, step, at = [0], [0], [0, 0], {}, [0], [None]
 
     def bank():
         nb[0] += 1
@@ -113,6 +117,8 @@ def build(g, T, nxt, prv, place):
         return [x for x in out if x[0] in SCRATCH or x[0][0] == "#"]
 
     def add(eng, f, rd, wr, cost, kind="c", **kw):
+        x = (parts(wr) + parts(rd))[0]
+        kw["tag"] = (step[0], eng + kind + ("#" if psum(x) else x[0]) + "".join("#" if psum(y) else y[0] for y in parts(rd)), at[0])
         ops.append(dict(eng=eng, f=f, rd=parts(rd), wr=parts(wr), cost=cost, kind=kind, lead=lead[0],
                         gather=any(isinstance(x, tuple) and x[0] == "@" for x in rd), **kw))
 
@@ -124,10 +130,10 @@ def build(g, T, nxt, prv, place):
             o["haste"] = True
 
     def chunks():
-        for n, c in enumerate(ORD):
-            lead[0] = OPT["STEP"] * (len(ORD) - 1 - n)
+        for c in ORD:
+            lead[0], at[0] = 0, c
             yield c
-        lead[0] = 0
+        at[0] = None
 
     def price(o, a, b=None):
         if a[0] == "@":
@@ -137,17 +143,8 @@ def build(g, T, nxt, prv, place):
             r = 1.0 if psum(a) or psum(b) else 2.0
         return OPT["OV"] + max(64, size(a) * r) * CY
 
-    def halves(*xs):
-        n = size(xs[0])
-        ok = all(x[0] != "@" and isinstance(x[1][-1], slice) and x[1][-1].start is not None and x[1][-1].step is None
-                 and x[1][-1].stop - x[1][-1].start == n for x in xs)
-        if not OPT["SPLIT"] or n < 300 or not ok:
-            return [xs]
-        cut = lambda x, a, b: (x[0], x[1][:-1] + (slice(x[1][-1].start + a, x[1][-1].start + b),))
-        return [[cut(x, a, b) for x in xs] for a, b in ((0, n // 2), (n // 2, n))]
-
     def tt(o, a, b, op):
-        add("v", lambda: [g.vector.tensor_tensor(R(x), R(y), R(z), op) for x, y, z in halves(o, a, b)][-1], [a, b], [o], price(o, a, b))
+        add("v", lambda: g.vector.tensor_tensor(R(o), R(a), R(b), op), [a, b], [o], price(o, a, b))
 
     def ts(o, a, s1, op0, s2=None, op1=None):
         if op1 is None:
@@ -166,7 +163,7 @@ def build(g, T, nxt, prv, place):
 
     def act(o, a, func, bias=0.0, scale=1.0, more=0.0, **kw):
         c = price(o, a) if a[0] == "@" else OPT["OV"] + max(64, size(a)) * CY
-        add("s", lambda: [g.scalar.activation(R(x), R(y), func, bias=R(bias), scale=R(scale)) for x, y in halves(o, a)][-1], [a, bias, scale], [o], c + more, **kw)
+        add("s", lambda: g.scalar.activation(R(o), R(a), func, bias=R(bias), scale=R(scale)), [a, bias, scale], [o], c + more, **kw)
 
     def mm(o, l, r, start=True, stop=True, early=False):
         c = max(64, size(r)) * OPT["PE"] * (1 if narrow(r) else 4)
@@ -200,6 +197,12 @@ def build(g, T, nxt, prv, place):
         else:
             add(eng, lambda: qu.dma_start(R(o), R(a)), [a], [o], c, "d")
 
+    def again(how, o, a):
+        if how == "S":
+            act(o, a, AF.Copy)
+        else:
+            dma("y", o, a)
+
     def send(m, src, to):
         add("g", None, [src], [], OPT["RC"], "r", msg=m, src=R(src), to=to, spare=OPT["SPARE"].get(m[0], 0.0))
 
@@ -221,18 +224,34 @@ def build(g, T, nxt, prv, place):
     vis = lambda n: cols(n, PAD + V0, WP)
     whole = lambda n: cols(n, 0, WP + PAD)
     DT = cols("G", 0, 992)
-    st = lambda n, c: cols(n, PAD + CH[c][0], PAD + CH[c][1])
-    ch = lambda n, c: cols(n, CH[c][0], CH[c][1])
+    mc = lambda c: (MC[c[0]][0], MC[c[1]][1]) if isinstance(c, tuple) else MC[c]
+    st = lambda n, c: cols(n, PAD + 16 * mc(c)[0], PAD + 16 * mc(c)[1])
+    ch = lambda n, c: cols(n, 16 * mc(c)[0], 16 * mc(c)[1])
     bk = lambda n, c: cols(n, 0, CH[c][1] - CH[c][0])
-    lst = lambda n, c, o=0: cols(n, o + MC[c][0], o + MC[c][1])
-    two = lambda n, e, c: ap(n, e, slice(*CH[c]))
+    lst = lambda n, c, o=0: cols(n, o + mc(c)[0], o + mc(c)[1])
+    two = lambda n, e, c: ap(n, e, slice(16 * mc(c)[0], 16 * mc(c)[1]))
+
+    def run(key, c):
+        h = c
+        while h < VC and OPT[key][h + 1].islower():
+            h += 1
+        return c, h
+
     EOFF = (WP + PAD, PAD)
     ew = lambda e, c: cols("Ew", EOFF[e] + CH[c][0], EOFF[e] + CH[c][1])
     msk, sc, scl = cols("rk", 0, 992), cols("rk", 992, W), cols("rk", 999, W, 8)
-    q_twice = lambda c: "V" in (OPT["T0"][c], OPT["T1"][c])
+    q_twice = lambda c: "V" in (OPT["T0"][c] + OPT["T1"][c]).upper()
     dv = lambda t, shot: "D1" if (shot, t) == (1, 1) else "DV"
-    v_twice = lambda c, key="DV": OPT[key][c] == "V"
-    ups = lambda t, shot, c: OPT[dv(t, shot)][c] != "V"
+    v_twice = lambda c, key="DV": OPT[key][c] in "vV"
+    load = lambda t, c: OPT["PL" if t > 1 else "P1"][c]
+    keeps = lambda t, shot, c: OPT[dv(t, shot)][c] == "P" and load(t, c) == "K"
+    ups = lambda t, shot, c: OPT[dv(t, shot)][c] not in "vV" and not keeps(t, shot, c)
+    signed = lambda s: If if s > 0 else Nf
+
+    def opened(c):
+        z = bk(bank(), c)
+        mm(z, Ib, st("kA", c), True, False)
+        return z
 
     def span(key, c, off=0, top=VC):
         if OPT[key][c] == "d":
@@ -241,6 +260,10 @@ def build(g, T, nxt, prv, place):
         while h < top and OPT[key][h + 1] == "d":
             h += 1
         return off + CH[c][0], off + CH[h][1]
+
+    def both(r):
+        cs = [c for c in range(VC + 1) if r[0] <= PAD + CH[c][0] < r[1] and q_twice(c)]
+        return [("q",) + r] + ([("q'", PAD + CH[cs[0]][0], PAD + CH[cs[-1]][1])] if cs else [])
 
     fill(ap("cu"), 0)
     fill(ap("ones"), 1.0)
@@ -303,10 +326,7 @@ def build(g, T, nxt, prv, place):
 
     def mask(src, e):
         for m in range(8):
-            if m < OPT["MV"]:
-                ts(cols("rk", m, 992, 8), ap(src), float((m - e) & 7), A.not_equal, float(2 ** 24), A.mult)
-            else:
-                act(cols("rk", m, 992, 8), ap(src), AF.Abs, bias=-float(2 ** 24) * ((m - e) & 7), scale=float(2 ** 24))
+            act(cols("rk", m, 992, 8), ap(src), AF.Abs, bias=-float(2 ** 24) * ((m - e) & 7), scale=float(2 ** 24))
 
     def scan():
         add("v", lambda: g.vector.tensor_tensor_scan(R(sc), R(msk), R(DT), 8.0e6, A.min, A.add), [msk, DT], [sc], 0.04 + 992 * CY)
@@ -338,6 +358,7 @@ def build(g, T, nxt, prv, place):
     act(ap("Eb"), ap("E"), AF.Copy)
     act(Nf, If, AF.Copy, scale=-1.0)
     act(Nb, If, AF.Copy, scale=-1.0)
+    act(ap("N2"), If, AF.Copy, scale=2.0)
     act(ap("BP"), If, AF.Copy, scale=float(2 ** 63))
     act(ap("BN"), ap("BP"), AF.Copy, scale=-float(2 ** 63))
     act(ap("BP"), ap("BP"), AF.Copy, scale=float(2 ** 63))
@@ -350,17 +371,20 @@ def build(g, T, nxt, prv, place):
     def speeds(t, shot, c):
         nv, key = ch("nv%d" % t, c), dv(t, shot)
         if OPT[key][c] == "P":
-            z = bk(bank(), c)
-            mm(z, If, st("vs", c), True, False)
+            z, s = bk(bank(), c), 1 if ups(t, shot, c) else -1
+            mm(z, signed(s), st("vs", c), True, False)
             act(nv, ind(whole("vs"), lst("j%d" % t, c)), AF.Copy)
-            mm(z, Nf, nv, False, True)
+            mm(z, signed(-s), nv, False, True)
             act(nv, z, AF.Copy)
-        elif OPT[key][c] != "V":
-            act(nv, ind(whole("vs"), lst("j%d" % t, c)), AF.Copy, scale=-1.0)
-            if span(key, c):
-                dma("g", cols("nv%d" % t, *span(key, c)), cols("vs", *span(key, c, PAD)), True)
-        else:
-            tt(nv, ind(whole("vs"), lst("j%d" % t, c)), st("vs'", c), A.subtract)
+            if keeps(t, shot, c):
+                held[t, c] = z
+        elif OPT[key][c] == "D":
+            c = run(key, c)
+            act(ch("nv%d" % t, c), ind(whole("vs"), lst("j%d" % t, c)), AF.Copy, scale=-1.0)
+            dma("g", ch("nv%d" % t, c), st("vs", c), True)
+        elif OPT[key][c] == "V":
+            c = run(key, c)
+            tt(ch("nv%d" % t, c), ind(whole("vs"), lst("j%d" % t, c)), st("vs'", c), A.subtract)
 
     def tests(t):
         qn = "q0b" if t == 1 else "q"
@@ -368,23 +392,25 @@ def build(g, T, nxt, prv, place):
         win = cols(qn, 0, WP)
         for a, b in OPT["HALF"]:
             cnt = []
-            lead[0] = OPT["FIRST"] * ((a, b) == OPT["HALF"][0])
+            lead[0], at[0] = OPT["FIRST"] * ((a, b) == OPT["HALF"][0]), (a, b)
             for e in (0, 1):
+                key, made = "FT"[t > 1] + str(e), []
                 for c in [c for c in ORD if a <= MC[c][0] < b]:
-                    how, got = OPT["FT"[t > 1] + str(e)][c], ind(win, lst(of, c, 124 * e))
-                    d, s = two("D", e, c), NEAR
+                    how, r = OPT[key][c], run(key, c)
+                    got, d, s = ind(win, lst(of, r, 124 * e)), two("D", e, c), -NEAR if how in "vV" else NEAR
                     if how == "V":
-                        tt(d, got, ch("sg1", c) if t == 1 else st("q'", c), A.subtract)
-                        s = -NEAR
+                        tt(two("D", e, r), got, ch("sg1", r) if t == 1 else st("q'", r), A.subtract)
                     elif how == "D":
-                        act(d, got, AF.Copy, scale=-1.0)
-                        dma("g", d, st("q", c), True)
-                    else:
+                        act(two("D", e, r), got, AF.Copy, scale=-1.0)
+                        dma("g", two("D", e, r), st("q", r), True)
+                    elif how == "P":
                         x = two("ind", e, c) if t == 1 else d
                         d = bk(bank(), c)
-                        mm(d, Ib if t == 1 else If, st(qn, c), True, False, t == 1 or OPT["TF"])
+                        mm(d, Ib if t == 1 else If, st(qn, c), True, False)
                         act(x, got, AF.Copy)
                         mm(d, Nb if t == 1 else Nf, x, False, True)
+                    made.append((c, d, s))
+                for c, d, s in made:
                     if OPT["E%d" % e][c] == "S":
                         act(ew(e, c), d, AF.Copy, scale=s)
                     else:
@@ -402,54 +428,94 @@ def build(g, T, nxt, prv, place):
             ts(cols("j%d" % t, a, b), cols("cw", a, b), float(WP), A.min)
             haste(first)
             act(cols("lvl", a, b), m, AF.Sign, bias=-2048.0)
+            if t > 1:
+                z = cols(bank(), a, b)
+                group([(z, If, cols("i8b", a, b)), (z, ap("Ic"), cols("lvl", a, b))])
+                cp(cols("so", a, b), z)
 
     def mutual(t, shot):
-        j, kn = "j%d" % t, "kA" if t <= 2 else "kB"
+        j, kn, once = "j%d" % t, "kA" if t <= 2 else "kB", t == 1
         for (lo, hi), nxv in OPT["SPREAD"]:
+            at[0] = (lo, hi)
             for b in range(16):
                 o = cols("X", PAD + 16 * lo + b, PAD + 16 * hi, 16)
                 if b < nxv:
                     ts(o, cols("cw", lo, hi), cols("oh", b, b + 1), A.mult)
                 else:
                     act(o, cols("cw", lo, hi), AF.Copy, scale=cols("oh", b, b + 1))
-        k0 = "kk01" if t == 1 else "kk%d" % t
 
-        def partner(c):
-            speeds(t, shot, c)
-            own = ap("kV", t // 3) if c == VC else st("kB" if t <= 2 else "kA", c)
-            if OPT["K0"][c] == "V":
-                tt(ch(k0, c), ind(ap(kn), lst(j, c)), own, A.mult)
-            else:
+        def signs(c):
+            key = "G1" if t == 1 else "PR"
+            r = run(key, c)
+            got = ind(ap("Ew"), lst("so", r))
+            if OPT[key][c] == "S":
+                act(ch("sg1" if t == 1 else "pr", r), got, AF.Sign)
+            elif OPT[key][c] == "V":
+                tt(ch("pr", r), got, ch("nv%d" % t, r), A.mult)
+
+        def hits(c):
+            n = two("ind", 0, c)
+            if OPT["PR"][c] in "sS":
                 z = bk(bank(), c)
-                act(two("ind", 0, c), ind(ap(kn), lst(j, c)), AF.Copy)
-                mm(z, Ib, own, early=True)
-                tt(ch(k0, c), z, two("ind", 0, c), A.mult)
+                mm(z, Ib, ch("pr", c), early=True)
+                tt(ch("pr", c), z, ch("nv%d" % t, c), A.mult)
+            if OPT["NS"][c] == "S":
+                act(n, ch("pr", c), AF.Sign, scale=-1.0 if ups(t, shot, c) else 1.0)
+            else:
+                ts(n, ch("pr", c), 0.0, A.is_lt if ups(t, shot, c) else A.is_gt)
+            if OPT["KK"][c] in "sS":
+                return
+            z = bk(bank(), c)
+            group([(z, Ib, st(kn, c)), (z, Ib, n)])
+            if OPT["KM"][c] == "S":
+                act(two("ind", 1, c), z, AF.Relu, bias=-1.0)
+            else:
+                ts(two("ind", 1, c), z, -1.0, A.add, 0.0, A.max)
 
         for (a, b), then in zip(OPT["BACK"], OPT["THEN"]):
             for c in [c for c in ORD if a <= MC[c][0] < b]:
+                at[0] = c
                 if OPT["MG"][c] == "S":
                     act(ch("mg", c), ind(ap("X"), lst(j, c)), AF.Identity, bias=-float(CENTER[c]))
-                    if c == OPT["MID"]:
-                        gate(len(ops) - 1)
                 else:
                     ts(ch("mg", c), ind(ap("X"), lst(j, c)), -float(CENTER[c]), A.add)
             z = cols(bank(), a, b)
             lanes(z, (If, cols("tgt", a, b)), lambda l: cols("mg", 16 * a + l, 16 * b, 16),
-                  [(ap("Ic"), cols("lvl", a, b)), (If, cols("i8b", a, b))])
-            ts(cols("so", a, b), z, 0.0, A.max, float(2 * WP), A.min)
+                  [(ap("Ic"), cols("lvl", a, b)), (If, cols("i8b", a, b))] if once else [(If, cols("cw", a, b))])
+            ts(cols("so" if once else "sk", a, b), z, 0.0, A.max, float(WP + once * WP), A.min)
             haste(len(ops) - 2)
             if t < 4:
-                act(cols("ab", a, b), z, AF.Abs, bias=-2991.5)
+                act(cols("ab", a, b), z, AF.Abs, bias=-999.5 - once * WP)
             for c in then:
-                partner(c)
+                at[0] = c
+                speeds(t, shot, c)
+        for c in chunks():
+            signs(c)
+        for c in chunks() if t > 1 else ():
+            hits(c)
+        for c in chunks():
+            key = "K1" if t == 1 else "KK"
+            r = run(key, c)
+            got = ind(ap(kn), lst("j1" if once else "sk", r))
+            if t == 1 and OPT[key][c] == "V":
+                tt(ch("kk01", r), got, ap("kV", 0) if c == VC else st("kB", r), A.mult)
+            elif OPT[key][c] == "V":
+                tt(ch("kk%d" % t, r), got, two("ind", 1, r), A.mult)
+            elif OPT[key][c] == "S":
+                act(two("ind", 1, r), got, AF.Copy)
 
     def cursor(t):
         if t == 4:
             return
         z = bank()
-        act(ap("ab"), ap("ab"), AF.Sign, bias=992.25, scale=-1.0)
-        for n in range(3 if t == 2 else 1):
-            act(cols(z, 124 * n, 124 * n + 124), ap("ab"), AF.Relu)
+        act(ap("mu"), ap("ab"), AF.Sign, bias=992.25, scale=-1.0)
+        y = cols(z, 372, 496)
+        if t == 1:
+            act(cols(z, 0, 124), ap("mu"), AF.Relu)
+        else:
+            group([(y, Ib, ap("mu")), (y, Ib, ap("lvl"))])
+            for n in range(3 if t == 2 else 1):
+                act(cols(z, 124 * n, 124 * n + 124), y, AF.Relu, bias=-1.0)
         if t == 1:
             tt(cols(z, 0, 124), ap("curB"), cols(z, 0, 124), A.subtract)
             ts(ap("ci"), cols(z, 0, 124), 2.0, A.add)
@@ -490,33 +556,75 @@ def build(g, T, nxt, prv, place):
         tt(cols("TB", 248, 372), cols(z, 248, 372), cols("TB", 124, 248), A.subtract)
 
     def update(t, shot, c):
-        kk, nv = ch("kk%d" % t, c), ch("nv%d" % t, c)
-        z = bk(bank(), c)
+        kk, nv, kn = ch("kk%d" % t, c), ch("nv%d" % t, c), "kA" if t <= 2 else "kB"
         up = ups(t, shot, c)
-        big = ap("BN" if up else "BP")
-        got = ind(ap("Ew"), lst("so", c))
-        if t == 1 or OPT["PR"][c] == "S":
-            sg = ch("sg1" if t == 1 else "pr", c)
-            if t > 1 or shot == 0:
-                act(sg, got, AF.Sign)
-            mm(z, big, sg, early=True)
+        how, key = load(t, c), "V1" if t == 1 else "V4" if t == 4 else "VU"
+        by = "V" if (t, c) == (2, VC) else OPT[key][c].upper()
+        s, z = -1 if up else 1, None
+        if t == 1:
+            z, other, op = bk(bank(), c), ch("kk01", c), A.min
+            mm(z, ap("BN" if up else "BP"), ch("sg1", c), early=True)
             tt(z, z, nv, A.mult)
+            act(z, z, AF.Relu)
+        elif OPT["KK"][c] in "sS":
+            z, other, op = bk(bank(), c), st(kn, c), A.mult
+            group([(z, Ib, two("ind", 0, c)), (z, Ib, two("ind", 1, c))])
+            act(z, z, AF.Relu, bias=-1.0)
+        zo = opened(c) if by == "O" else None
+        gain = lambda z: zo or z
+        if z is not None and how == "I":
+            tt(z, z, other, op)
+            act(kk, z, AF.Copy)
+            tt(gain(z), z, nv, A.mult)
         else:
-            tt(ch("pr", c), got, nv, A.mult)
-            mm(z, big, ch("pr", c))
-        tt(kk, z, ch("kk01", c) if t == 1 else kk, A.min)
-        act(z, kk, AF.Relu)
-        tt(z, z, nv, A.mult)
-        if up:
+            if z is not None:
+                tt(kk, z, other, op)
+            z = held.pop((t, c), None)
+            if z is None:
+                z = bk(bank(), c)
+                if how == "S":
+                    act(z, nv, AF.Copy, scale=float(s), early=True)
+                else:
+                    mm(z, signed(s), nv, early=True)
+            s = 1
+            tt(gain(z), z, kk, A.mult)
+        old = (Ib, st("q0b", c)) if t == 1 else (If, st("q", c))
+        aim = (app("Sel", slice(0, 8)), app("aimA", slice(0, 8), slice(*CH[c])))
+        if by == "O" and t == 4:
+            assert s > 0
+            for n, (l, r) in enumerate([(If, st("vs", c)), old, aim]):
+                mm(zo, l, r, False, n == 2)
+            act(st("q", c), zo, AF.Copy)
+            if c == VC:
+                send("a%d" % shot, vis("q"), prv)
+            return
+        if t == 4 and OPT["AQ"][c] == "O":
+            zo = opened(c)
+            if s < 0:
+                tt(zo, st("vs", c), z, A.subtract)
+            else:
+                tt(zo, z, st("vs", c), A.add)
+            for n, (l, r) in enumerate([old, aim]):
+                mm(zo, l, r, False, n == 1)
+            act(st("q", c), zo, AF.Copy)
+            if c == VC:
+                send("a%d" % shot, vis("q"), prv)
+            return
+        if by == "O":
+            mm(zo, signed(s), st("vs", c), False, True)
+            act(st("vs", c), zo, AF.Copy, scale=float(s))
+        elif s < 0:
             tt(st("vs", c), st("vs", c), z, A.subtract)
         else:
             tt(st("vs", c), z, st("vs", c), A.add)
         if t == 2 and c == VC:
             send("v%d" % shot, vis("vs"), nxt)
             return
-        old = (Ib, st("q0b", c)) if t == 1 else (If, st("q", c))
+        if t < 4 and v_twice(c):
+            dma("y", st("vs'", c), st("vs", c))
+        key = "Q" if t > 1 else "Q1"
         if t == 4:
-            z, aim = bk(bank(), c), (app("Sel", slice(0, 8)), app("aimA", slice(0, 8), slice(*CH[c])))
+            z = bk(bank(), c)
             if OPT["AQ"][c] == "P":
                 total(z, old, (If, st("vs", c)), aim)
                 act(st("q", c), z, AF.Copy)
@@ -529,39 +637,38 @@ def build(g, T, nxt, prv, place):
             if c == VC:
                 send("a%d" % shot, vis("q"), prv)
             return
-        if v_twice(c):
-            dma("y", st("vs'", c), st("vs", c))
-        key = "Q" if t > 1 else "Q1"
         how = OPT[key][c]
         if how in "dD":
             r = span(key, c, PAD, VC - (t == 2))
             if r:
-                for n in ("q", "q'")[:1 + q_twice(c)]:
-                    dma("g", cols(n, *r), cols("vs", *r), True)
+                for n, a, b in both(r):
+                    dma("g", cols(n, a, b), cols("vs", a, b), True)
             if t == 1 and r and r[1] == WP:
                 send("q%d" % shot, vis("q"), nxt)
             return
         else:
-            z = bk(bank(), c)
+            z = zo if (how, by, s) == ("V", "O", 1) and t > 1 else bk(bank(), c)
             if how == "P":
                 total(z, old, (If, st("vs", c)))
                 act(st("q", c), z, AF.Copy)
+            elif z is zo:
+                tt(st("q", c), z, st("q", c), A.add)
             else:
                 mm(z, *old, early=True)
                 tt(st("q", c), z, st("vs", c), A.add)
             if q_twice(c):
-                if OPT["Q2"][c] == "S":
-                    act(st("q'", c), z if how == "P" else st("q", c), AF.Copy)
+                if OPT["Q2"][c] == "S" and how == "P":
+                    act(st("q'", c), z, AF.Copy)
                 else:
-                    dma("y", st("q'", c), st("q", c))
+                    again(OPT["Q2"][c], st("q'", c), st("q", c))
         if t == 1 and c == VC:
             send("q%d" % shot, vis("q"), nxt)
 
     def q_start():
         for c in ORD:
             if OPT["Q1"][c] == "D":
-                for n in ("q", "q'")[:1 + q_twice(c)]:
-                    dma("g", cols(n, *span("Q1", c, PAD)), ("q0", (ALL, slice(*span("Q1", c)))))
+                for n, a, b in both(span("Q1", c, PAD)):
+                    dma("g", cols(n, a, b), ("q0", (ALL, slice(a - PAD, b - PAD))))
 
     def inverse(after):
         for c in ORD:
@@ -573,64 +680,77 @@ def build(g, T, nxt, prv, place):
     def newton(cs, after):
         for c in cs:
             z = bk(bank(), c)
-            mm(z, Ib, st("kA", c))
+            mm(z, Nb, st("kA", c))
             ops[-1]["after"] = after
+            if OPT["NW"][c] == "O":
+                act(st("X", c), ch("rk", c), AF.Square)
+                zo = opened(c)
+                tt(zo, z, st("X", c), A.mult)
+                mm(zo, ap("N2"), ch("rk", c), False, True)
+                act(ch("rk", c), zo, AF.Copy)
+                continue
             tt(z, z, ch("rk", c), A.mult)
-            act(z, z, AF.Identity, bias=-2.0)
+            act(z, z, AF.Identity, bias=2.0)
             tt(ch("rk", c), z, ch("rk", c), A.mult)
 
     def squares(after):
         for c in ORD:
             o = ap("Gh") if c == VC else ch("nv4", c)
             act(o, st("kA", c), AF.Square, after=after)
-            act(o, o, AF.Copy, scale=-1.0)
 
     AV = {4: ("q", "vs'"), 3: ("vs'", "vs"), 2: ("vs", "vs'"), 1: ("vs'", None)}
 
+    plus = lambda t, shot, c: not ups(t, shot, c)
+
     def product(t, shot, c):
-        av, kk, d, up = AV[t][0], ch("kk%d" % t, c), two("D", 0, c), ups(t, shot, c)
+        av, kk, d, up = AV[t][0], ch("kk%d" % t, c), two("D", 0, c), plus(t, shot, c)
         got = ind(whole(av), lst("j%d" % t, c))
-        x = bk(bank(), c)
-        key = "DA" if t > 1 else "A%d" % shot
-        if OPT[key][c] == "P":
-            act(kk, kk, AF.Relu, after=ends[t] if OPT["RL"] else mark[t == 4])
-            mm(x, If if up else Nf, st(av, c), True, False, "fresh")
+        x, key = None, "DA%d" % t if t > 1 else "A%d" % shot
+        if OPT[key][c] in "OP":
+            if OPT[key][c] == "O":
+                x = opened(c)
+                act(x, st(av, c), AF.Copy, scale=1.0 if up else -1.0)
+            else:
+                x = bk(bank(), c)
+                mm(x, If if up else Nf, st(av, c), True, False, "fresh")
             act(d, got, AF.Copy)
             mm(x, Nf if up else If, d, False, True)
-        elif OPT[key][c] == "S":
-            act(kk, kk, AF.Relu, after=ends[t] if OPT["RL"] else mark[t == 4])
-            act(x, st(av, c), AF.Copy, early="fresh")
-            act(d, got, AF.Copy)
-            if up:
-                tt(x, x, d, A.subtract)
-            else:
-                tt(x, d, x, A.subtract)
-        elif OPT[key][c] == "V":
+            return x
+        if OPT[key][c] in "vV":
             act(st("q'", c), st(av, c), AF.Copy)
-            tt(d, got, st("q'", c), A.subtract)
-        else:
-            act(d, got, AF.Copy, scale=-1.0)
-            if span(key, c):
-                dma("g", ap("D", 0, slice(*span(key, c))), cols(av, *span(key, c, PAD)), True)
-        return x
+        r = run(key, c)
+        got = ind(whole(av), lst("j%d" % t, r))
+        if OPT[key][c] == "V":
+            tt(two("D", 0, r), got, st("q'", r), A.subtract)
+        elif OPT[key][c] == "D":
+            act(two("D", 0, r), got, AF.Copy, scale=-1.0)
+            dma("g", two("D", 0, r), st(av, r), True)
 
     def backward(t, shot, c, x):
         av, new = AV[t]
         kk, nv = ch("kk%d" % t, c), ch("nv%d" % t, c)
-        last = shot == 1 and t == 1
+        last, bb = shot == 1 and t == 1, "BB%d" % t
         d = two("D", 0, c)
-        ys = lambda a, b: ap("D", 1, slice(a, b)) if t % 2 else cols("X", PAD + a, PAD + b)
+        ys = lambda a, b: ap("D", 1, slice(a, b)) if t == 1 else cols("nv%d" % t, a, b)
         y = ys(*CH[c])
-        if OPT["DA" if t > 1 else "A%d" % shot][c] in "PS":
+        if x is not None:
             tt(x, x, kk, A.mult)
         else:
-            act(x, kk, AF.Relu, early=True)
+            r = 1 if plus(t, shot, c) != (OPT["DA%d" % t if t > 1 else "A%d" % shot][c] in "vV") else -1
+            x = bk(bank(), c)
+            if OPT["KL" if t > 1 else "KM%d" % shot][c] == "S":
+                act(x, kk, AF.Copy, scale=float(r), early=True)
+            else:
+                mm(x, signed(r), kk, early=True)
             tt(x, x, d, A.mult)
 
         def gains():
             if last:
-                z = bk(bank(), c)
-                if OPT["U"][c] == "P":
+                z = opened(c) if OPT["U"][c] == "O" else bk(bank(), c)
+                if OPT["U"][c] == "O":
+                    tt(z, x, nv, A.mult)
+                    mm(z, If, ch("G", c), False, True)
+                elif OPT["U"][c] == "P":
                     tt(y, x, nv, A.mult)
                     total(z, (If, ch("G", c)), (If, y))
                 else:
@@ -640,13 +760,9 @@ def build(g, T, nxt, prv, place):
                 dma("y", ("yg", (ALL, slice(*CH[c]))), y)
             elif (shot, t) == (0, 4):
                 tt(ch("G", c), x, nv, A.mult)
-            elif (shot, t, c) == (1, 3, VC) and not OPT["GV"]:
+            elif (shot, t, c) == (1, 3, VC):
                 tt(y, x, nv, A.mult)
                 dma("g", ch("G", c), y, True)
-                send("G", ch("G", c), prv)
-            elif (shot, t, c) == (1, 3, VC):
-                tt(x, x, nv, A.mult)
-                tt(ch("G", c), x, ch("G", c), A.add)
                 send("G", ch("G", c), prv)
             else:
                 tt(y, x, nv, A.mult)
@@ -658,7 +774,7 @@ def build(g, T, nxt, prv, place):
                     dma("g", cols("G", *r), ys(*r), True)
 
         def less(o):
-            if ups(t, shot, c):
+            if plus(t, shot, c):
                 tt(o, st(av, c), x, A.subtract)
             else:
                 tt(o, x, st(av, c), A.add)
@@ -667,20 +783,32 @@ def build(g, T, nxt, prv, place):
             less(st(new, c))
             send("w%d" % shot, st(new, c), prv)
             gains()
-        elif t > 1 and OPT["BB"][c] == "P":
-            act(d, x, AF.Copy)
-            z = bk(bank(), c)
-            total(z, (If, st(av, c)), (Nf if ups(t, shot, c) else If, d), (If, st("q", c)))
+        elif t > 1 and OPT[bb][c] == "O":
+            z = opened(c)
+            less(z)
+            mm(z, If, st("q", c), False, True)
             act(st(new, c), z, AF.Copy)
             gains()
-        elif t > 1 and OPT["BB"][c] in "dD":
+        elif t > 1 and OPT[bb][c] == "Q":
+            z = opened(c)
+            act(z, x, AF.Copy, scale=-1.0 if plus(t, shot, c) else 1.0)
+            mm(z, If, st(av, c), False, False)
+            mm(z, If, st("q", c), False, True)
+            act(st(new, c), z, AF.Copy)
+            gains()
+        elif t > 1 and OPT[bb][c] in "dD":
             less(st(new, c))
-            r = span("BB", c, PAD, VC - (t == 3))
+            r = span(bb, c, PAD, VC - (t == 3))
             if r:
                 dma("g", cols(new, *r), cols("q", *r), True)
             gains()
         else:
-            if OPT["YA"][c] == "I":
+            if t == 1 and OPT["L%d" % shot][c] == "Q":
+                z = opened(c)
+                act(z, x, AF.Copy, scale=-1.0 if plus(t, shot, c) else 1.0)
+                mm(z, If, st(av, c), False, True)
+                gains()
+            elif OPT["YA" if t > 1 else "Y%d" % shot][c] == "I":
                 gains()
                 z = x
                 less(z)
@@ -700,28 +828,31 @@ def build(g, T, nxt, prv, place):
                         add("g", lambda: g.dma_start(T.yv[:, r[0]:r[1]], R(ap("D", 0, slice(*r))), accum_op=A.add),
                             [ap("D", 0, slice(*r)), ap("ones")], [], (r[1] - r[0]) * 1024 / 600e3, "d")
                     return
-                if how == "P":
-                    ts(d, z, -3.0, A.max, 3.0, A.min)
-                    z = bk(bank(), c)
-                    total(z, (If, ch("v0f", c)), (Nf, d))
-                    if not shot:
-                        act(ch("v0f", c), z, AF.Copy)
+                s = -1.0 if how == "O" else 1.0
+                if how == "O":
+                    zo = opened(c)
+                    ts(zo, z, -3.0, A.max, 3.0, A.min)
+                    z = zo
+                    mm(z, Nf, ch("v0f", c), False, True)
                 else:
                     ts(z, z, -3.0, A.max, 3.0, A.min)
                     tt(ch("v0f", c), ch("v0f", c), z, A.subtract)
                     z = ch("v0f", c)
                 if shot:
-                    act(ch("v0f", c), z, AF.Copy, scale=0.0625)
+                    act(ch("v0f", c), z, AF.Copy, scale=0.0625 * s)
                     dma("s", ("yv", (ALL, slice(*CH[c]))), ch("v0f", c))
                 else:
                     for n in ("vs", "vs'")[:1 + v_twice(c, "D1")]:
-                        act(st(n, c), z, AF.Copy, scale=2.0 ** -8)
+                        act(st(n, c), z, AF.Copy, scale=2.0 ** -8 * s)
+                    if how == "O":
+                        act(ch("v0f", c), z, AF.Copy, scale=s)
 
     send("k", ap("kV", 0), nxt)
     for shot in (0, 1):
         q_start()
         for t in (1, 2, 3, 4):
             first = len(ops)
+            step[0] += 1
             if shot == 1 and t == 1:
                 for c in chunks():
                     speeds(1, 1, c)
@@ -729,19 +860,18 @@ def build(g, T, nxt, prv, place):
                 tests(t)
                 mutual(t, shot)
             gate(first)
-            mark[1] = len(ops) - 1
             for c in chunks():
                 update(t, shot, c)
                 if c == OPT["CUR"] and (shot, t) != (1, 1):
                     cursor(t)
                 if c == OPT["INV"][2]:
-                    mark[2] = ends[t] = len(ops) - 1
+                    mark[1] = len(ops) - 1
             mark[0] = len(ops) - 1
             if (shot, t) == OPT["INV"][:2]:
-                inverse(mark[2])
+                inverse(mark[1])
             if (shot, t) == (0, 1):
                 arrive("k")
-                turn(True, ["k"], [vis("kB"), ap("kV", 1)])
+                turn(True, ["k"], [vis("kB")])
             if t == 2:
                 arrive("q%d" % shot)
                 turn(True, ["q"], [vis("q")])
@@ -756,6 +886,7 @@ def build(g, T, nxt, prv, place):
                 arrive("G")
                 turn(False, ["G"], [ch("G", VC)], ["Gh"])
             first = len(ops)
+            step[0] += 1
             x = {c: product(t, shot, c) for c in chunks()}
             gate(first)
             for c in chunks():
@@ -782,9 +913,17 @@ def build(g, T, nxt, prv, place):
     return ops
 
 
+BITS = {}
+
+
 def region(x):
-    p = range(128)[x[1][0]]
-    return slice(p[0] // 32, p[-1] // 32 + 1), flat(x[0])[x[1][1:]].ravel()
+    key = ("#" if psum(x) else x[0], repr(x[1]))
+    if key not in BITS:
+        p, n = range(128)[x[1][0]], flat(x[0]).size
+        m = np.zeros((4, n), np.uint8)
+        m[p[0] // 32:p[-1] // 32 + 1, flat(x[0])[x[1][1:]].ravel()] = 1
+        BITS[key] = int.from_bytes(np.packbits(m.ravel()).tobytes(), "big")
+    return BITS[key]
 
 
 def needs(ops, name, banks):
@@ -795,26 +934,23 @@ def needs(ops, name, banks):
         deps, me = set(), who(n)
         R = [(name(x), region(x)) for x in o["rd"]]
         Wr = [(name(x), region(x)) for x in o["wr"]]
-        for k, (qd, c) in R + Wr:
+        for k, b in R + Wr:
             if k not in wr:
-                wr[k], rd[k], last[k] = np.full((4, flat(k).size), -1), {}, {}
-            deps.update(np.unique(wr[k][qd][:, c]).tolist())
-        for k, (qd, c) in Wr:
-            for m, arr in list(rd[k].items()):
-                if arr[qd][:, c].any():
-                    deps.add(m)
-                    arr[qd, c] = False
-                    if not arr.any():
-                        del rd[k][m]
+                wr[k], rd[k], last[k] = {}, {}, {}
+            deps.update(m for m, x in wr[k].items() if x & b)
+        for k, b in Wr:
+            deps.update(m for m, x in rd[k].items() if x & b)
+            rd[k] = {m: x & ~b for m, x in rd[k].items() if x & ~b}
         for k, _ in R + Wr:
             if psum((k,)):
                 deps.update(m for e, m in last[k].items() if (e != me if banks else e == me == "t"))
                 last[k][me] = n
-        for k, (qd, c) in R:
-            rd[k].setdefault(n, np.zeros((4, flat(k).size), bool))[qd, c] = True
-        for k, (qd, c) in Wr:
-            wr[k][qd, c] = n
-        deps -= {-1, n}
+        for k, b in R:
+            rd[k][n] = rd[k].get(n, 0) | b
+        for k, b in Wr:
+            wr[k] = {m: x & ~b for m, x in wr[k].items() if x & ~b}
+            wr[k][n] = wr[k].get(n, 0) | b
+        deps.discard(n)
         out.append(deps)
     return out
 
@@ -847,45 +983,78 @@ def arrange(ops):
                 for m in deps[d] - deps[n]:
                     deps[n].add(m)
                     kids[m].append(n)
-    cases = [[dict(o, cost=o["cost"] * (ga if o.get("gather") else pe if o["eng"] == "t" else 1.0 if o["kind"] == "c" else slow), lag=lag, slow=slow)
-              for o in ops] for ga, pe, lag, slow in OPT["CASES"]]
+    cases = [[dict(o, cost=o["cost"] * (ga if o["gather"] else pe if o["eng"] == "t" else slow if o["kind"] != "c" else 1.0),
+                   lag=lag, slow=slow) for o in ops] for ga, pe, lag, slow in OPT["CASES"]]
     rules = []
-    for case in cases[:OPT["MAKE"]]:
-        for patience in OPT["WAIT"]:
-            chain = [-2.0 * n for n in range(len(ops))]
-            for _ in range(OPT["PASS"]):
-                end = forwards(case, deps, kids, names, left, chain, issue, delay, hop, patience)[5]
-                chain = [x + o["lead"] for x, o in zip(backwards(case, deps, kids, end, issue, delay, hop), ops)]
-                rules.append((chain, patience))
+    for patience in OPT["WAIT"]:
+        chain = [-2.0 * n for n in range(len(ops))]
+        for _ in range(OPT["PASS"]):
+            end = forwards(cases[0], deps, kids, names, left, chain, issue, delay, hop, patience)[5]
+            chain = [x + o["lead"] for x, o in zip(backwards(cases[0], deps, kids, end, issue, delay, hop), ops)]
+            rules.append((chain, patience))
 
     def replay(case, seq, place, was):
-        clock, pipe, used, end = [dict(x) for x in was]
+        clock, pipe, used, end = dict(was[0]), dict(was[1]), {b: dict(x) for b, x in was[2].items()}, was[3][:]
         for n in seq:
             o = case[n]
-            e = o["eng"]
-            t = max([clock.get(e, 0.0)] + [end[m] + hop(case[m], o) for m in deps[n]]
-                    + [x + OPT["HOP"] * o["lag"] for k in names[n] for (b, f), x in used.items() if b == place[k] and f != e])
-            if o["kind"] != "a":
-                clock[e] = t + issue(o)
-            if o["kind"] in "dr":
-                pipe[o["kind"]] = max(t + issue(o) + delay(o) / 2, pipe.get(o["kind"], 0.0)) + o["cost"]
-            end[n] = pipe[o["kind"]] + delay(o) / 2 if o["kind"] in "dr" else t + o["cost"]
+            e, t = o["eng"], clock[o["eng"]]
+            for m, h in o["from"]:
+                if end[m] + h > t:
+                    t = end[m] + h
             for k in names[n]:
-                used[place[k], e] = end[n]
+                for f, x in used[place[k]].items():
+                    if f != e and x + o["wake"] > t:
+                        t = x + o["wake"]
+            if o["kind"] == "c":
+                end[n] = clock[e] = t + o["cost"]
+            elif o["kind"] == "a":
+                end[n] = t
+            else:
+                clock[e] = t + issue(o)
+                pipe[o["kind"]] = max(clock[e] + delay(o) / 2, pipe[o["kind"]]) + o["cost"]
+                end[n] = pipe[o["kind"]] + delay(o) / 2
+            for k in names[n]:
+                used[place[k]][e] = end[n]
         return clock, pipe, used, end
 
-    state, was = None, [({}, {}, {}, {}) for _ in cases]
-    for gate in [n for n, o in enumerate(ops) if "gate" in o] + [None]:
-        best = None
-        for chain, patience in rules:
-            s = forwards(cases[0], deps, kids, names, left, chain, issue, delay, hop, patience, state, gate)
-            now = [replay(case, s[9][len(state[9]) if state else 0:], s[0], w) for case, w in zip(cases, was)]
-            owed = [] if gate is None else [n for n in set(range(gate)) - set(s[9]) if ops[n]["eng"] == "v"]
-            late = sum(max(x[3].values() if gate is None else [x[3][m] for m in deps[gate]]) + OPT["OWE"] * sum(case[n]["cost"] for n in owed)
-                       for case, x in zip(cases, now))
-            if best is None or late < best[0]:
-                best = (late, s, now)
-        state, was = best[1:]
+    for case in cases:
+        for n, o in enumerate(case):
+            o.update({"from": [(m, hop(case[m], o)) for m in deps[n]], "wake": OPT["HOP"] * o["lag"]})
+    was = [({e: 0.0 for e in ENG}, {"d": 0.0, "r": 0.0}, {b: {} for b in BANKS}, [0.0] * len(ops)) for _ in cases]
+    state, dice = None, np.random.default_rng(OPT["SEED"])
+    gates = [n for n, o in enumerate(ops) if "gate" in o] + [None] * (1 + OPT["AHEAD"])
+    kin = [lambda o: o["tag"], lambda o: o["tag"][:2], lambda o: o["tag"][2], lambda o: (o["tag"][0], o["tag"][2])]
+    best = None
+    for gate, far in zip(gates, gates[OPT["AHEAD"]:]):
+        some, best, done, unit = rules + ([best[2:]] if best else []), None, len(state[9]) if state else 0, None
+        for turn in range(len(some) + OPT["TRIES"]):
+            if turn < len(some):
+                chain, patience = some[turn]
+            else:
+                chain, patience = list(best[2]), best[3]
+                for _ in range(1 + turn % 2):
+                    like, n, x = kin[dice.integers(4)], best[1][dice.integers(done, len(best[1]))], float(dice.normal()) * OPT["SHAKE"]
+                    for m in best[1][done:]:
+                        if like(ops[m]) == like(ops[n]):
+                            chain[m] += x
+            s = forwards(cases[0], deps, kids, names, left, chain, issue, delay, hop, patience, state, far)
+            if s is None:
+                continue
+            owed = [] if far is None else [n for n in set(range(far)) - set(s[9]) if ops[n]["eng"] == "v"]
+            late = []
+            for case, w in zip(cases, was):
+                x = replay(case, s[9][done:], s[0], w)[3]
+                late.append(max(x if far is None else [x[m] for m in deps[far]]) + OPT["OWE"] * sum(case[n]["cost"] for n in owed)
+                            - max(w[0].values()))
+                if best and len(late) == 2 and sum(late) > 1.004 * sum(each[:2]):
+                    break
+            else:
+                unit = unit or late
+                mean = sum(a * x / b for a, b, x in zip(late, unit, OPT["WEIGHT"])) + OPT["WORST"] * max(a / b for a, b in zip(late, unit))
+                if best is None or mean <= best[0]:
+                    best, each = (mean, s[9], chain, patience), late
+        state = forwards(cases[0], deps, kids, names, left, best[2], issue, delay, hop, best[3], state, gate)
+        was = [replay(case, state[9][done:], state[0], w) for case, w in zip(cases, was)]
     return state[9], state[0]
 
 
@@ -922,11 +1091,11 @@ def forwards(ops, deps, kids, names, left, chain, issue, delay, hop, patience, s
     used, ready = {b: dict(x) for b, x in used.items()}, {e: list(x) for e, x in ready.items()}
     end, wait, can, out = list(end), list(wait), list(can), list(out)
 
-    def start(n, spare):
+    def start(n):
         o, t = ops[n], can[n]
         new = [k for k in names[n] if k not in place]
         if new:
-            if len(free) < len(new) + (spare if o.get("early") else 0):
+            if len(free) < len(new):
                 return None
             t = max(t, sorted(free.values())[len(new) - 1] + OPT["HOP"] * o["lag"])
         for k in names[n]:
@@ -935,11 +1104,10 @@ def forwards(ops, deps, kids, names, left, chain, issue, delay, hop, patience, s
         return t
 
     while len(out) < len(ops) and (until is None or wait[until]):
-        for spare in (OPT["RES"], 0):
-            cand = {e: [(t, n) for n in ready[e] for t in [start(n, spare)] if t is not None] for e in ENG}
-            when = [(max(clock[e], min(c)[0]), e) for e, c in cand.items() if c]
-            if when:
-                break
+        cand = {e: [(t, n) for n in ready[e] for t in [start(n)] if t is not None] for e in ENG}
+        when = [(max(clock[e], min(c)[0]), e) for e, c in cand.items() if c]
+        if not when:
+            return None
         now, e = min(when)
         t, n = max([x for x in cand[e] if x[0] <= now + 0.05], key=lambda x: chain[x[1]])
         soon = [x for x in cand[e] if x[0] < now + patience["haste" in ops[x[1]]] * issue(ops[n])

import numpy as np
from concourse.mybir import AluOpType, ActivationFunctionType

W, V0, VI, PAD = 1984, 1664, 320, 8
WP = W + PAD
MC = [(0, 20), (20, 48), (48, 76), (76, 104), (104, 124)]
CH = [(16 * a, 16 * b) for a, b in MC]
VC = 4
ORD = (4, 3, 2, 1, 0)
CENTER = [8 * (a + b) + 8 for a, b in MC]
NEAR = 11228502 * 2.0 ** -24
GRID = 1.5 * 2 ** 23
BASE = float(2 ** 22 + 2048)
F, B, I, U = "float32", "bfloat16", "int32", "uint16"
MSG = ["k", "q0", "v0", "a0", "w0", "q1", "v1", "a1", "w1", "G"]

SCRATCH = {}
for _n, _s, _d in (
    [("q", [2, WP + PAD], F), ("vs", [2, WP + PAD], F), ("kV", [1, VI], B), ("D", [2, W], F), ("Ew", [2 * WP + PAD], B), ("X", [WP + PAD], F),
     ("kk01", [W], F), ("G", [W], F), ("Gh", [VI], F), ("rk", [W], F), ("v0f", [W], F), ("ind", [2, W], B), ("mg", [W], B), ("pr", [W], B),
     ("sg1", [W], B), ("q0b", [WP], B), ("kA", [WP + PAD], B), ("kB", [WP + PAD], B), ("aimA", [W], B), ("Wc", [16, 128], B),
     ("E", [256], F), ("Eb", [256], B), ("ones", [128], F), ("Nf", [128], F), ("N2", [128], F), ("Nb", [128], B), ("Ic", [128], B), ("Sel", [128], B),
     ("BP", [128], B), ("BN", [128], B), ("L", [16, 8], F), ("L1", [16, 8], F),
     ("iL", [16, 8], I), ("iS", [128], I), ("iO", [16], I), ("iG", [8], I), ("iP", [1], I), ("pcol", [1], F), ("oh", [16], F),
     ("G8", [8], B), ("bias", [124], B), ("i8", [124], F), ("i8b", [124], F), ("tgt", [124], F),
     ("ct", [2, 31, 16], I), ("conf", [31, 32], F),
     ("cu", [2, 4, 16], I), ("cf", [4, 32], F), ("cf2", [4, 32], F), ("curB", [124], F), ("c2", [124], F), ("ci", [124], I),
     ("Pi", [248], I), ("Ph", [248], I), ("JJ", [248], I), ("JJ2", [248], I), ("of", [248], U), ("of2", [248], U), ("A", [124], F),
     ("cw", [124], F), ("lvl", [124], B), ("so", [124], U), ("sk", [124], U), ("ab", [124], F), ("mu", [124], B),
     ("TA", [372], F), ("TB", [372], F), ("UV", [248], F), ("l_k", [VI], B)]
    + [("kk%d" % t, [W], F) for t in (1, 2, 3, 4)] + [("nv%d" % t, [W], F) for t in (1, 2, 3, 4)]
    + [("j%d" % t, [124], U) for t in (1, 2, 3, 4)] + [("l_" + m, [VI], F) for m in "qvawG"]
):
    SCRATCH[_n] = ("sbuf", [128] + _s, _d)
BANKS = ["P%d" % _n for _n in range(8)]
for _n in BANKS:
    SCRATCH[_n] = ("psum", [128, 512], F)
ENG = ["v", "s", "t", "g", "y"]
SEMAPHORES = ["e_" + e for e in ENG] + ["d%d" % n for n in range(130)] + ["r_" + m for m in MSG]

ALL = slice(None)
OPT = {"T0": "VVvPV", "T1": "VvvDP", "F0": "VvvPP", "F1": "VVvPP", "E0": "SSSVS", "E1": "SSSSS", "MG": "SSSSS",
       "DV": "DDVVV", "D1": "PVPVV", "PR": "VVVVV", "G1": "SSSsS", "NS": "SVSVV", "KM": "SSSSS", "KK": "SVVVS", "K1": "VVvVV",
       "PL": "SSSSS", "P1": "SSIIK", "VU": "OOOOV", "V1": "VOVVO", "V4": "VVVVV", "Q": "VVVDd", "Q1": "VPPVV", "Q2": "SSSDD", "AQ": "OVOOO",
       "DA4": "OPPVV", "DA3": "OOVPV", "DA2": "OVOPV", "A0": "PVPOV", "A1": "PPVOV", "KL": "TSSSS", "KM0": "TSSTS", "KM1": "STSSS",
       "BB4": "VQVDO", "BB3": "VVVDd", "BB2": "VOVOV", "L0": "VQQVV", "L1": "VQVVV", "YA": "AIIII", "Y0": "AAIAA", "Y1": "IAIAA",
       "GG": "DdDdd", "C0": "VOVVV", "C1": "VVDDD", "U": "VVPOO", "NW": "VOOOO",
       "HALF": ((0, 76), (76, 124)), "SPREAD": (((0, 76), 8), ((76, 124), 8)), "BACK": ((104, 124), (48, 104), (0, 48)), "THEN": ((4, 3, 2), (1, 0), ()),
       "INV": (0, 3, 1), "NEW": ((4, 3), (2, 1, 0)), "SQ": 4, "CUR": 2,
       "GI": 1.1, "GD": 2.2, "RD": 3.0, "RC": 2.5, "HOP": 0.2, "OV": 0.01, "GA": 1.56, "PE": 0.42e-3,
       "CASES": ((1.0, 1.1, 1.3, 0.85), (1.25, 1.0, 1.0, 0.5), (0.8, 1.0, 1.8, 0.65), (1.0, 1.3, 0.9, 0.55), (1.0, 1.0, 1.3, 1.4)),
       "WEIGHT": (0.2, 0.25, 0.15, 0.15, 0.25), "WORST": 0.5, "WAIT": ((0.3, 0.7, 1.0), (0.3, 0.7, 0.6)), "SPARE": {"k": 10.0, "q": 5.0, "a": 3.0},
       "FIRST": 4.0, "PASS": 3, "OWE": 0.8, "AHEAD": 1, "TRIES": 750, "SHAKE": 1.5, "SEED": 2}
CY = 0.83e-3


def ap(name, *idx):
    return (name, (ALL,) + idx)


def app(name, part, *idx):
    return (name, (part,) + idx)


def cols(name, a, b, step=None):
    if name[-1] == "'":
        return (name[:-1], (ALL, 1, slice(a, b, step)))
    if name in ("q", "vs"):
        return (name, (ALL, 0, slice(a, b, step)))
    return (name, (ALL, slice(a, b, step)))


def ind(win, off):
    return ("@", win, off)


FLAT = {n: np.arange(int(np.prod(s[1][1:]))).reshape(s[1][1:]) for n, s in SCRATCH.items()}


def psum(x):
    return x[0][0] == "#" or x[0] in BANKS


def flat(name):
    return FLAT["P0" if name[0] == "#" else name]


def size(x):
    return 16 * size(x[2]) if x[0] == "@" else int(flat(x[0])[x[1][1:]].size)


def narrow(*xs):
    return all(not psum(x) and SCRATCH[x[0]][2] in (B, U) for x in xs)


def build(g, T, nxt, prv, place):
    A, AF = AluOpType, ActivationFunctionType
    ops = []
    nb, lead, mark, held, step, at = [0], [0], [0, 0], {}, [0], [None]

    def bank():
        nb[0] += 1
        return "#%d" % nb[0]

    def R(x):
        if not isinstance(x, tuple):
            return x
        if x[0] == "@":
            return R(x[1]).indirect(R(x[2]))
        return T[place.get(x[0], x[0])][x[1]]

    def parts(xs):
        out = []
        for x in xs:
            if isinstance(x, tuple):
                out += [x[1], x[2]] if x[0] == "@" else [x]
        return [x for x in out if x[0] in SCRATCH or x[0][0] == "#"]

    def add(eng, f, rd, wr, cost, kind="c", **kw):
        x = (parts(wr) + parts(rd))[0]
        kw["tag"] = (step[0], eng + kind + ("#" if psum(x) else x[0]) + "".join("#" if psum(y) else y[0] for y in parts(rd)), at[0])
        ops.append(dict(eng=eng, f=f, rd=parts(rd), wr=parts(wr), cost=cost, kind=kind, lead=lead[0],
                        gather=any(isinstance(x, tuple) and x[0] == "@" for x in rd), **kw))

    def gate(first):
        [o for o in ops[first:] if o["cost"] > 0.3 and o["eng"] in "vs" and len(o["rd"]) > 1][0]["gate"] = True

    def haste(first):
        for o in ops[first:]:
            o["haste"] = True

    def chunks():
        for c in ORD:
            lead[0], at[0] = 0, c
            yield c
        at[0] = None

    def price(o, a, b=None):
        if a[0] == "@":
            return 0.06 + size(a) * OPT["GA"] * CY
        r = 0.5 if narrow(o, a) else 1.0
        if b is not None:
            r = 1.0 if psum(a) or psum(b) else 2.0
        return OPT["OV"] + max(64, size(a) * r) * CY

    def tt(o, a, b, op):
        add("v", lambda: g.vector.tensor_tensor(R(o), R(a), R(b), op), [a, b], [o], price(o, a, b))

    def ts(o, a, s1, op0, s2=None, op1=None):
        if op1 is None:
            add("v", lambda: g.vector.tensor_scalar(R(o), R(a), R(s1), None, op0), [a, s1], [o], price(o, a))
        else:
            add("v", lambda: g.vector.tensor_scalar(R(o), R(a), R(s1), R(s2), op0, op1), [a, s1, s2], [o], price(o, a))

    def cp(o, a):
        add("v", lambda: g.vector.tensor_copy(R(o), R(a)), [a], [o], price(o, a))

    def fill(o, c):
        add("v", lambda: g.vector.memset(R(o), c), [], [o], price(o, o))

    def flip(o, a):
        add("v", lambda: g.vector.transpose(R(o), R(a)), [a], [o], price(o, a))

    def act(o, a, func, bias=0.0, scale=1.0, more=0.0, **kw):
        c = price(o, a) if a[0] == "@" else OPT["OV"] + max(64, size(a)) * CY
        add("s", lambda: g.scalar.activation(R(o), R(a), func, bias=R(bias), scale=R(scale)), [a, bias, scale], [o], c + more, **kw)

    def mm(o, l, r, start=True, stop=True, early=False):
        c = max(64, size(r)) * OPT["PE"] * (1 if narrow(r) else 4)
        add("t", lambda: g.tensor.matmul(R(o), R(l), R(r), start, stop), [l, r], [o], c, early=early or (start and not stop))

    def lanes(o, first, src, last):
        group([(o, l, r) for l, r in [first] + [(ap("Wc", l), src(l)) for l in range(16)] + last])

    def group(terms):
        c = sum(max(64, size(r)) * OPT["PE"] * (1 if narrow(r) else 4) for _, _, r in terms)
        add("t", lambda: [g.tensor.matmul(R(o), R(l), R(r), n == 0, n == len(terms) - 1) for n, (o, l, r) in enumerate(terms)][-1],
            [x for p in terms for x in p[1:]], [terms[0][0]], c)

    def total(o, *terms):
        for n, (l, r) in enumerate(terms):
            mm(o, l, r, n == 0, n == len(terms) - 1, early=n == 0 and len(terms) > 1)

    def iota(o, pattern, base, mult):
        c = 0.13 + 2 * size(o) * CY
        if SCRATCH[o[0]][2] != I:
            add("g", lambda: g.iota(R(o), pattern, base, mult, allow_small_or_imprecise_dtypes=True), [], [o], c)
        else:
            add("g", lambda: g.iota(R(o), pattern, base, mult), [], [o], c)

    def dma(eng, o, a, acc=False):
        qu = {"g": g, "s": g.scalar, "y": g.sync}[eng]
        x = o if o[0] in SCRATCH else a
        c = size(x) * (2 if narrow(x) else 4) * 128 / 600e3
        if acc:
            add(eng, lambda: qu.dma_start(R(o), R(a), accum_op=A.add), [a, o], [o], 2 * c, "d")
        else:
            add(eng, lambda: qu.dma_start(R(o), R(a)), [a], [o], c, "d")

    def again(how, o, a):
        if how == "S":
            act(o, a, AF.Copy)
        else:
            dma("y", o, a)

    def send(m, src, to):
        add("g", None, [src], [], OPT["RC"], "r", msg=m, src=R(src), to=to, spare=OPT["SPARE"].get(m[0], 0.0))

    def arrive(m):
        add("t", None, [], [ap("l_" + m[0])], 0.0, "a", msg=m)

    def turn(fwd, msgs, outs, plus=(), onto=None):
        z = bank()
        s1 = 16 if fwd else 112
        for a, b, lo in ((0, 160, 128 - s1), (160, 320, 64)):
            total(cols(z, a, b), *([(cols("Eb" if m == "k" else "E", lo, lo + 128), cols("l_" + m[0], a, b)) for m in msgs]
                                   + [(If, cols(n, a, b)) for n in plus]))
        if onto:
            tt(onto[0], cols(z, 0, VI), onto[1], A.add)
        for d in outs:
            act(d, cols(z, 0, VI), AF.Copy)

    If, Ib, Nf, Nb = cols("E", 0, 128), cols("Eb", 0, 128), ap("Nf"), ap("Nb")
    vis = lambda n: cols(n, PAD + V0, WP)
    whole = lambda n: cols(n, 0, WP + PAD)
    DT = cols("G", 0, 992)
    mc = lambda c: (MC[c[0]][0], MC[c[1]][1]) if isinstance(c, tuple) else MC[c]
    st = lambda n, c: cols(n, PAD + 16 * mc(c)[0], PAD + 16 * mc(c)[1])
    ch = lambda n, c: cols(n, 16 * mc(c)[0], 16 * mc(c)[1])
    bk = lambda n, c: cols(n, 0, CH[c][1] - CH[c][0])
    lst = lambda n, c, o=0: cols(n, o + mc(c)[0], o + mc(c)[1])
    two = lambda n, e, c: ap(n, e, slice(16 * mc(c)[0], 16 * mc(c)[1]))

    def run(key, c):
        h = c
        while h < VC and OPT[key][h + 1].islower():
            h += 1
        return c, h

    EOFF = (WP + PAD, PAD)
    ew = lambda e, c: cols("Ew", EOFF[e] + CH[c][0], EOFF[e] + CH[c][1])
    msk, sc, scl = cols("rk", 0, 992), cols("rk", 992, W), cols("rk", 999, W, 8)
    q_twice = lambda c: "V" in (OPT["T0"][c] + OPT["T1"][c]).upper()
    dv = lambda t, shot: "D1" if (shot, t) == (1, 1) else "DV"
    v_twice = lambda c, key="DV": OPT[key][c] in "vV"
    load = lambda t, c: OPT["PL" if t > 1 else "P1"][c]
    keeps = lambda t, shot, c: OPT[dv(t, shot)][c] == "P" and load(t, c) == "K"
    ups = lambda t, shot, c: OPT[dv(t, shot)][c] not in "vV" and not keeps(t, shot, c)
    signed = lambda s: If if s > 0 else Nf

    def opened(c):
        z = bk(bank(), c)
        mm(z, Ib, st("kA", c), True, False)
        return z

    def span(key, c, off=0, top=VC):
        if OPT[key][c] == "d":
            return None
        h = c
        while h < top and OPT[key][h + 1] == "d":
            h += 1
        return off + CH[c][0], off + CH[h][1]

    def both(r):
        cs = [c for c in range(VC + 1) if r[0] <= PAD + CH[c][0] < r[1] and q_twice(c)]
        return [("q",) + r] + ([("q'", PAD + CH[cs[0]][0], PAD + CH[cs[-1]][1])] if cs else [])

    fill(ap("cu"), 0)
    fill(ap("ones"), 1.0)
    for gi in range(8):
        a, y = gi // 2, gi % 2
        dma("y" if y else "s", app("ct", slice(32 * a, 32 * a + 32), y), ("con", (slice(8 * gi, 8 * gi + 8), ALL)))
    for gi in range(8):
        a, y = gi // 2, gi % 2
        dma("y" if y else "s", app("cu", slice(32 * a, 32 * a + 31), y), ("cur", (gi, ALL)))
    dma("y", cols("q0b", PAD, WP), ("q0", (ALL, ALL)))
    dma("y", ap("sg1"), ("q0", (ALL, ALL)))
    dma("y", ap("pr"), ("v0", (ALL, ALL)))
    dma("y", cols("kA", PAD, WP), ("kap", (ALL, ALL)))
    dma("y", ap("kV", 0), ("kap", (ALL, slice(V0, W))))
    dma("y", cols("kB", PAD, PAD + V0), ("kap", (ALL, slice(0, V0))))
    dma("y", app("aimA", slice(0, 8)), ("aim", (ALL, ALL)))
    iota(ap("iL"), [[-32, 4], [-1, 4], [-4, 8]], 0, 1)
    iota(ap("iG"), [[-16, 8]], 128, 1)
    iota(ap("iS"), [[1, 128]], 2048, -16)
    iota(ap("iO"), [[-1, 16]], 16, 1)
    iota(ap("iP"), [[0, 1]], 0, 1)
    iota(ap("i8"), [[16, 124]], 8, 0)
    for h in (0, 1):
        add("g", lambda h=h: g.affine_select(R(cols("E", 128 * h, 128 * h + 128)), R(ap("ones")), [[-1, 128]], A.is_equal, 0.0, 0, 1),
            [ap("ones")], [cols("E", 128 * h, 128 * h + 128)], 0.4)
    fill(cols("q0b", 0, PAD), 0.0)
    fill(ap("Wc"), 0.0)
    fill(ap("bias"), -8.5 * 16384)
    for n in ("vs", "vs'", "X", "Ew", "kA", "q", "kB"):
        fill(cols(n, 0, PAD), 0.0)
        fill(cols(n, WP, WP + PAD), 0.0)
    fill(cols("Ew", 2 * WP, 2 * WP + PAD), 0.0)
    ts(ap("L"), ap("iL"), 0.0, A.is_equal, 2048.0, A.mult)
    ts(ap("L1", ALL, slice(0, 7)), ap("iL", ALL, slice(0, 7)), 4.0, A.is_equal, -2049.0, A.mult)
    ts(ap("L1", ALL, 7), ap("iL", ALL, 7), -28.0, A.is_equal, -1.0, A.mult)
    tt(ap("L"), ap("L"), ap("L1"), A.add)
    ts(ap("L1", ALL, slice(0, 6)), ap("iL", ALL, slice(0, 6)), 8.0, A.is_equal)
    ts(ap("L1", ALL, 6), ap("iL", ALL, 6), -24.0, A.is_equal)
    ts(ap("iG"), ap("iG"), 4, A.arith_shift_right)
    ts(ap("iS"), ap("iS"), 4, A.arith_shift_right)
    tt(ap("L", ALL, slice(0, 7)), ap("L", ALL, slice(0, 7)), ap("L1", ALL, slice(0, 7)), A.add)
    ts(ap("Sel"), ap("iS"), 128.0, A.is_equal, -1.0, A.mult)
    for c in ORD:
        act(st("vs", c), ch("pr", c), AF.Copy, scale=0.0625)
        if v_twice(c):
            dma("y", st("vs'", c), st("vs", c))
    for k in (slice(0, 16), slice(16, 31)):
        for y in (0, 1):
            ts(ap("conf", k, slice(16 * y, 16 * y + 16)), ap("ct", y, k), 8.0, A.add)
    n0, n1 = bank(), bank()
    mm(cols(n0, 0, 512), ap("L"), ap("conf", slice(0, 16)))
    mm(cols(n1, 0, 480), ap("L"), ap("conf", slice(16, 31)))
    for y in (0, 1):
        cp(ap("cf", ALL, slice(16 * y, 16 * y + 16)), ap("cu", y))
    ts(ap("G8"), ap("iG"), 8.0, A.is_equal, 16384.0, A.mult)
    flip(ap("cf2"), ap("cf"))
    ts(ap("iP"), ap("iP"), 15, A.bitwise_and)
    for z in range(4):
        cp(cols("curB", z, 124, 4), ap("cf2", z, slice(0, 31)))

    def mask(src, e):
        for m in range(8):
            act(cols("rk", m, 992, 8), ap(src), AF.Abs, bias=-float(2 ** 24) * ((m - e) & 7), scale=float(2 ** 24))

    def scan():
        add("v", lambda: g.vector.tensor_tensor_scan(R(sc), R(msk), R(DT), 8.0e6, A.min, A.add), [msk, DT], [sc], 0.04 + 992 * CY)

    def unpack(jj, of):
        ts(cols(jj, 0, 124), cols("Pi", 0, 124), 11, A.arith_shift_right)
        ts(cols(jj, 124, 248), cols("Pi", 0, 124), 2047, A.bitwise_and)
        ts(cols(of, 0, 124), cols(jj, 0, 124), -2048.0, A.add)
        ts(cols(of, 124, 248), cols(jj, 124, 248), -1.0, A.mult, 2048.0, A.add)

    mask("curB", 0)
    flip(ap("conf", slice(0, 16)), cols(n0, 0, 512))
    cp(ap("pcol"), ap("iP"))
    ts(ap("iO"), ap("iO"), 15, A.bitwise_and)
    flip(ap("conf", slice(16, 31)), cols(n1, 0, 480))
    ts(ap("i8"), ap("i8"), ap("pcol"), A.add)
    for qq in range(4):
        o, a = cols("G", 248 * qq, 248 * qq + 248), ap("conf", ALL, slice(8 * qq, 8 * qq + 8))
        if qq % 2:
            act(o, a, AF.Copy)
        else:
            cp(o, a)
    ts(ap("oh"), ap("iO"), 0.0, A.is_equal)
    ts(cols("G", 7, 992, 8), cols("G", 7, 992, 8), BASE, A.add)
    scan()
    cp(cols("Pi", 0, 124), scl)
    for l in range(16):
        act(ap("Wc", l, slice(l, 128, 16)), ap("G8"), AF.Copy)
    act(ap("Eb"), ap("E"), AF.Copy)
    act(Nf, If, AF.Copy, scale=-1.0)
    act(Nb, If, AF.Copy, scale=-1.0)
    act(ap("N2"), If, AF.Copy, scale=2.0)
    act(ap("BP"), If, AF.Copy, scale=float(2 ** 63))
    act(ap("BN"), ap("BP"), AF.Copy, scale=-float(2 ** 63))
    act(ap("BP"), ap("BP"), AF.Copy, scale=float(2 ** 63))
    unpack("JJ", "of")
    act(ap("Ic"), If, AF.Copy, scale=WP / 2)
    act(ap("i8b"), ap("i8"), AF.Identity, bias=WP / 2)
    for (a, b), c in zip(MC, CENTER):
        act(cols("tgt", a, b), cols("i8", a, b), AF.Identity, bias=16.0 * 16384 * c, scale=-16384.0)

    def speeds(t, shot, c):
        nv, key = ch("nv%d" % t, c), dv(t, shot)
        if OPT[key][c] == "P":
            z, s = bk(bank(), c), 1 if ups(t, shot, c) else -1
            mm(z, signed(s), st("vs", c), True, False)
            act(nv, ind(whole("vs"), lst("j%d" % t, c)), AF.Copy)
            mm(z, signed(-s), nv, False, True)
            act(nv, z, AF.Copy)
            if keeps(t, shot, c):
                held[t, c] = z
        elif OPT[key][c] == "D":
            c = run(key, c)
            act(ch("nv%d" % t, c), ind(whole("vs"), lst("j%d" % t, c)), AF.Copy, scale=-1.0)
            dma("g", ch("nv%d" % t, c), st("vs", c), True)
        elif OPT[key][c] == "V":
            c = run(key, c)
            tt(ch("nv%d" % t, c), ind(whole("vs"), lst("j%d" % t, c)), st("vs'", c), A.subtract)

    def tests(t):
        qn = "q0b" if t == 1 else "q"
        jj, of = ("JJ2", "of2") if t == 2 else ("JJ", "of")
        win = cols(qn, 0, WP)
        for a, b in OPT["HALF"]:
            cnt = []
            lead[0], at[0] = OPT["FIRST"] * ((a, b) == OPT["HALF"][0]), (a, b)
            for e in (0, 1):
                key, made = "FT"[t > 1] + str(e), []
                for c in [c for c in ORD if a <= MC[c][0] < b]:
                    how, r = OPT[key][c], run(key, c)
                    got, d, s = ind(win, lst(of, r, 124 * e)), two("D", e, c), -NEAR if how in "vV" else NEAR
                    if how == "V":
                        tt(two("D", e, r), got, ch("sg1", r) if t == 1 else st("q'", r), A.subtract)
                    elif how == "D":
                        act(two("D", e, r), got, AF.Copy, scale=-1.0)
                        dma("g", two("D", e, r), st("q", r), True)
                    elif how == "P":
                        x = two("ind", e, c) if t == 1 else d
                        d = bk(bank(), c)
                        mm(d, Ib if t == 1 else If, st(qn, c), True, False)
                        act(x, got, AF.Copy)
                        mm(d, Nb if t == 1 else Nf, x, False, True)
                    made.append((c, d, s))
                for c, d, s in made:
                    if OPT["E%d" % e][c] == "S":
                        act(ew(e, c), d, AF.Copy, scale=s)
                    else:
                        ts(ew(e, c), d, s, A.mult)
                    ts(two("ind", e, c), ew(e, c), GRID, A.add, GRID, A.is_equal)
                z = cols(bank(), a, b)
                cnt.append(z)
                lanes(z, (Ib, cols("bias", a, b)), lambda l: ap("ind", e, slice(16 * a + l, 16 * b, 16)), [])
            m = cnt[1]
            first = len(ops)
            tt(cols("A", a, b), cnt[0], cols(jj, a, b), A.min)
            tt(m, m, cols(jj, 124 + a, 124 + b), A.min)
            tt(m, m, cols("A", a, b), A.max)
            act(cols("cw", a, b), m, AF.Abs, bias=-2048.0)
            ts(cols("j%d" % t, a, b), cols("cw", a, b), float(WP), A.min)
            haste(first)
            act(cols("lvl", a, b), m, AF.Sign, bias=-2048.0)
            if t > 1:
                z = cols(bank(), a, b)
                group([(z, If, cols("i8b", a, b)), (z, ap("Ic"), cols("lvl", a, b))])
                cp(cols("so", a, b), z)

    def mutual(t, shot):
        j, kn, once = "j%d" % t, "kA" if t <= 2 else "kB", t == 1
        for (lo, hi), nxv in OPT["SPREAD"]:
            at[0] = (lo, hi)
            for b in range(16):
                o = cols("X", PAD + 16 * lo + b, PAD + 16 * hi, 16)
                if b < nxv:
                    ts(o, cols("cw", lo, hi), cols("oh", b, b + 1), A.mult)
                else:
                    act(o, cols("cw", lo, hi), AF.Copy, scale=cols("oh", b, b + 1))

        def signs(c):
            key = "G1" if t == 1 else "PR"
            r = run(key, c)
            got = ind(ap("Ew"), lst("so", r))
            if OPT[key][c] == "S":
                act(ch("sg1" if t == 1 else "pr", r), got, AF.Sign)
            elif OPT[key][c] == "V":
                tt(ch("pr", r), got, ch("nv%d" % t, r), A.mult)

        def hits(c):
            n = two("ind", 0, c)
            if OPT["PR"][c] in "sS":
                z = bk(bank(), c)
                mm(z, Ib, ch("pr", c), early=True)
                tt(ch("pr", c), z, ch("nv%d" % t, c), A.mult)
            if OPT["NS"][c] == "S":
                act(n, ch("pr", c), AF.Sign, scale=-1.0 if ups(t, shot, c) else 1.0)
            else:
                ts(n, ch("pr", c), 0.0, A.is_lt if ups(t, shot, c) else A.is_gt)
            if OPT["KK"][c] in "sS":
                return
            z = bk(bank(), c)
            group([(z, Ib, st(kn, c)), (z, Ib, n)])
            if OPT["KM"][c] == "S":
                act(two("ind", 1, c), z, AF.Relu, bias=-1.0)
            else:
                ts(two("ind", 1, c), z, -1.0, A.add, 0.0, A.max)

        for (a, b), then in zip(OPT["BACK"], OPT["THEN"]):
            for c in [c for c in ORD if a <= MC[c][0] < b]:
                at[0] = c
                if OPT["MG"][c] == "S":
                    act(ch("mg", c), ind(ap("X"), lst(j, c)), AF.Identity, bias=-float(CENTER[c]))
                else:
                    ts(ch("mg", c), ind(ap("X"), lst(j, c)), -float(CENTER[c]), A.add)
            z = cols(bank(), a, b)
            lanes(z, (If, cols("tgt", a, b)), lambda l: cols("mg", 16 * a + l, 16 * b, 16),
                  [(ap("Ic"), cols("lvl", a, b)), (If, cols("i8b", a, b))] if once else [(If, cols("cw", a, b))])
            ts(cols("so" if once else "sk", a, b), z, 0.0, A.max, float(WP + once * WP), A.min)
            haste(len(ops) - 2)
            if t < 4:
                act(cols("ab", a, b), z, AF.Abs, bias=-999.5 - once * WP)
            for c in then:
                at[0] = c
                speeds(t, shot, c)
        for c in chunks():
            signs(c)
        for c in chunks() if t > 1 else ():
            hits(c)
        for c in chunks():
            key = "K1" if t == 1 else "KK"
            r = run(key, c)
            got = ind(ap(kn), lst("j1" if once else "sk", r))
            if t == 1 and OPT[key][c] == "V":
                tt(ch("kk01", r), got, ap("kV", 0) if c == VC else st("kB", r), A.mult)
            elif OPT[key][c] == "V":
                tt(ch("kk%d" % t, r), got, two("ind", 1, r), A.mult)
            elif OPT[key][c] == "S":
                act(two("ind", 1, r), got, AF.Copy)

    def cursor(t):
        if t == 4:
            return
        z = bank()
        act(ap("mu"), ap("ab"), AF.Sign, bias=992.25, scale=-1.0)
        y = cols(z, 372, 496)
        if t == 1:
            act(cols(z, 0, 124), ap("mu"), AF.Relu)
        else:
            group([(y, Ib, ap("mu")), (y, Ib, ap("lvl"))])
            for n in range(3 if t == 2 else 1):
                act(cols(z, 124 * n, 124 * n + 124), y, AF.Relu, bias=-1.0)
        if t == 1:
            tt(cols(z, 0, 124), ap("curB"), cols(z, 0, 124), A.subtract)
            ts(ap("ci"), cols(z, 0, 124), 2.0, A.add)
            ts(ap("ci"), ap("ci"), 7, A.bitwise_and)
            cp(ap("c2"), ap("ci"))
            mask("c2", 0)
            scan()
            cp(cols("Pi", 0, 124), scl)
            mask("c2", 2)
            unpack("JJ2", "of2")
            scan()
            act(cols("TA", 0, 124), scl, AF.Copy)
            mask("c2", 4)
            scan()
            act(cols("TA", 124, 248), scl, AF.Copy)
            tables()
        elif t == 2:
            tt(cols(z, 0, 372), cols(z, 0, 372), ap("TB"), A.mult)
            tt(cols("Pi", 0, 124), cols(z, 0, 124), cols("TA", 0, 124), A.add)
            tt(ap("UV"), cols(z, 124, 372), cols("TA", 124, 372), A.add)
            unpack("JJ", "of")
        else:
            tt(cols(z, 0, 124), cols(z, 0, 124), cols("UV", 124, 248), A.mult)
            tt(cols("Pi", 0, 124), cols(z, 0, 124), cols("UV", 0, 124), A.add)
            unpack("JJ", "of")

    def tables():
        z = bank()
        cp(ap("Pi"), cols("TA", 0, 248))
        ts(cols(z, 0, 124), cols("JJ2", 124, 248), -2048.0, A.mult, float(2 ** 23 + 4096), A.add)
        ts(ap("Ph"), ap("Pi"), 11, A.arith_shift_right)
        ts(cols("Pi", 0, 124), cols("Pi", 0, 124), 2047, A.bitwise_and)
        ts(cols(z, 124, 248), cols("Pi", 0, 124), -2048.0, A.mult, float(2 ** 23 + 4096), A.add)
        tt(cols(z, 0, 248), cols(z, 0, 248), ap("Ph"), A.subtract)
        tt(cols("TB", 0, 248), cols(z, 0, 248), cols("TA", 0, 248), A.subtract)
        tt(cols(z, 248, 372), cols("TA", 0, 124), cols(z, 124, 248), A.subtract)
        act(cols("TA", 248, 372), cols("TB", 124, 248), AF.Copy)
        tt(cols("TB", 248, 372), cols(z, 248, 372), cols("TB", 124, 248), A.subtract)

    def update(t, shot, c):
        kk, nv, kn = ch("kk%d" % t, c), ch("nv%d" % t, c), "kA" if t <= 2 else "kB"
        up = ups(t, shot, c)
        how, key = load(t, c), "V1" if t == 1 else "V4" if t == 4 else "VU"
        by = "V" if (t, c) == (2, VC) else OPT[key][c].upper()
        s, z = -1 if up else 1, None
        if t == 1:
            z, other, op = bk(bank(), c), ch("kk01", c), A.min
            mm(z, ap("BN" if up else "BP"), ch("sg1", c), early=True)
            tt(z, z, nv, A.mult)
            act(z, z, AF.Relu)
        elif OPT["KK"][c] in "sS":
            z, other, op = bk(bank(), c), st(kn, c), A.mult
            group([(z, Ib, two("ind", 0, c)), (z, Ib, two("ind", 1, c))])
            act(z, z, AF.Relu, bias=-1.0)
        zo = opened(c) if by == "O" else None
        gain = lambda z: zo or z
        if z is not None and how == "I":
            tt(z, z, other, op)
            act(kk, z, AF.Copy)
            tt(gain(z), z, nv, A.mult)
        else:
            if z is not None:
                tt(kk, z, other, op)
            z = held.pop((t, c), None)
            if z is None:
                z = bk(bank(), c)
                if how == "S":
                    act(z, nv, AF.Copy, scale=float(s), early=True)
                else:
                    mm(z, signed(s), nv, early=True)
            s = 1
            tt(gain(z), z, kk, A.mult)
        old = (Ib, st("q0b", c)) if t == 1 else (If, st("q", c))
        aim = (app("Sel", slice(0, 8)), app("aimA", slice(0, 8), slice(*CH[c])))
        if by == "O" and t == 4:
            assert s > 0
            for n, (l, r) in enumerate([(If, st("vs", c)), old, aim]):
                mm(zo, l, r, False, n == 2)
            act(st("q", c), zo, AF.Copy)
            if c == VC:
                send("a%d" % shot, vis("q"), prv)
            return
        if t == 4 and OPT["AQ"][c] == "O":
            zo = opened(c)
            if s < 0:
                tt(zo, st("vs", c), z, A.subtract)
            else:
                tt(zo, z, st("vs", c), A.add)
            for n, (l, r) in enumerate([old, aim]):
                mm(zo, l, r, False, n == 1)
            act(st("q", c), zo, AF.Copy)
            if c == VC:
                send("a%d" % shot, vis("q"), prv)
            return
        if by == "O":
            mm(zo, signed(s), st("vs", c), False, True)
            act(st("vs", c), zo, AF.Copy, scale=float(s))
        elif s < 0:
            tt(st("vs", c), st("vs", c), z, A.subtract)
        else:
            tt(st("vs", c), z, st("vs", c), A.add)
        if t == 2 and c == VC:
            send("v%d" % shot, vis("vs"), nxt)
            return
        if t < 4 and v_twice(c):
            dma("y", st("vs'", c), st("vs", c))
        key = "Q" if t > 1 else "Q1"
        if t == 4:
            z = bk(bank(), c)
            if OPT["AQ"][c] == "P":
                total(z, old, (If, st("vs", c)), aim)
                act(st("q", c), z, AF.Copy)
            else:
                mm(z, *old, early=True)
                tt(st("q'", c), z, st("vs", c), A.add)
                z = bk(bank(), c)
                mm(z, *aim, early=True)
                tt(st("q", c), z, st("q'", c), A.add)
            if c == VC:
                send("a%d" % shot, vis("q"), prv)
            return
        how = OPT[key][c]
        if how in "dD":
            r = span(key, c, PAD, VC - (t == 2))
            if r:
                for n, a, b in both(r):
                    dma("g", cols(n, a, b), cols("vs", a, b), True)
            if t == 1 and r and r[1] == WP:
                send("q%d" % shot, vis("q"), nxt)
            return
        else:
            z = zo if (how, by, s) == ("V", "O", 1) and t > 1 else bk(bank(), c)
            if how == "P":
                total(z, old, (If, st("vs", c)))
                act(st("q", c), z, AF.Copy)
            elif z is zo:
                tt(st("q", c), z, st("q", c), A.add)
            else:
                mm(z, *old, early=True)
                tt(st("q", c), z, st("vs", c), A.add)
            if q_twice(c):
                if OPT["Q2"][c] == "S" and how == "P":
                    act(st("q'", c), z, AF.Copy)
                else:
                    again(OPT["Q2"][c], st("q'", c), st("q", c))
        if t == 1 and c == VC:
            send("q%d" % shot, vis("q"), nxt)

    def q_start():
        for c in ORD:
            if OPT["Q1"][c] == "D":
                for n, a, b in both(span("Q1", c, PAD)):
                    dma("g", cols(n, a, b), ("q0", (ALL, slice(a - PAD, b - PAD))))

    def inverse(after):
        for c in ORD:
            act(ch("rk", c), st("kA", c), AF.Ln, more=1.3 * (c == ORD[0]), after=after)
            after = len(ops) - 1
        for c in ORD:
            act(ch("rk", c), ch("rk", c), AF.Exp, scale=-1.0, more=1.5 * (c == ORD[0]), after=after)

    def newton(cs, after):
        for c in cs:
            z = bk(bank(), c)
            mm(z, Nb, st("kA", c))
            ops[-1]["after"] = after
            if OPT["NW"][c] == "O":
                act(st("X", c), ch("rk", c), AF.Square)
                zo = opened(c)
                tt(zo, z, st("X", c), A.mult)
                mm(zo, ap("N2"), ch("rk", c), False, True)
                act(ch("rk", c), zo, AF.Copy)
                continue
            tt(z, z, ch("rk", c), A.mult)
            act(z, z, AF.Identity, bias=2.0)
            tt(ch("rk", c), z, ch("rk", c), A.mult)

    def squares(after):
        for c in ORD:
            o = ap("Gh") if c == VC else ch("nv4", c)
            act(o, st("kA", c), AF.Square, after=after)

    AV = {4: ("q", "vs'"), 3: ("vs'", "vs"), 2: ("vs", "vs'"), 1: ("vs'", None)}

    plus = lambda t, shot, c: not ups(t, shot, c)

    def product(t, shot, c):
        av, kk, d, up = AV[t][0], ch("kk%d" % t, c), two("D", 0, c), plus(t, shot, c)
        got = ind(whole(av), lst("j%d" % t, c))
        x, key = None, "DA%d" % t if t > 1 else "A%d" % shot
        if OPT[key][c] in "OP":
            if OPT[key][c] == "O":
                x = opened(c)
                act(x, st(av, c), AF.Copy, scale=1.0 if up else -1.0)
            else:
                x = bk(bank(), c)
                mm(x, If if up else Nf, st(av, c), True, False, "fresh")
            act(d, got, AF.Copy)
            mm(x, Nf if up else If, d, False, True)
            return x
        if OPT[key][c] in "vV":
            act(st("q'", c), st(av, c), AF.Copy)
        r = run(key, c)
        got = ind(whole(av), lst("j%d" % t, r))
        if OPT[key][c] == "V":
            tt(two("D", 0, r), got, st("q'", r), A.subtract)
        elif OPT[key][c] == "D":
            act(two("D", 0, r), got, AF.Copy, scale=-1.0)
            dma("g", two("D", 0, r), st(av, r), True)

    def backward(t, shot, c, x):
        av, new = AV[t]
        kk, nv = ch("kk%d" % t, c), ch("nv%d" % t, c)
        last, bb = shot == 1 and t == 1, "BB%d" % t
        d = two("D", 0, c)
        ys = lambda a, b: ap("D", 1, slice(a, b)) if t == 1 else cols("nv%d" % t, a, b)
        y = ys(*CH[c])
        if x is not None:
            tt(x, x, kk, A.mult)
        else:
            r = 1 if plus(t, shot, c) != (OPT["DA%d" % t if t > 1 else "A%d" % shot][c] in "vV") else -1
            x = bk(bank(), c)
            if OPT["KL" if t > 1 else "KM%d" % shot][c] == "S":
                act(x, kk, AF.Copy, scale=float(r), early=True)
            else:
                mm(x, signed(r), kk, early=True)
            tt(x, x, d, A.mult)

        def gains():
            if last:
                z = opened(c) if OPT["U"][c] == "O" else bk(bank(), c)
                if OPT["U"][c] == "O":
                    tt(z, x, nv, A.mult)
                    mm(z, If, ch("G", c), False, True)
                elif OPT["U"][c] == "P":
                    tt(y, x, nv, A.mult)
                    total(z, (If, ch("G", c)), (If, y))
                else:
                    tt(z, x, nv, A.mult)
                    tt(z, z, ch("G", c), A.add)
                tt(y, z, ch("rk", c), A.mult)
                dma("y", ("yg", (ALL, slice(*CH[c]))), y)
            elif (shot, t) == (0, 4):
                tt(ch("G", c), x, nv, A.mult)
            elif (shot, t, c) == (1, 3, VC):
                tt(y, x, nv, A.mult)
                dma("g", ch("G", c), y, True)
                send("G", ch("G", c), prv)
            else:
                tt(y, x, nv, A.mult)
                apart = t <= 2 or (shot, t) == (1, 3)
                if c == VC and apart:
                    dma("g", ap("Gh"), y, True)
                elif span("GG", c):
                    r = span("GG", c, 0, VC - apart)
                    dma("g", cols("G", *r), ys(*r), True)

        def less(o):
            if plus(t, shot, c):
                tt(o, st(av, c), x, A.subtract)
            else:
                tt(o, x, st(av, c), A.add)

        if t == 3 and c == VC:
            less(st(new, c))
            send("w%d" % shot, st(new, c), prv)
            gains()
        elif t > 1 and OPT[bb][c] == "O":
            z = opened(c)
            less(z)
            mm(z, If, st("q", c), False, True)
            act(st(new, c), z, AF.Copy)
            gains()
        elif t > 1 and OPT[bb][c] == "Q":
            z = opened(c)
            act(z, x, AF.Copy, scale=-1.0 if plus(t, shot, c) else 1.0)
            mm(z, If, st(av, c), False, False)
            mm(z, If, st("q", c), False, True)
            act(st(new, c), z, AF.Copy)
            gains()
        elif t > 1 and OPT[bb][c] in "dD":
            less(st(new, c))
            r = span(bb, c, PAD, VC - (t == 3))
            if r:
                dma("g", cols(new, *r), cols("q", *r), True)
            gains()
        else:
            if t == 1 and OPT["L%d" % shot][c] == "Q":
                z = opened(c)
                act(z, x, AF.Copy, scale=-1.0 if plus(t, shot, c) else 1.0)
                mm(z, If, st(av, c), False, True)
                gains()
            elif OPT["YA" if t > 1 else "Y%d" % shot][c] == "I":
                gains()
                z = x
                less(z)
            else:
                z = bk(bank(), c)
                less(z)
                gains()
            if t > 1:
                tt(st(new, c), z, st("q", c), A.add)
            else:
                how = OPT["C%d" % shot][c]
                if how in "dD":
                    ts(z, z, -3.0, A.max, 3.0, A.min)
                    act(d, z, AF.Copy, scale=-0.0625)
                    if how == "D":
                        r = span("C1", c)
                        add("g", lambda: g.dma_start(T.yv[:, r[0]:r[1]], R(ap("D", 0, slice(*r))), accum_op=A.add),
                            [ap("D", 0, slice(*r)), ap("ones")], [], (r[1] - r[0]) * 1024 / 600e3, "d")
                    return
                s = -1.0 if how == "O" else 1.0
                if how == "O":
                    zo = opened(c)
                    ts(zo, z, -3.0, A.max, 3.0, A.min)
                    z = zo
                    mm(z, Nf, ch("v0f", c), False, True)
                else:
                    ts(z, z, -3.0, A.max, 3.0, A.min)
                    tt(ch("v0f", c), ch("v0f", c), z, A.subtract)
                    z = ch("v0f", c)
                if shot:
                    act(ch("v0f", c), z, AF.Copy, scale=0.0625 * s)
                    dma("s", ("yv", (ALL, slice(*CH[c]))), ch("v0f", c))
                else:
                    for n in ("vs", "vs'")[:1 + v_twice(c, "D1")]:
                        act(st(n, c), z, AF.Copy, scale=2.0 ** -8 * s)
                    if how == "O":
                        act(ch("v0f", c), z, AF.Copy, scale=s)

    send("k", ap("kV", 0), nxt)
    for shot in (0, 1):
        q_start()
        for t in (1, 2, 3, 4):
            first = len(ops)
            step[0] += 1
            if shot == 1 and t == 1:
                for c in chunks():
                    speeds(1, 1, c)
            else:
                tests(t)
                mutual(t, shot)
            gate(first)
            for c in chunks():
                update(t, shot, c)
                if c == OPT["CUR"] and (shot, t) != (1, 1):
                    cursor(t)
                if c == OPT["INV"][2]:
                    mark[1] = len(ops) - 1
            mark[0] = len(ops) - 1
            if (shot, t) == OPT["INV"][:2]:
                inverse(mark[1])
            if (shot, t) == (0, 1):
                arrive("k")
                turn(True, ["k"], [vis("kB")])
            if t == 2:
                arrive("q%d" % shot)
                turn(True, ["q"], [vis("q")])
                arrive("v%d" % shot)
                turn(True, ["v"], [vis("vs")], onto=(vis("q"), vis("q")))
                if q_twice(VC):
                    act(vis("q'"), vis("q"), AF.Copy)
                if v_twice(VC):
                    dma("y", vis("vs'"), vis("vs"))
        for t in (4, 3, 2, 1):
            if (shot, t) == (1, 1):
                arrive("G")
                turn(False, ["G"], [ch("G", VC)], ["Gh"])
            first = len(ops)
            step[0] += 1
            x = {c: product(t, shot, c) for c in chunks()}
            gate(first)
            for c in chunks():
                backward(t, shot, c, x[c])
            if (shot, t) == (0, 4):
                dma("y", ap("mg"), ("v0", (ALL, ALL)))
                for c in ORD:
                    act(ch("v0f", c), ch("mg", c), AF.Copy, scale=16.0)
                squares(mark[0])
            if (shot, t) == (1, 4):
                for c in [c for c in ORD if OPT["C1"][c] in "dD"]:
                    act(ch("v0f", c), ch("v0f", c), AF.Copy, scale=0.0625, after=mark[0])
                    add("y", lambda c=c: g.sync.dma_start(T.yv[:, CH[c][0]:CH[c][1]], R(ch("v0f", c))), [ch("v0f", c)],
                        [cols("ones", 4 * c, 4 * c + 4)], 0.4, "d")
            if (shot, t) == (0, OPT["SQ"]):
                dma("g", cols("G", 0, V0), cols("nv4", 0, V0), True)
            if t == 4:
                arrive("a%d" % shot)
                turn(False, ["a"], [vis("q")])
            if t == 3:
                newton(OPT["NEW"][shot], max(n for n, o in enumerate(ops) if o["kind"] == "r" and o["msg"][0] == "w"))
                arrive("w%d" % shot)
                turn(False, ["w"], [], onto=(vis("vs"), vis("q")))
    return ops


BITS = {}


def region(x):
    key = ("#" if psum(x) else x[0], repr(x[1]))
    if key not in BITS:
        p, n = range(128)[x[1][0]], flat(x[0]).size
        m = np.zeros((4, n), np.uint8)
        m[p[0] // 32:p[-1] // 32 + 1, flat(x[0])[x[1][1:]].ravel()] = 1
        BITS[key] = int.from_bytes(np.packbits(m.ravel()).tobytes(), "big")
    return BITS[key]


def needs(ops, name, banks):
    wr, rd, last = {}, {}, {}
    who = lambda m: ops[m]["eng"] if ops[m]["kind"] == "c" else "x%d" % m
    out = []
    for n, o in enumerate(ops):
        deps, me = set(), who(n)
        R = [(name(x), region(x)) for x in o["rd"]]
        Wr = [(name(x), region(x)) for x in o["wr"]]
        for k, b in R + Wr:
            if k not in wr:
                wr[k], rd[k], last[k] = {}, {}, {}
            deps.update(m for m, x in wr[k].items() if x & b)
        for k, b in Wr:
            deps.update(m for m, x in rd[k].items() if x & b)
            rd[k] = {m: x & ~b for m, x in rd[k].items() if x & ~b}
        for k, _ in R + Wr:
            if psum((k,)):
                deps.update(m for e, m in last[k].items() if (e != me if banks else e == me == "t"))
                last[k][me] = n
        for k, b in R:
            rd[k][n] = rd[k].get(n, 0) | b
        for k, b in Wr:
            wr[k] = {m: x & ~b for m, x in wr[k].items() if x & ~b}
            wr[k][n] = wr[k].get(n, 0) | b
        deps.discard(n)
        out.append(deps)
    return out


def arrange(ops):
    deps = needs(ops, lambda x: x[0], False)
    sent = {o["msg"]: n for n, o in enumerate(ops) if o["kind"] == "r"}
    for n, o in enumerate(ops):
        if o["kind"] == "a":
            deps[n] = deps[n] | {sent[o["msg"]]}
        if "after" in o:
            deps[n] = deps[n] | {o["after"]}
    issue = lambda o: o["cost"] if o["kind"] == "c" else 0.0 if o["kind"] == "a" else OPT["GI"] * o["slow"] if o["eng"] == "g" else 0.06
    delay = lambda o: {"c": 0.0, "a": 0.0, "d": OPT["GD"], "r": OPT["RD"]}[o["kind"]] * o["slow"]
    hop = lambda a, b: (0.0 if a["eng"] == b["eng"] == "t" and a["kind"] == "c" else OPT["HOP"] * a["lag"]) + a.get("spare", 0.0) * (b["kind"] == "a")
    kids = [[] for _ in ops]
    for n, d in enumerate(deps):
        for m in d:
            kids[m].append(n)
    names = [sorted(set(x[0] for x in o["rd"] + o["wr"] if psum(x))) for o in ops]
    left, users = {}, {}
    for n, ns in enumerate(names):
        for k in ns:
            left[k] = left.get(k, 0) + 1
            users.setdefault(k, []).append(n)
    for n, o in enumerate(ops):
        if o.get("early") is True:
            us = users[names[n][0]]
            for d in deps[us[us.index(n) + 1]] - {n}:
                for m in deps[d] - deps[n]:
                    deps[n].add(m)
                    kids[m].append(n)
    cases = [[dict(o, cost=o["cost"] * (ga if o["gather"] else pe if o["eng"] == "t" else slow if o["kind"] != "c" else 1.0),
                   lag=lag, slow=slow) for o in ops] for ga, pe, lag, slow in OPT["CASES"]]
    rules = []
    for patience in OPT["WAIT"]:
        chain = [-2.0 * n for n in range(len(ops))]
        for _ in range(OPT["PASS"]):
            end = forwards(cases[0], deps, kids, names, left, chain, issue, delay, hop, patience)[5]
            chain = [x + o["lead"] for x, o in zip(backwards(cases[0], deps, kids, end, issue, delay, hop), ops)]
            rules.append((chain, patience))

    def replay(case, seq, place, was):
        clock, pipe, used, end = dict(was[0]), dict(was[1]), {b: dict(x) for b, x in was[2].items()}, was[3][:]
        for n in seq:
            o = case[n]
            e, t = o["eng"], clock[o["eng"]]
            for m, h in o["from"]:
                if end[m] + h > t:
                    t = end[m] + h
            for k in names[n]:
                for f, x in used[place[k]].items():
                    if f != e and x + o["wake"] > t:
                        t = x + o["wake"]
            if o["kind"] == "c":
                end[n] = clock[e] = t + o["cost"]
            elif o["kind"] == "a":
                end[n] = t
            else:
                clock[e] = t + issue(o)
                pipe[o["kind"]] = max(clock[e] + delay(o) / 2, pipe[o["kind"]]) + o["cost"]
                end[n] = pipe[o["kind"]] + delay(o) / 2
            for k in names[n]:
                used[place[k]][e] = end[n]
        return clock, pipe, used, end

    for case in cases:
        for n, o in enumerate(case):
            o.update({"from": [(m, hop(case[m], o)) for m in deps[n]], "wake": OPT["HOP"] * o["lag"]})
    was = [({e: 0.0 for e in ENG}, {"d": 0.0, "r": 0.0}, {b: {} for b in BANKS}, [0.0] * len(ops)) for _ in cases]
    state, dice = None, np.random.default_rng(OPT["SEED"])
    gates = [n for n, o in enumerate(ops) if "gate" in o] + [None] * (1 + OPT["AHEAD"])
    kin = [lambda o: o["tag"], lambda o: o["tag"][:2], lambda o: o["tag"][2], lambda o: (o["tag"][0], o["tag"][2])]
    best = None
    for gate, far in zip(gates, gates[OPT["AHEAD"]:]):
        some, best, done, unit = rules + ([best[2:]] if best else []), None, len(state[9]) if state else 0, None
        for turn in range(len(some) + OPT["TRIES"]):
            if turn < len(some):
                chain, patience = some[turn]
            else:
                chain, patience = list(best[2]), best[3]
                for _ in range(1 + turn % 2):
                    like, n, x = kin[dice.integers(4)], best[1][dice.integers(done, len(best[1]))], float(dice.normal()) * OPT["SHAKE"]
                    for m in best[1][done:]:
                        if like(ops[m]) == like(ops[n]):
                            chain[m] += x
            s = forwards(cases[0], deps, kids, names, left, chain, issue, delay, hop, patience, state, far)
            if s is None:
                continue
            owed = [] if far is None else [n for n in set(range(far)) - set(s[9]) if ops[n]["eng"] == "v"]
            late = []
            for case, w in zip(cases, was):
                x = replay(case, s[9][done:], s[0], w)[3]
                late.append(max(x if far is None else [x[m] for m in deps[far]]) + OPT["OWE"] * sum(case[n]["cost"] for n in owed)
                            - max(w[0].values()))
                if best and len(late) == 2 and sum(late) > 1.004 * sum(each[:2]):
                    break
            else:
                unit = unit or late
                mean = sum(a * x / b for a, b, x in zip(late, unit, OPT["WEIGHT"])) + OPT["WORST"] * max(a / b for a, b in zip(late, unit))
                if best is None or mean <= best[0]:
                    best, each = (mean, s[9], chain, patience), late
        state = forwards(cases[0], deps, kids, names, left, best[2], issue, delay, hop, best[3], state, gate)
        was = [replay(case, state[9][done:], state[0], w) for case, w in zip(cases, was)]
    return state[9], state[0]


def backwards(ops, deps, kids, end, issue, delay, hop):
    clock = {e: 0.0 for e in ENG}
    can, wait, lead = [0.0] * len(ops), [len(k) for k in kids], [0.0] * len(ops)
    ready = {e: [] for e in ENG}
    for n, o in enumerate(ops):
        if not wait[n]:
            can[n] = 0.0 if o["kind"] == "c" else o["cost"] + delay(o)
            ready[o["eng"]].append(n)
    for _ in ops:
        now, e = min((max(clock[e], min(can[n] for n in r)), e) for e, r in ready.items() if r)
        n = max([n for n in ready[e] if can[n] <= now + 0.05], key=lambda n: end[n])
        ready[e].remove(n)
        lead[n] = max(can[n], clock[e]) + issue(ops[n])
        if ops[n]["kind"] != "a":
            clock[e] = lead[n]
        for m in deps[n]:
            o = ops[m]
            can[m] = max(can[m], lead[n] + hop(o, ops[n]) + (0.0 if o["kind"] == "c" else o["cost"] + delay(o)))
            wait[m] -= 1
            if not wait[m]:
                ready[o["eng"]].append(m)
    return lead


def forwards(ops, deps, kids, names, left, chain, issue, delay, hop, patience, state=None, until=None):
    if state is None:
        state = ({}, {b: 0.0 for b in BANKS}, {b: {} for b in BANKS}, {e: 0.0 for e in ENG}, {"d": 0.0, "r": 0.0}, [0.0] * len(ops),
                 [len(d) for d in deps], [0.0] * len(ops), {e: [n for n, o in enumerate(ops) if o["eng"] == e and not deps[n]] for e in ENG}, [], left)
    place, free, used, clock, pipe, end, wait, can, ready, out, left = state
    place, free, clock, pipe, left = dict(place), dict(free), dict(clock), dict(pipe), dict(left)
    used, ready = {b: dict(x) for b, x in used.items()}, {e: list(x) for e, x in ready.items()}
    end, wait, can, out = list(end), list(wait), list(can), list(out)

    def start(n):
        o, t = ops[n], can[n]
        new = [k for k in names[n] if k not in place]
        if new:
            if len(free) < len(new):
                return None
            t = max(t, sorted(free.values())[len(new) - 1] + OPT["HOP"] * o["lag"])
        for k in names[n]:
            if k in place:
                t = max([t] + [x + OPT["HOP"] * o["lag"] for e, x in used[place[k]].items() if e != o["eng"]])
        return t

    while len(out) < len(ops) and (until is None or wait[until]):
        cand = {e: [(t, n) for n in ready[e] for t in [start(n)] if t is not None] for e in ENG}
        when = [(max(clock[e], min(c)[0]), e) for e, c in cand.items() if c]
        if not when:
            return None
        now, e = min(when)
        t, n = max([x for x in cand[e] if x[0] <= now + 0.05], key=lambda x: chain[x[1]])
        soon = [x for x in cand[e] if x[0] < now + patience["haste" in ops[x[1]]] * issue(ops[n])
                and chain[x[1]] > chain[n] + patience[2]]
        if soon:
            t, n = max(soon, key=lambda x: chain[x[1]])
        o = ops[n]
        t = max(t, clock[e])
        for k in names[n]:
            if k not in place:
                place[k] = min(free, key=free.get)
                del free[place[k]]
        if o["kind"] != "a":
            clock[e] = t + issue(o)
        if o["kind"] in pipe:
            pipe[o["kind"]] = max(t + issue(o) + delay(o) / 2, pipe[o["kind"]]) + o["cost"]
            end[n] = pipe[o["kind"]] + delay(o) / 2
        else:
            end[n] = t + o["cost"]
        for k in names[n]:
            used[place[k]][e] = end[n]
            left[k] -= 1
            if not left[k]:
                free[place[k]] = max(used[place[k]].values())
        ready[e].remove(n)
        out.append(n)
        for k in kids[n]:
            can[k] = max(can[k], end[n] + hop(o, ops[k]))
            wait[k] -= 1
            if not wait[k]:
                ready[ops[k]["eng"]].append(k)
    return place, free, used, clock, pipe, end, wait, can, ready, out, left


def order(ops, place):
    deps = needs(ops, lambda x: place.get(x[0], x[0]), True)
    who = lambda m: ops[m]["eng"] if ops[m]["kind"] == "c" else "x%d" % m
    known = {e: {} for e in ENG}
    snap, waits = [], []
    for n, o in enumerate(ops):
        kn, w = known[o["eng"]], []
        if o["kind"] != "a":
            for m in sorted(deps[n], reverse=True):
                if kn.get(who(m), -1) < m and not (who(m) == "t" == who(n)):
                    w.append(m)
                    kn[who(m)] = m
                    for k2, m2 in snap[m].items():
                        kn[k2] = max(kn.get(k2, -1), m2)
        waits.append(w)
        snap.append({} if o["kind"] == "a" else dict(kn))
    waiters = {}
    for n, w in enumerate(waits):
        for m in w:
            waiters.setdefault(m, []).append(n)
    sems, slot = [], {}
    for n, o in enumerate(ops):
        if o["kind"] in "dr":
            kind = o["kind"] + o["eng"]
            passed = lambda w: w < n and (ops[w]["eng"] == o["eng"] or (ops[w]["kind"] == "c" and snap[n].get(ops[w]["eng"], -1) >= w)
                                          or snap[n].get("x%d" % w, -1) >= w)
            s = [s for s, (k, m, _) in enumerate(sems) if k == kind and o["kind"] == "d" and snap[n].get("x%d" % m, -1) >= m
                 and all(passed(w) for w in waiters.get(m, []))]
            if s:
                sems[s[0]] = (kind, n, sems[s[0]][2] + 1)
                slot[n] = (s[0], sems[s[0]][2])
            else:
                sems.append((kind, n, 1))
                slot[n] = (len(sems) - 1, 1)
    return waits, slot, known["g"]


PLAN = {}


def rank_program(g, core, T, topo):
    rank = T.rank_of(core)
    if rank is None:
        return
    n = len(T.cores)
    nxt, prv = T.cores[(rank + 1) % n], T.cores[(rank - 1) % n]
    place = {}
    ops = build(g, T, nxt, prv, place)
    if not PLAN:
        seq, where = arrange(ops)
        PLAN.update(seq=seq, where=where, rest=order([ops[m] for m in seq], where))
    place.update(PLAN["where"])
    ops = [ops[m] for m in PLAN["seq"]]
    waits, slot, known = PLAN["rest"]
    wanted = set(m for w in waits for m in w)
    count = {e: 0 for e in ENG}
    for m, o in enumerate(ops):
        if o["kind"] == "c":
            if m in wanted:
                count[o["eng"]] += 1
                o["tok"] = ("e_" + o["eng"], count[o["eng"]])
        elif o["kind"] == "a":
            src = prv if o["msg"][0] in "kqv" else nxt
            o["tok"] = ("r_" + o["msg"], len(topo.engines(src, core)))
        else:
            o["tok"] = ("d%d" % slot[m][0], 16 * slot[m][1] if o["kind"] == "d" else len(topo.engines(core, o["to"])))
    qu = {"v": g.vector, "s": g.scalar, "t": g.tensor, "g": g, "y": g.sync}
    for o, w in zip(ops, waits):
        for m in w:
            qu[o["eng"]].wait_ge(T.sem[ops[m]["tok"][0]], ops[m]["tok"][1])
        if o["kind"] == "a":
            continue
        if o["kind"] == "r":
            rid, pid = topo.addr(o["to"])[:2]
            g.remote_dma(T["l_" + o["msg"][0]][:], o["src"], T.sem["r_" + o["msg"]], T.sem[o["tok"][0]], pid, rid, topo.mask(core, o["to"]))
            continue
        ins = o["f"]()
        if "tok" in o:
            ins.then_inc(T.sem[o["tok"][0]], 16 if o["kind"] == "d" else 1)
    for m, o in enumerate(ops):
        if o["kind"] != "c" and known.get("x%d" % m, -1) < m:
            g.wait_ge(T.sem[o["tok"][0]], o["tok"][1])
    for e in ENG:
        if count[e]:
            g.wait_ge(T.sem["e_" + e], count[e])
